import numpy as np, ml_dtypes
CORES = [36,164,52,180,100,228,116,244]
N = 8
BF = ml_dtypes.bfloat16
def gentries(a):
    return np.ascontiguousarray(a.reshape(8, 16, -1).transpose(0, 2, 1)).reshape(8, -1)
def gtable(e):
    e = np.asarray(e); return np.ascontiguousarray(e.reshape(8, -1, 16).transpose(0, 2, 1)).reshape(128, -1).astype(np.int32)
W, B, L, S, RO, ST = 2048, 512, 256, 8, 4, 5
def parts(rng):
    X = rng.integers(0, 201, (N, 8, 1, W)) + rng.integers(0, 56, (N, 8, 16, W))
    c = rng.integers(0, 101, (N, 8, 1, L)) + rng.integers(0, 56, (N, 8, 16, L))
    return X, rng.integers(0, W, (N, 8, 16, B)), rng.integers(0, W, (N, 8, 16, L)), c, rng.integers(0, B, (N, 8, L))
def pack(X, TT, T, c, b):
    return {"clk": X.reshape(N, 128, W).astype(np.float32).astype(BF), "ttab": TT.reshape(N, 128, B).astype(np.int32), "trav": T.reshape(N, 128, L).astype(np.int32),
            "last": c.reshape(N, 128, L).astype(np.float32).astype(BF), "slot": np.stack([gtable(a) for a in b])}
def setup_inputs(rng):
    return pack(*parts(rng))
def setup_inputs_spread(rng):
    pw = rng.choice(np.array([0.25, 0.5, 1.0, 2.0, 4.0]), (N, 8, 1, 1))
    sz = np.exp2(rng.integers(0, 8, (N, 8, 1, W)))
    X = np.clip(np.floor(256 * rng.random((N, 8, 1, W)) ** pw + sz * (rng.random((N, 8, 16, W)) - 0.5)), 0, 255).astype(np.int64)
    c = np.minimum(np.floor(256 * rng.random((N, 8, 1, L)) ** 2 * rng.random((N, 8, 16, L))), 255).astype(np.int64)
    pt = rng.choice(np.array([0.5, 1.0, 3.0]), (N, 8, 16, 1))
    T = np.minimum(np.floor(W * rng.random((N, 8, 16, L)) ** pt), W - 1).astype(np.int64)
    TT = np.minimum(np.floor(W * rng.random((N, 8, 16, B)) ** pt[::-1]), W - 1).astype(np.int64)
    b = np.minimum(np.floor(B * rng.random((N, 8, L)) ** 2), B - 1).astype(np.int64)
    return pack(X, TT, T, c, b)
def setup_inputs_ends(rng):
    X = 255 * rng.integers(0, 2, (N, 8, 16, W)); TT = (W - 1) * rng.integers(0, 2, (N, 8, 16, B)); T = (W - 1) * rng.integers(0, 2, (N, 8, 16, L))
    c = 255 * rng.integers(0, 2, (N, 8, 16, L)); b = (B - 1) * rng.integers(0, 2, (N, 8, L))
    for q in range(N):
        for g, size in ((3, 1), (7, 4)):
            P = np.sort(np.append(rng.permutation(15)[:size - 1], 15)); v = np.zeros(16, np.int64); v[P] = 255
            X[q, g] = (255 - v)[:, None]
            if size > 1:
                for t in (0, W - 1):
                    for s in (0, B - 1): X[q, g, int(np.argmin(v)), (((t * 511) >> 3) + 613 * int(P[0]) + 37 * s) & (W - 1)] = 254
            X[q, g, :, 0] = v; X[q, g, :, W - 1] = v
            c[q, g, P] = 255 * (np.arange(L) % 4 == 1)
            T[q, g, :, L - 1] = W - 1; b[q, g, L - 1] = B - 1
        X[q, 5] = 255; c[q, 5] = 0
        X[q, 6] = 255; c[q, 6] = 255
        if q % 2: c[q, 6, 15, L - 1] = 0
    return pack(X, TT, T, c, b)
def setup_inputs_corners(rng):
    X, TT, T, c, b = parts(rng); j = np.arange(W); i = np.arange(L)
    T[:, 0] = np.where(i % 2 == 0, 0, W - 1); b[:, 0] = np.where(i % 3 == 0, 0, B - 1)
    T[:, 1] = rng.integers(0, W, (N, 1, L))
    same = rng.integers(0, W, (N, 16, 1)); T[:, 2] = same; TT[:, 2] = same
    c[:, 3] = 255; b[:, 3] = (B - 99 + rng.integers(0, 100, (N, L))) & (B - 1)
    X[:, 4] = np.maximum(X[:, 4], 1); c[:, 4] = 0
    r = rng.integers(1, 255, (N, 16, 1)); X[:, 5] = r; c[:, 5] = r + rng.integers(-1, 2, (N, 16, L))
    o = np.argsort(rng.random((N, 16, W)), axis=1)
    X[:, 6] = np.where(j % 4 == 0, 100, np.where(j % 4 == 2, np.where(o < rng.integers(11, 13, (N, 1, W)), 120, 50), np.where(o < rng.integers(8, 11, (N, 1, W)), 101, 99)))
    T[:, 6] = 4 * rng.integers(0, W // 4, (N, 16, L)); TT[:, 6] = 2 * rng.integers(0, W // 2, (N, 16, B)) + 1; c[:, 6] = 0
    T[:, 7] = np.where(rng.random((N, 16, L)) < 0.5, (W - 1) * rng.integers(0, 2, (N, 16, L)), T[:, 7]); b[:, 7] = np.where(rng.random((N, L)) < 0.5, B - 1, b[:, 7])
    for a in (X, TT, T, c, b):
        for q in range(N): a[q] = np.roll(a[q], q, axis=0)
    return pack(X, TT, T, c, b)
def setup_inputs_crowd(rng):
    X, TT, T, c, b = parts(rng); one = rng.integers(0, B, (N, 8)); i = np.arange(L)
    for g in (0, 1, 2, 7): b[:, g] = one[:, g, None]
    b[:, 1, 0] = (one[:, 1] + 1) & (B - 1); b[:, 2, L - 1] = (one[:, 2] + 1) & (B - 1)
    b[:, 3] = one[:, 3, None] ^ rng.integers(0, 4, (N, L))
    b[:, 4] = B - 1; T[:, 4] = T[:, 4, :, :1].copy(); c[:, 4] = 255
    b[:, 5] = np.where(i % 2 == 0, one[:, 5, None], B - 1 - one[:, 5, None])
    b[:, 6] = 0; T[:, 6] = T[:, 6, :, :1].copy(); c[:, 6] = 255; c[:, 6, :, L - 1] = 0; X[:, 6] = np.maximum(X[:, 6], 1)
    for q in range(N):
        z = int(rng.integers(0, W)); X[q, 6, :, z] = 1; T[q, 6, :, L - 1] = z; TT[q, 6, :, 0] = z
    T[:, 7] = T[:, 7, :, :1].copy(); c[:, 7] = 0
    return pack(X, TT, T, c, b)
def high(rng, X, TT, T, c, g):
    o = np.argsort(rng.random((N, 16, W)), axis=1)
    X[:, g] = 255 - ((o < rng.integers(3, 7, (N, 1, W))) & (np.arange(W) % 2 == 1))
    T[:, g] = 2 * rng.integers(0, W // 2, (N, 16, L)); TT[:, g] = 2 * rng.integers(0, W // 2, (N, 16, B)); c[:, g] = rng.integers(253, 256, (N, 16, L))
def near(rng, X, TT, T, c, b, g):
    t = np.arange(W); v = np.zeros(16, np.int64); v[0] = 255; v[15] = 255
    for q in range(N):
        s = rng.permutation(B)[:L]; two = []
        for p, lo, hi in ((0, W - 8, W - 1), (15, 0, 8)):
            n = (((t * 511) >> 3)[None, :] + 613 * p + 37 * s[:, None]) & (W - 1)
            ok = (n >= lo) & (n <= hi) & (t > 8) & (t < W - 8)
            two.append(np.argmax(ok * rng.random((L, W)), axis=1))
        X[q, g] = (255 - v)[:, None]; X[q, g, 1, W - 8:] = 254
        for a in two: X[q, g][:, a] = v[:, None]
        T[q, g, :8] = two[0]; T[q, g, 8:] = two[1]; TT[q, g][:, s] = T[q, g]; b[q, g] = s
        c[q, g, 0] = rng.integers(0, 255, L); c[q, g, 15] = rng.integers(0, 255, L)
def setup_inputs_ties(rng):
    X, TT, T, c, b = parts(rng); o = rng.permutation(8)
    base = np.array([0, 0, 1, 64, 127, 127, 252, 252])[o].reshape(1, 8, 1, 1)
    X = base + rng.integers(0, 3, (N, 8, 1, W)) + (rng.random((N, 8, 16, W)) < 0.25)
    c = base + rng.integers(0, 2, (N, 8, 16, L))
    few = rng.integers(0, W, 8); T[:, ::2] = few[rng.integers(0, 8, (N, 4, 16, L))]
    high(rng, X, TT, T, c, int(np.argmax(o == 7))); near(rng, X, TT, T, c, b, int(np.argmax(o == 5)))
    return pack(X, TT, T, c, b)
def check_inputs(d):
    bad = []
    for k, lo, hi in (("clk", 0, 255), ("ttab", 0, W - 1), ("trav", 0, W - 1), ("last", 0, 255), ("slot", 0, B - 1)):
        a = np.asarray(d[k]).astype(np.float64)
        if not (np.min(a) >= lo and np.max(a) <= hi): bad.append("range of " + k)
        if np.any(a != np.floor(a)): bad.append("whole numbers in " + k)
    return bad
def pick(X, n):
    return np.take_along_axis(X, n.reshape(N, 8, 1, 16 * L), 3).reshape(N, 8, 16, 16, L)
def reference(clk, ttab, trav, last, slot):
    X = clk.astype(np.float32).astype(np.int32).reshape(N, 8, 16, W); TT = ttab.astype(np.int32).reshape(N, 8, 16, B)
    T = trav.astype(np.int32).reshape(N, 8, 16, L); c = last.astype(np.float32).astype(np.int32).reshape(N, 8, 16, L)
    b = np.stack([gentries(a) for a in slot]).astype(np.int32)
    bound = np.full((N, 8), 9, np.int32); row = np.arange(16, dtype=np.int32)[None, None, :, None]; lane = np.arange(L, dtype=np.int32)
    for v in range(RO):
        if v > 0:
            T = np.roll(T, ST, axis=0); c = np.roll(c, ST, axis=0); b = np.roll(b, ST, axis=0)
        at = np.broadcast_to(b[:, :, None, :], (N, 8, 16, L))
        H = np.take_along_axis(TT, at, 3); x = pick(X, T); y = pick(X, H)
        take = np.sum(y >= x, axis=2) >= bound[:, :, None, None]
        T = np.where(take, H, T); z = np.where(take[:, :, None], y, x)
        m = np.min(z, axis=3); M = np.max(z, axis=3)
        free = m > c; c = m
        n = (((T * (2 * m + 1)) >> 3) + 613 * row + 37 * at) & (W - 1)
        e = pick(X, n)
        ready = free & (np.sum(e >= m[:, :, :, None], axis=2) >= 12)
        T = np.where(ready, n, T)
        score = np.where(ready, np.sum(np.abs(e - M[:, :, :, None]), axis=2), -1)
        best = np.argmax(score, axis=2)
        has = np.any(ready, axis=2)
        low = np.argmax(b[:, :, :, None] == b[:, :, None, :], axis=3)
        np.put_along_axis(TT, at, np.take_along_axis(T, np.broadcast_to(low[:, :, None, :], (N, 8, 16, L)), 3), 3)
        col = np.broadcast_to((S * lane + (np.sum(M, axis=2) & (S - 1)))[:, :, None, :], (N, 8, 16, L))
        np.put_along_axis(X, col, (np.take_along_axis(X, col, 3) + M) >> 1, 3)
        b = np.where(has, np.take_along_axis(n, best[:, :, None, :], 2)[:, :, 0] & (B - 1), (b + 97) & (B - 1)).astype(np.int32)
        bound = 9 + (np.sum(~has, axis=2) & 1)
    return {"yclk": X.reshape(N, 128, W).astype(np.float32).astype(BF), "yttab": TT.reshape(N, 128, B).astype(np.float32), "ytrav": T.reshape(N, 128, L).astype(np.float32),
            "ylast": c.reshape(N, 128, L).astype(np.float32).astype(BF), "yslot": np.stack([gtable(a) for a in b]).astype(np.float32)}

@@ -1,0 +1,688 @@
+from concourse.mybir import AluOpType as Op, AxisListType, ActivationFunctionType as Fn
+
+NR, VISITS, STEP = 8, 4, 5
+W, B, L = 2048, 512, 256
+UP = """
+Vga:e:0'=15 Vga:e:1=-5 Vga:e:1'=20 Vga:xg:0=-10 Vga:xg:0'=-5 Vga:xg:1=45 Vga:xj:a=70 Vga:z:0=60 Vga:z:0'=-20 Vga:z:1=90
+Vga:z:1'=75 ac:K:0=-90 ac:K:1=90 ac:ab:0=70 ac:ab:1=55 ac:cmp2:0=40 ac:couT:0=55 ac:couT:1=-30 ac:m8:0=-30 ac:m8:1=90
+ac:nr:0=-75 ac:nr:1=30 ac:xb:a=-50 ac:xr:a=15 co:Hu:0=50 co:Hu:1=45 co:T1u:0=80 co:T1u:0'=-90 co:T1u:1=90 co:TT:0=30
+co:TT:1=-5 co:Tu:0=-40 co:Tu:1=5 co:X:a=-70 co:bout:0=-80 co:bout:1=-15 co:bu:0=-85 co:bu:1=-80 co:nu:0=10 co:nu:1=85
+co:ui:a=-40 ga:e:0=-30 ga:e:0'=-20 ga:e:1=55 ga:e:1'=40 ga:xg:0=15 ga:xg:0'=-45 ga:xg:1=-25 ga:xg:1'=15 ga:xj:a=45
+ga:z:0=-10 ga:z:0'=45 ga:z:1=-20 ga:z:1'=30 mm:Dsmax:0=5 mm:Dsmax:1=75 mm:Dsmin:0=90 mm:K:0=5 mm:K:1=-80 mm:M:0=-30
+mm:M:1=-40 mm:M:a=-30 mm:Scmp:0=10 mm:Sfree:0=40 mm:Sfree:1=20 mm:Z0:a=15 mm:Z272:a=40 mm:Z312:1=-90 sc:ks:0=5
+sc:ks:1=85 sc:smax:0=-10 sc:smax:1=-75 sc:smax:1'=70 sc:smin:0=-70 sc:smin:0'=-10 sc:smin:1=90 sc:smin:1'=15
+st:bout:a=50 tr:kt:0=-60 tr:kt:1=-5 ts:Spar:0=-15 ts:Spar:0'=35 ts:Spar:1=75
+ts:bbf:a=50 ts:bi:0=-75 ts:bi:1=40 ts:fbk:a=-5 ts:half:a=70 ts:nn:0=-25 ts:nn:1=25 ts:offu:a=40 ts:p1:a=-25 ts:p2:a=-90
+ts:par:a=10 ts:srcb:0=-60 ts:srcb:1=-30 ts:u7:a=80 tt:E:a=40 tt:SS:0=55 tt:SS:1=-15 tt:SdH:0=-20 tt:SdH:0'=-90
+tt:SdH:1=5 tt:Sland:0=15 tt:Sland:0'=10 tt:Sland:1=90 tt:Sm8:0=60 tt:Sm8:1=75 tt:Snr:0=-65 tt:Snr:1=-50 tt:cmp2:0=90
+tt:cmp2:1=-15 tt:cmp:0=25 tt:cmp:0'=-50 tt:cmp:1=-60 tt:cmp:1'=-15 tt:dH:0=30 tt:dH:1=-55 tt:free:a=80 tt:ji:a=30
+tt:ki:0=-40 tt:ki:1=-15 tt:ni:0=-30 tt:ni:1=50 tt:srcT:0=-60 tt:srcT:1=90 ts:SS:0=30 ts:SS:0'=-5 ts:SS:1=-20
+ac:K:1=-115 ac:ab:1=25 ac:nr:1=55 ac:xb:a=-25 co:Tu:1=-35 co:X:a=40 co:bu:0=25 co:ju:a=-70 ga:e:0'=75 mm:Dsmax:0=30
+mm:Scmp:0=60 sc:smax:0=-5 sc:smax:1=20 sc:smin:0=-15 tr:kt:1=55 ts:SS:1=-65 ts:bbf:a=-20 ts:fbk:a=20 ts:offu:a=-45
+ts:p1:a=-50 ts:srcb:1=-20 ts:u7:a=-140 tt:E:a=-35 tt:SS:1=20 tt:Snr:0=-25 tt:cmp2:1=-20 tt:cmp:0'=-35 tt:dH:1=-30
+io:pi:a=900 as:I:a=800 as:B1:a=700 io:rr:a=600 as:Ash:a=500 io:jc:a=400 io:iot:a=300 me:ones:a=900 me:onesF:a=800
+me:Cmat:a=100 Vga:xg:1'@0=-100 ga:xg:1@0=200 ga:xg:1'@0=200 co:Tu:1@0=300 co:Hu:1@0=100 co:bu:1@0=200 tt:cmp:1@0=150
+tt:cmp:1'@0=120 co:Tu:0@0=300 co:bu:0@0=200 lo:X:a=900 lo:TTi:a=500 lo:Tin:a=500
+co:Hu:0@0=50 co:TT:1@0=15 co:X:a@0=-20 co:ju:a@0=-55 ga:e:0@0=-70 sc:smax:0'@0=-85 sc:smax:1'@0=-80 sc:smin:0'@0=-90
+sc:smin:0@0=30 tr:kt:0@0=-90 ts:SS:0'@0=45 ts:fbk:a@0=-90 ts:offu:a@0=-80 ts:p1:a@0=-15 ts:p2:a@0=-65 ts:srcb:1@0=35
+tt:E:a@0=-20 tt:SdH:0'@0=90 tt:cmp:0'@0=-30 tt:cmp:0@0=45 tt:cmp:1'@0=-30 tt:cmp:1@0=-65 tt:ki:1@0=15
+ac:hz:a=5 ac:nr:1=-85 co:Hu:0=-75 co:T1u:0'=175 co:TT:1=-15 co:Tu:0=95 co:bu:0=-25 ga:e:0=-30 ga:xg:1=-5 ga:xj:a=-55
+sc:smax:0=-50 sc:smax:1=50 sc:smin:1=-80 ts:Spar:0=55 ts:bbf:a=-15 ts:half:a=-120 ts:offu:a=-35 tt:SdH:0=45
+tt:SdH:0'=110 tt:Sland:0=-35 tt:cmp:0'=5 tt:free:1=75 tt:ki:0=90 tt:ki:1=-45
+ac:K:1=-25 ac:nr:1=55 co:Hu:1=-135 co:T1u:0=-35 co:TT:0=60 co:bu:0=50 co:bu:1=70 co:nu:1=-120 co:ui:a=25 ga:e:0=50
+ga:xg:0=-105 ga:xj:a=50 sc:smax:0=-15 sc:smax:0'=-15 sc:smax:1=-45 sc:smax:1'=-40 sc:smin:0'=-15 tr:kt:0=95
+ts:bi:1=-110 ts:half:a=-35 ts:srcb:1=20 tt:SS:0=-145 tt:SS:1=-10 tt:cmp:0'=-10 tt:cmp:1=-30 tt:free:1=-70
+"""
+CFG = {"nch": 2, "pw": 1024, "slack": 100.0, "tau": 2500.0, "flex": 1, "trans": 1, "raw": 0,
+       "ns": [0, 0], "f1": [64, 128], "f2": [128, 128], "mg": 1, "nrA": 1, "frA": 0, "xnA": 1, "up": {}}
+for _t in UP.split():
+    CFG["up"][_t.split("=")[0]] = CFG["up"].get(_t.split("=")[0], 0) + int(_t.split("=")[1])
+LOW = 2040 * 8192
+BANKS = ("S0", "S1", "M0", "M1", "D0", "D1", "KB", "Z")
+MAGIC = 12582912.0
+REF = {"f": 1.25, "g": 1.56, "s": 3.8, "ov": 40.0, "pe": 0.42, "lat": 100.0, "same": 50.0, "rem": 2200.0, "rb": 0.02,
+       "dma": 1800.0, "db": 0.006, "tt2": 1.0}
+
+
+def scratch(cfg):
+    w = L // cfg["nch"]; nc = w // 16
+    s = {}
+    def sb(names, n, dtp):
+        for nm in names.split():
+            s[nm] = ("sbuf", [128, n], dtp)
+    sb("X", W, "bfloat16"); sb("TTi", B, "int32"); sb("TT", B + 16, "float32")
+    sb("Tin ni nn p1 xn", L, "int32"); sb("bin ki bi ui u7 ji jc j8", 16, "int32")
+    sb("cin0 cin1 cin2 cin3 cout0 cout1 cout2 cout3 p2 free nr E xj xb hz rr ones", L, "bfloat16")
+    for v in range(VISITS - 1):
+        sb("src%d land%d" % (v, v), L + 16, "int32")
+    sb("Tout dH m8 K kt ks maskK xr", L, "float32"); sb("bout fbk junk cols", 16, "float32")
+    sb("Tu Hu T1u nu", L, "uint16"); sb("bu ju", 16, "uint16"); sb("offu", 32, "uint16")
+    sb("xg cmp z smin smax e cmp2 ab", 16 * L, "bfloat16")
+    sb("bbf nh", 16, "bfloat16"); sb("scol par", 8, "float32"); sb("half pi p15 h1", 8, "int32")
+    sb("I negI I16 I37 Ipen Iq BD Cmat", 128, "bfloat16"); sb("B1 B8 BH", 144, "bfloat16")
+    sb("onesF Ash A0 A1", 160, "float32"); sb("rmin rmax", cfg["pw"], "bfloat16"); sb("rk", w, "float32")
+    sb("iot", B, "float32")
+    for b in BANKS:
+        s[b] = ("psum", [128, 512], "float32")
+    return s
+
+
+def semaphores(cfg):
+    n = ["qV", "qA", "qP", "qG", "sent"] + ["ld%d" % i for i in range(5)] + ["st%d" % i for i in range(5)]
+    for v in range(VISITS - 1):
+        n += ["arr%s%d_%d" % (x, v, ch) for ch in range(cfg["nch"]) for x in "Tb"] + ["arrc%d" % v]
+    return n
+
+
+SCRATCH = scratch(CFG)
+SEMAPHORES = semaphores(CFG)
+
+
+def R(name, lo, hi, step=1, p0=0, p1=128):
+    return (name, lo, hi, step, p0, p1)
+
+
+def cnt(a):
+    return (a[2] - a[1] + a[3] - 1) // a[3]
+
+
+def view(T, a):
+    if not isinstance(a, tuple):
+        return a
+    if a[0] == "ind":
+        return view(T, a[1]).indirect(view(T, a[2]))
+    if a[3] == 1:
+        return T[a[0]][a[4]:a[5], a[1]:a[2]]
+    return T[a[0]][a[4]:a[5], a[1]:a[2]:a[3]]
+
+
+def parts(a):
+    if not isinstance(a, tuple):
+        return []
+    return [a[1], a[2]] if a[0] == "ind" else [a]
+
+
+def program(cfg):
+    sc = scratch(cfg)
+    nch, pw = cfg["nch"], cfg["pw"]
+    w = L // nch; nc = w // 16; pl = pw // 16
+    ops = []
+    cur = ["a", "@c"]
+
+    def turns():
+        for ch in range(nch - 1, -1, -1):
+            cur[0] = str(ch)
+            yield ch
+        cur[0] = "a"
+
+    def two(a):
+        return sc[a[0]][2] in ("bfloat16", "uint16") and sc[a[0]][0] == "sbuf"
+
+    def add(eng, kind, args, reads, writes, n, cls, **kw):
+        rd = []
+        for a in reads:
+            rd += parts(a)
+        wr = []
+        for a in writes:
+            if a[0] == "ind":
+                wr.append(a[1]); rd.append(a[2])
+            else:
+                wr.append(a)
+        o = {"eng": eng, "kind": kind, "args": args, "rd": rd, "wr": wr, "n": n, "cls": cls}
+        a = wr[0] if wr else rd[0]
+        nm = a[0]
+        if nm in BANKS:
+            nm = nm[0] + (rd[-1][0].rstrip("012").replace("Tin", "land") if nm[0] in "DS" else str(a[1]) if nm == "Z" else "")
+        elif nm[:3] in ("src", "lan", "cin", "cou", "Tou"):
+            nm = nm[:3].replace("Tou", "src") + "Tb"[a[1] // L]
+        o["tag"] = "%s:%s:%s" % (kind[:2], nm, cur[0])
+        o["vis"] = cur[1]
+        o.update(kw); ops.append(o)
+        return o
+
+    def cls_of(out, ins):
+        if out[0] == "ind":
+            return "s"
+        if ins[0][0] == "ind":
+            return "g"
+        return "h" if two(out) and all(two(a) for a in ins) else "c"
+
+    def copy(out, in_):
+        add("V", "copy", (out, in_), [in_], [out], cnt(in_ if out[0] == "ind" else out), cls_of(out, [in_]))
+
+    def gather(out, win, off):
+        a = ("ind", win, off)
+        add("F" if cfg["flex"] else "A", "gather", (out, a), [a], [out], cnt(out), "g")
+
+    def tt(out, a, b, op):
+        c = cls_of(out, [a, b])
+        if c in "hc" and sc[a[0]][0] == "sbuf" and sc[b[0]][0] == "sbuf":
+            c = "t" + c
+        add("V", "tt", (out, a, b, op), [a, b], [out], cnt(out), c)
+
+    def ts(out, a, s1, s2, op0, op1=None):
+        add("V", "ts", (out, a, s1, s2, op0, op1), [a, s1, s2], [out], cnt(out), cls_of(out, [a]))
+
+    def scan(out, d0, d1, op0, op1):
+        add("V", "scan", (out, d0, d1, op0, op1), [d0, d1], [out], cnt(out), cls_of(out, [d0, d1]))
+
+    def act(out, in_, fn, bias=0.0, scale=1.0, acc=None):
+        add("A", "act", (out, in_, fn, bias, scale, acc), [in_, bias, scale], [out] + ([acc] if acc else []), cnt(out),
+            "g" if in_[0] == "ind" else "c")
+
+    def pe(mms, grp=None):
+        cyc = 0
+        rd, wr = [], []
+        for o, l, r, st, sp in mms:
+            cyc += max(64, cnt(r)) * (4 if sc[r[0]][2] == "float32" else 1)
+            rd += [l, r]; wr.append(o)
+        add("P", "mm", mms, rd, wr, cyc, "p", grp=grp, first=mms[0][3], last=mms[-1][4])
+
+    def memset(out, val):
+        add("V", "memset", (out, val), [], [out], cnt(out), "h" if two(out) else "c")
+
+    def iota(out, pat, base, cm):
+        add("G", "iota", (out, pat, base, cm, sc[out[0]][2] != "int32"), [], [out], 2 * cnt(out) + 150, "c")
+
+    def asel(out, in_, pat, cmp, base, cm):
+        add("G", "asel", (out, in_, pat, cmp, base, cm), [in_], [out], 2 * cnt(out) + 200, "c")
+
+    def load(q, buf, src, k, nbytes):
+        add(q, "load", (buf, src), [], [buf], nbytes, "d", sem=("ld%d" % k, 16))
+
+    def store(q, dst, buf, k, nbytes):
+        add(q, "store", (dst, buf), [buf], [], nbytes, "d", sem=("st%d" % k, 16))
+
+    def send(src, dst, sem, nbytes):
+        add("G", "send", (src, dst, sem), [src], [dst], nbytes, "r", sem=(sem, None))
+
+    def whole(nm):
+        return R(nm, 0, sc[nm][1][1])
+
+    load("S", whole("X"), "clk", 0, 128 * W * 2 + 128 * L * 4)
+    load("A", whole("Tin"), "trav", 1, 128 * L * 8)
+    load("A", whole("bin"), "slot", 2, 128 * L * 8)
+    load("S", whole("TTi"), "ttab", 3, 128 * W * 2 + 128 * (L + B) * 4)
+    load("S", whole("cin0"), "last", 4, 128 * W * 2 + 128 * (L + B) * 4 + 128 * L * 2)
+    I, ones = whole("I"), whole("ones")
+    memset(ones, 1.0); memset(whole("onesF"), 1.0)
+    b1 = whole("B1")
+    asel(b1, R("ones", 0, 144), [[0, 9], [1, 16]], Op.is_equal, -15, 0)
+    asel(b1, b1, [[1, 144]], Op.is_ge, 0, -1)
+    asel(b1, b1, [[-1, 144]], Op.is_ge, 15, 1)
+    ts(whole("B8"), b1, 8192.0, None, Op.mult)
+    ts(whole("BH"), b1, 0.5, None, Op.mult)
+    asel(I, R("ones", 0, 128), [[-1, 128]], Op.is_equal, 0, 1)
+    for nm, val in (("negI", -1.0), ("I16", 8.0 if cfg["frA"] else 16.0), ("Iq", -0.5), ("I37", 37.0), ("Ipen", -2.0 ** 26)):
+        ts(whole(nm), I, val, None, Op.mult)
+    memset(whole("rmin"), 0.0); memset(R("rmin", 0, pw, 16), 255.0)
+    memset(whole("rmax"), 255.0); memset(R("rmax", 0, pw, 16), 0.0)
+    iota(whole("rr"), [[0, 16], [256, 16]], 0, 0)
+    iota(whole("iot"), [[1, B]], -256, 0)
+    iota(R("pi", 0, 1), [[1, 1]], 0, 1)
+    ts(R("p15", 0, 1), R("pi", 0, 1), 15, None, Op.bitwise_and)
+    ts(R("p15", 1, 2), R("pi", 0, 1), 3, None, Op.bitwise_and)
+    ts(R("h1", 0, 1), R("pi", 0, 1), 4, 1, Op.logical_shift_right, Op.bitwise_and)
+    vcol, c512, c8, c256, h0f, h1f = [R("cols", i, i + 1) for i in range(6)]
+    t0 = 20.0 if cfg["frA"] else 28.0
+    thb = {}
+    for ns in sorted(set(cfg["ns"])):
+        thb[ns] = R("cols", 6 + len(thb), 7 + len(thb))
+        ts(thb[ns], R("p15", 1, 2), 4.0 - ns // 4, -8.0, Op.is_ge, Op.mult)
+        if cfg["nrA"]:
+            ts(thb[ns], thb[ns], 250.0, 250.0 * t0 - 125.0, Op.mult, Op.add)
+        else:
+            ts(thb[ns], thb[ns], t0, None, Op.add)
+    ts(vcol, R("p15", 0, 1), 613.0, 37.0 * 256 - 7.0 / 16, Op.mult, Op.add)
+    ts(c512, R("p15", 0, 1), float(B), None, Op.add)
+    ts(c8, R("p15", 0, 1), 8.0, None, Op.mult)
+    ts(c256, R("p15", 0, 1), 256.0, None, Op.mult)
+    ts(h0f, R("h1", 0, 1), -1.0, 1.0, Op.mult, Op.add)
+    ts(h1f, R("h1", 0, 1), 1.0, None, Op.mult)
+    asel(whole("Ash"), whole("onesF"), [[-1, 160]], Op.is_equal, 16, 1)
+    ts(whole("A0"), whole("Ash"), h0f, None, Op.mult)
+    ts(whole("A1"), whole("Ash"), h1f, None, Op.mult)
+    bd = whole("BD")
+    asel(bd, R("ones", 0, 128), [[16, 8], [0, 16]], Op.is_ge, 15, -1)
+    asel(bd, bd, [[-16, 8], [0, 16]], Op.is_ge, 0, 1)
+    memset(whole("Cmat"), 0.0)
+    memset(R("Cmat", 0, 128, 1, 0, 1), -float(LOW))
+    iota(R("Cmat", 0, 128, 1, 32, 33), [[0, 8], [-512, 16]], 15 * 512 + 256, 0)
+    ts(whole("rk"), R("rmax", 0, w), 0.0, -2.0 ** 28, Op.is_equal, Op.mult)
+    ts(whole("maskK"), whole("rr"), c256, 0.25, Op.is_le, Op.mult)
+    ts(whole("maskK"), whole("maskK"), vcol, None, Op.add)
+    iota(whole("jc"), [[128, 16]], 0, 0)
+    ts(whole("j8"), whole("jc"), c8, None, Op.add)
+    copy(R("TT", 0, B), whole("TTi"))
+
+    def sel(nm, k):
+        return R(nm, 15 - k, 143 - k)
+
+    Xw = whole("X")
+    dturn = [0]
+    for v in range(VISITS):
+        last = v == VISITS - 1
+        cur[1] = "@%d" % v
+        tab = whole("TTi") if v == 0 else R("TT", 0, B)
+        def Tin(ch):
+            return R("Tin", ch * w, ch * w + w) if v == 0 else R("land%d" % (v - 1), ch * w, ch * w + w)
+        def bin_(ch):
+            return R("bin", ch * nc, ch * nc + nc) if v == 0 else R("land%d" % (v - 1), L + ch * nc, L + ch * nc + nc)
+        def Tout(ch, a, b):
+            return R("Tout" if last else "src%d" % v, ch * w + a, ch * w + b)
+        def ln(nm, ch):
+            return R(nm, ch * w, ch * w + w)
+        def lc(nm, ch):
+            return R(nm, ch * nc, ch * nc + nc)
+        def ps(ch, k):
+            o = (ch // 2) * 3 * w + k * w
+            return R("S%d" % (ch % 2), o, o + w)
+        def pm(ch):
+            return R("M%d" % ch, 0, 512, 4)
+        def strided(nm, ch, k):
+            return R(nm, 16 * ch * w + k, 16 * (ch + 1) * w, 16)
+        def pieces(ch):
+            return [(a, min(a + pl, (ch + 1) * w)) for a in range(ch * w, (ch + 1) * w, pl)]
+        cin, cout = "cin%d" % v, "cout%d" % v
+        for ch in turns():
+            copy(ln("Tu", ch), Tin(ch))
+            copy(lc("bu", ch), bin_(ch))
+            copy(ln("Hu", ch), ("ind", tab, lc("bu", ch)))
+            tt(ln("dH", ch), ("ind", tab, lc("bu", ch)), Tin(ch), Op.subtract)
+            act(ln("K", ch), ("ind", whole("iot"), lc("bu", ch)), Fn.Identity, vcol, 37.0)
+            for a, b in pieces(ch):
+                cur[0] = "%d%s" % (ch, "'" * ((a - ch * w) // pl))
+                gather(R("xg", 16 * a, 16 * b), Xw, R("Tu", a, b))
+                tt(R("cmp", 16 * a, 16 * b), ("ind", Xw, R("Hu", a, b)), R("xg", 16 * a, 16 * b), Op.is_ge)
+        ball = whole("bin") if v == 0 else R("land%d" % (v - 1), L, L + 16)
+        ts(whole("bbf"), ball, -256.0, None, Op.add)
+        ts(whole("fbk"), ball, 97.0 - LOW - 8192, None, Op.add)
+        pe([(R("Z", 0, L), R("Ash", 16, 144), whole("maskK"), True, False)] +
+           [(R("Z", r, L, 16), whole("I37"), whole("bbf"), False, r == 15) for r in range(16)])
+        tt(whole("E"), R("Z", 0, L), whole("K"), Op.is_equal)
+        pe([(R("Z", 256, 272), I, whole("bbf"), True, False)] +
+           [(R("Z", 256, 272), sel("B8", r), R("E", r, L, 16), False, r == 15) for r in range(16)])
+        ts(R("offu", 0, 32, 2), R("Z", 256, 272), 256.0, c512, Op.add, Op.min)
+        for ch in turns():
+            t1 = ps(ch, 0)
+            for a in range(0, w, 64):
+                pe([(R(t1[0], t1[1] + a, t1[1] + a + 64), sel("B1", k),
+                     R("cmp", 16 * (ch * w + a) + k, 16 * (ch * w + a + 64), 16), k == 0, k == 15) for k in range(16)])
+            def sub(r, a, b):
+                return R(r[0], r[1] + a * r[3], r[1] + (b - 1) * r[3] + 1, r[3])
+            s1 = cfg["f1"][ch]
+            for a in range(0, w, s1):
+                cur[0] = "%d%s" % (ch, "'" * (a // s1))
+                u = sub(t1, a, a + s1)
+                if v == 0:
+                    ts(u, u, 9.0, None, Op.is_ge)
+                else:
+                    ts(u, u, -9.0, R("par", v, v + 1), Op.add, Op.is_ge)
+                tt(u, u, sub(ln("dH", ch), a, a + s1), Op.mult)
+                tt(u, u, sub(Tin(ch), a, a + s1), Op.add)
+                copy(sub(ln("T1u", ch), a, a + s1), u)
+            cur[0] = str(ch)
+            for a, b in pieces(ch):
+                cur[0] = "%d%s" % (ch, "'" * ((a - ch * w) // pl))
+                zz = R("z", 16 * a, 16 * b)
+                gather(zz, Xw, R("T1u", a, b))
+                scan(R("smin", 16 * a, 16 * b), R("rmin", 0, 16 * (b - a)), zz, Op.max, Op.min)
+                scan(R("smax", 16 * a, 16 * b), R("rmax", 0, 16 * (b - a)), zz, Op.min, Op.max)
+            cur[0] = str(ch)
+            m = strided("smin", ch, 15)
+            pe([(R("M%d" % ch, j, 512, 4), I, m, True, True) for j in range(4)])
+            act(ln(cout, ch), m, Fn.Copy)
+            s2 = cfg["f2"][ch]
+            for a in range(0, w, s2):
+                cur[0] = "%d%s" % (ch, "'" * (a // s2))
+                def u(r):
+                    return sub(r, a, a + s2)
+                act(u(ln("m8", ch)), u(m), Fn.Identity, 0.125, 0.25)
+                tt(u(ps(ch, 1)), u(t1), u(ln("m8", ch)), Op.mult)
+                tt(u(ln("ni", ch)), u(ps(ch, 1)), u(ln("K", ch)), Op.add)
+                ts(u(ln("nn", ch)), u(ln("ni", ch)), W - 1, None, Op.bitwise_and)
+                copy(u(ln("nu", ch)), u(ln("nn", ch)))
+            cur[0] = str(ch)
+            tt(ps(ch, 2), ln("nn", ch), t1, Op.subtract)
+            if cfg["frA"]:
+                o = ps(ch, 3)
+                pe([(o, I, m, True, False), (o, whole("negI"), ln(cin, ch), False, True)])
+                act(ln("free", ch), o, Fn.Sign, -0.5)
+            else:
+                tt(ln("free", ch), pm(ch), ln(cin, ch), Op.is_gt)
+            if not cfg["mg"]:
+                ts(ln("p1", ch), ln("ni", ch), B - 1, None, Op.bitwise_and)
+                ts(ln("p2", ch), ln("p1", ch), -256.0, None, Op.add)
+            for a, b in pieces(ch):
+                cur[0] = "%d%s" % (ch, "'" * ((a - ch * w) // pl))
+                gather(R("e", 16 * a, 16 * b), Xw, R("nu", a, b))
+        if cfg["mg"]:
+            ts(whole("p1"), whole("ni"), B - 1, None, Op.bitwise_and)
+            ts(whole("p2"), whole("p1"), -256.0, None, Op.add)
+        if not last:
+            send(whole(cout), whole("cin%d" % (v + 1)), "arrc%d" % v, 128 * L * 2)
+        else:
+            store("S", "ylast", whole(cout), 0, 128 * L * 2)
+        pe([(R("Z", 272, 288), sel("B1", r), R("smax", 15 + 16 * r, 16 * L, 256), r == 0, r == 15) for r in range(16)])
+        copy(whole("ui"), R("Z", 272, 288))
+        ts(whole("u7"), whole("ui"), 7, None, Op.bitwise_and)
+        tt(whole("ji"), whole("u7"), whole("j8"), Op.add)
+        copy(whole("ju"), whole("ji"))
+        gather(whole("xj"), Xw, whole("ju"))
+        mm = [(R("Z", 0, L), I, whole("xj"), True, False), (R("Z", 0, L), I, R("smax", 15, 16 * L, 16), False, not cfg["xnA"])]
+        if cfg["xnA"]:
+            pe(mm + [(R("Z", 0, L), whole("Iq"), ones, False, True)])
+            act(whole("xr"), R("Z", 0, L), Fn.Identity, MAGIC, 0.5)
+            act(whole("xb"), whole("xr"), Fn.Identity, -MAGIC)
+            copy(("ind", Xw, whole("ju")), whole("xb"))
+        else:
+            pe(mm)
+            ts(whole("xn"), R("Z", 0, L), 0.5, -0.25, Op.mult, Op.add)
+            copy(("ind", Xw, whole("ju")), whole("xn"))
+        if last:
+            store("S", "yclk", Xw, 1, 128 * W * 2)
+        for ch in turns():
+            M = strided("smax", ch, 15)
+            def blk(nm, p, k=1):
+                return R(nm, 16 * ch * w + p * w, 16 * ch * w + (p + k) * w)
+            c2 = ps(ch, 1)
+            ns = cfg["ns"][ch]
+            m = strided("smin", ch, 15)
+            def diff(q, sub):
+                d = "D%d" % (dturn[0] % 2); dturn[0] += 1
+                pe([(R(d, 0, 512), I, R("e", 16 * ch * w + q, 16 * (ch + 1) * w, 4), True, False)] +
+                   [(R(d, j, 512, 4), whole("negI"), sub, False, j == 3) for j in range(4)])
+                return R(d, 0, 512)
+            def of(nm, q, j):
+                return R(nm, 16 * ch * w + 512 * q + j, 16 * ch * w + 512 * (q + 1), 4)
+            for q in range(3, -1, -1):
+                sign = 4 * q >= 16 - ns
+                if sign:
+                    act(blk("cmp2", 4 * q, 4), diff(q, m), Fn.Sign, 0.5)
+                else:
+                    tt(blk("cmp2", 4 * q, 4), R("e", 16 * ch * w + q, 16 * (ch + 1) * w, 4), R("M%d" % ch, 0, 512), Op.is_ge)
+                mm = [(c2, whole("I16"), ln("free", ch), False, True)] if q == 0 else []
+                pe([(c2, sel("BH" if sign else "B1", 4 * j + q), of("cmp2", q, j), q == 3 and j == 0, False)
+                    for j in range(4)] + mm, grp=("c", v, ch))
+            if cfg["nrA"]:
+                act(ln("nr", ch), c2, Fn.Sigmoid, thb[ns], -250.0)
+            else:
+                ts(ln("nr", ch), c2, thb[ns], None, Op.is_lt)
+            tt(ps(ch, 2), ps(ch, 2), ln("nr", ch), Op.mult)
+            tt(Tout(ch, 0, w), ln("nn", ch), ps(ch, 2), Op.subtract)
+            if not last:
+                send(Tout(ch, 0, w), R("land%d" % v, ch * w, ch * w + w), "arrT%d_%d" % (v, ch), 128 * w * 4)
+            for c in range(nc - 1, -1, -1):
+                cc = ch * nc + c
+                copy(("ind", whole("TT"), R("offu", 2 * cc, 2 * cc + 1)), Tout(ch, 16 * c, 16 * c + 16))
+            key = R("KB", ch * w, ch * w + w)
+            for q in range(4):
+                act(blk("ab", 4 * q, 4), diff(q, M), Fn.Abs)
+                mm = [(key, whole("Cmat"), R("ones", 0, w), True, False)] if q == 0 else []
+                pe(mm + [(key, sel("B8", 4 * j + q), of("ab", q, j), False, False) for j in range(4)], grp=("k", v, ch))
+            pe([(key, I, ln("p2", ch), False, False), (key, whole("Ipen"), ln("nr", ch), False, True)], grp=("k", v, ch))
+            add("V", "tr", (ln("kt", ch), key), [key], [ln("kt", ch)], w, "c")
+            scan(ln("ks", ch), whole("rk"), ln("kt", ch), Op.add, Op.max)
+            sw = 304 + ch * nc
+            mm = []
+            for h in (0, 1):
+                o = R("Z", sw + h, sw + nc, 2)
+                far = 32 * h
+                mm += [(o, R("A%d" % h, 16, 144), R("ks", ch * w + 15 + 16 * h, ch * w + w, 32), True, False),
+                       (o, R("A%d" % h, far, far + 128), R("ks", ch * w + 31 - 16 * h, ch * w + w, 32), False, True)]
+            pe(mm)
+            tt(lc("ki", ch), R("Z", sw, sw + nc), lc("fbk", ch), Op.max)
+            if last:
+                ts(lc("bi", ch), lc("ki", ch), B - 1, None, Op.bitwise_and)
+                copy(lc("bout", ch), lc("bi", ch))
+            else:
+                bo = L + ch * nc
+                ts(R("src%d" % v, bo, bo + nc), lc("ki", ch), B - 1, None, Op.bitwise_and)
+                send(R("src%d" % v, bo, bo + nc), R("land%d" % v, bo, bo + nc), "arrb%d_%d" % (v, ch), 128 * nc * 4)
+        if last:
+            store("S", "ytrav", whole("Tout"), 2, 128 * L * 4)
+            store("S", "yttab", R("TT", 0, B), 3, 128 * B * 4)
+            store("A", "yslot", whole("bout"), 4, 128 * 64)
+        else:
+            pe([(R("Z", 0, L), bd, whole("nr"), True, True)])
+            act(whole("hz"), R("Z", 0, L), Fn.Relu, -15.0, acc=R("scol", 0, 1))
+            ts(R("half", 0, 1), R("scol", 0, 1), 0.5, -0.25, Op.mult, Op.add)
+            ts(R("par", v + 1, v + 2), R("half", 0, 1), -2.0, R("scol", 0, 1), Op.mult, Op.add)
+    seen = {}
+    for i, o in enumerate(ops):
+        dep = set()
+        for a in o["rd"]:
+            for lo, hi, j, wr in seen.get(a[0], []):
+                if wr and lo < a[2] and a[1] < hi:
+                    dep.add(j)
+        o["raw"] = set(dep) if cfg["raw"] else None
+        for a in o["wr"]:
+            for lo, hi, j, wr in seen.get(a[0], []):
+                if lo < a[2] and a[1] < hi:
+                    dep.add(j)
+                    if wr and cfg["raw"]:
+                        o["raw"].add(j)
+        for a in o["wr"]:
+            if a[3] == 1 and a[4] == 0 and a[5] == 128:
+                seen[a[0]] = [t for t in seen.get(a[0], []) if not (a[1] <= t[0] and t[1] <= a[2])]
+        for a in o["wr"]:
+            seen.setdefault(a[0], []).append((a[1], a[2], i, True))
+        for a in o["rd"]:
+            seen.setdefault(a[0], []).append((a[1], a[2], i, False))
+        dep.discard(i)
+        o["dep"] = sorted(dep)
+        o["banks"] = sorted(set(a[0] for a in o["rd"] + o["wr"] if a[0] in BANKS))
+    return ops
+
+
+def cost(o, eng, m):
+    c, n, cyc = o["cls"], o["n"], 0.83 * m["f"]
+    if c == "d":
+        return 60.0, m["dma"] + n * m["db"]
+    if c == "r":
+        return 500.0, m["rem"] + n * m["rb"]
+    if c == "p":
+        t = n * m["pe"] * m["f"]
+        return t, t
+    if c == "g":
+        t = (50.0 if eng == "V" else 65.0) + n * m["g"] * cyc
+    elif c == "s":
+        t = 50.0 + n * m["s"] * cyc
+    else:
+        k = {"h": 0.5, "c": 1.0, "th": m["tt2"], "tc": 2.0}[c]
+        t = m["ov"] + max(64.0, n * k) * cyc
+    return t, t
+
+
+def loose(o, j, a, b):
+    return a == b and (a == "P" or (a in "VA" and o["raw"] is not None and j not in o["raw"] and o["cls"] != "d"))
+
+
+def gap(o, j, a, b, m):
+    if loose(o, j, a, b):
+        return 0.0
+    return m["same"] if a == b else m["lat"]
+
+
+def schedule(ops, cfg, m):
+    n = len(ops)
+    succ = [[] for _ in ops]
+    for i, o in enumerate(ops):
+        for j in o["dep"]:
+            succ[j].append(i)
+    rank = [0.0] * n
+    for i in range(n - 1, -1, -1):
+        rank[i] = cost(ops[i], "A", m)[1] + max([rank[j] + m["lat"] for j in succ[i]] + [0.0])
+    up = cfg["up"]
+    prio = [rank[i] + 100.0 * (up.get(o["tag"], 0) + up.get(o["tag"] + o["vis"], 0)) for i, o in enumerate(ops)]
+    tau = [cfg["tau"] + 100.0 * (up.get("V" + o["tag"], 0) + up.get("V" + o["tag"] + o["vis"], 0)) for o in ops]
+    left = [len(o["dep"]) for o in ops]
+    ready = [i for i in range(n) if left[i] == 0]
+    done = [0.0] * n; on = [None] * n; extra = [[] for _ in ops]
+    free = {e: 0.0 for e in "VAPGS"}
+    lastb = {b: {} for b in BANKS}; opened = {}
+    seq = []; lastg = []; fed = {}
+    while ready:
+        cand = {e: [] for e in "VAPGS"}
+        for i in ready:
+            o = ops[i]
+            if o["eng"] == "P" and o["first"] and any(b in opened for b in o["banks"]):
+                continue
+            for e in ("AV" if o["eng"] == "F" else o["eng"]):
+                if (i, e) not in fed:
+                    fed[i, e] = max([done[j] + gap(o, j, on[j], e, m) for j in o["dep"]] + [0.0])
+                t = max(free[e], fed[i, e])
+                for b in o["banks"]:
+                    for e2, j in lastb[b].items():
+                        if e2 != e:
+                            t = max(t, done[j] + m["lat"])
+                if o["eng"] == "F" and e == "V":
+                    cand[e].append((t + max(0.0, tau[i]), i, t))
+                else:
+                    cand[e].append((t, i, t))
+        best = None
+        for e in "VAPGS":
+            if cand[e]:
+                t0 = min(c[0] for c in cand[e])
+                c = max((c for c in cand[e] if c[0] <= t0 + cfg["slack"]), key=lambda c: prio[c[1]])
+                if best is None or t0 < best[0]:
+                    best = (t0, e, c)
+        e, i, t = best[1], best[2][1], best[2][2]
+        o = ops[i]
+        hold, fin = cost(o, e, m)
+        free[e] = t + hold; done[i] = t + fin; on[i] = e
+        if o["kind"] in ("iota", "asel"):
+            extra[i] += lastg; lastg[:] = [i]
+        for b in o["banks"]:
+            extra[i] += [j for e2, j in lastb[b].items() if e2 != e]
+            lastb[b][e] = i
+        if o.get("grp"):
+            if o["first"]:
+                opened[o["banks"][0]] = o["grp"]
+            if o["last"]:
+                del opened[o["banks"][0]]
+        seq.append(i); ready.remove(i)
+        for j in succ[i]:
+            left[j] -= 1
+            if left[j] == 0:
+                ready.append(j)
+    assert len(seq) == n
+    return seq, on, extra, max(done)
+
+
+def replay(ops, seq, on, extra, m):
+    free = {e: 0.0 for e in "VAPGS"}; done = {}; busy = {e: 0.0 for e in "VAPGS"}
+    for i in seq:
+        e = on[i]; t = free[e]
+        for j in ops[i]["dep"] + extra[i]:
+            t = max(t, done[j] + gap(ops[i], j, on[j], e, m))
+        hold, fin = cost(ops[i], e, m)
+        free[e] = t + hold; done[i] = t + fin; busy[e] += hold
+    return max(done.values()), busy, done
+
+
+def plan(cfg):
+    ops = program(cfg)
+    seq, on, extra, _ = schedule(ops, cfg, REF)
+    pos = {}; num = {e: 0 for e in "VAPGS"}
+    for i in seq:
+        num[on[i]] += 1; pos[i] = num[on[i]]
+    known = {e: {} for e in "VAPGS"}; clock = {}; waits = {}; signals = set()
+    for i in seq:
+        e = on[i]; need = {}
+        for j in ops[i]["dep"] + extra[i]:
+            if loose(ops[i], j, on[j], e) and "sem" not in ops[j]:
+                continue
+            key = ops[j]["sem"][0] if "sem" in ops[j] else on[j]
+            if known[e].get(key, 0) < pos[j] and (key not in need or pos[need[key]] < pos[j]):
+                need[key] = j
+        js = sorted(need.values(), key=lambda j: -seq.index(j))
+        ws = []
+        for j in js:
+            key = ops[j]["sem"][0] if "sem" in ops[j] else on[j]
+            if known[e].get(key, 0) >= pos[j]:
+                continue
+            ws.append(j); signals.add(j)
+            for k2, val in (clock[j].items() if cfg["trans"] else [(key, pos[j])]):
+                known[e][k2] = max(known[e].get(k2, 0), val)
+        waits[i] = ws
+        if ops[i]["kind"] == "send":
+            clock[i] = {ops[i]["sem"][0]: pos[i]}
+        else:
+            clock[i] = dict(known[e]); clock[i][ops[i]["sem"][0] if "sem" in ops[i] else e] = pos[i]
+    count = {}; num = {e: 0 for e in "VAPGS"}
+    for i in seq:
+        if i in signals and "sem" not in ops[i]:
+            num[on[i]] += 1; count[i] = num[on[i]]
+    return ops, seq, on, waits, count, num
+
+
+PLAN = []
+
+
+def rank_program(g, core, T, topo):
+    rank = T.rank_of(core)
+    if rank is None:
+        return
+    if not PLAN:
+        PLAN.append(plan(CFG))
+    ops, seq, on, waits, count, num = PLAN[0]
+    dst = T.cores[(rank + STEP) % NR]; frm = T.cores[(rank - STEP) % NR]
+    rid, pid = topo.addr(dst, core)
+    mask = topo.mask(core, dst)
+    n_out, n_in = len(topo.engines(core, dst)), len(topo.engines(frm, core))
+    Q = {"V": g.vector, "A": g.scalar, "P": g.tensor, "G": g, "S": g.sync}
+    sent = 0; own = []
+    for i in seq:
+        o = ops[i]; e = on[i]; q = Q[e]; k = o["kind"]; a = o["args"]
+        for j in waits[i]:
+            if "sem" in ops[j]:
+                q.wait_ge(T.sem[ops[j]["sem"][0]], ops[j]["sem"][1] or n_in)
+            else:
+                q.wait_ge(T.sem["q" + on[j]], count[j])
+        if k == "send":
+            g.remote_dma(view(T, a[1]), view(T, a[0]), T.sem[a[2]], T.sem.sent, pid, rid, mask)
+            sent += n_out; own.append((a[2], n_in))
+            continue
+        if k in ("load", "store"):
+            ins = q.dma_start(view(T, a[0]), T[a[1]][:]) if k == "load" else q.dma_start(T[a[0]][:], view(T, a[1]))
+            ins.then_inc(T.sem[o["sem"][0]], 16); own.append(o["sem"])
+            continue
+        x = [view(T, y) for y in a] if k != "mm" else a
+        if k == "mm":
+            for out, l, r, st, sp in a:
+                ins = q.matmul(view(T, out), view(T, l), view(T, r), st, sp)
+        elif k == "copy" or (k == "gather" and e == "V"):
+            ins = q.tensor_copy(x[0], x[1])
+        elif k == "gather":
+            ins = q.activation(x[0], x[1], Fn.Copy)
+        elif k == "tt":
+            ins = q.tensor_tensor(x[0], x[1], x[2], x[3])
+        elif k == "ts":
+            ins = q.tensor_scalar(x[0], x[1], x[2], x[3], x[4]) if x[5] is None else q.tensor_scalar(*x)
+        elif k == "scan":
+            ins = q.tensor_tensor_scan(x[0], x[1], x[2], 0.0, x[3], x[4])
+        elif k == "tr":
+            ins = q.transpose(x[0], x[1])
+        elif k == "act":
+            if x[2] == Fn.Copy:
+                ins = q.activation(x[0], x[1], x[2])
+            else:
+                ins = q.activation(x[0], x[1], x[2], bias=x[3], scale=x[4], accum_out=x[5])
+        elif k == "memset":
+            ins = q.memset(x[0], x[1])
+        elif k == "iota":
+            if x[4]:
+                ins = q.iota(x[0], x[1], x[2], x[3], allow_small_or_imprecise_dtypes=True)
+            else:
+                ins = q.iota(x[0], x[1], x[2], x[3])
+        else:
+            ins = q.affine_select(x[0], x[1], x[2], x[3], 0.0, x[4], x[5])
+        if i in count:
+            ins.then_inc(T.sem["q" + e], 1)
+    for e in "VAPG":
+        if num[e]:
+            g.wait_ge(T.sem["q" + e], num[e])
+    g.wait_ge(T.sem.sent, sent)
+    for s, val in own:
+        g.wait_ge(T.sem[s], val)

@@ -1,67 +1,49 @@
-from concourse.mybir import AluOpType as Op, AxisListType, ActivationFunctionType as Fn
+from concourse.mybir import AluOpType as Op, ActivationFunctionType as Fn
 
 NR, VISITS, STEP = 8, 4, 5
 W, B, L = 2048, 512, 256
-UP = """
-Vga:e:0'=15 Vga:e:1=-5 Vga:e:1'=20 Vga:xg:0=-10 Vga:xg:0'=-5 Vga:xg:1=45 Vga:xj:a=70 Vga:z:0=60 Vga:z:0'=-20 Vga:z:1=90
-Vga:z:1'=75 ac:K:0=-90 ac:K:1=90 ac:ab:0=70 ac:ab:1=55 ac:cmp2:0=40 ac:couT:0=55 ac:couT:1=-30 ac:m8:0=-30 ac:m8:1=90
-ac:nr:0=-75 ac:nr:1=30 ac:xb:a=-50 ac:xr:a=15 co:Hu:0=50 co:Hu:1=45 co:T1u:0=80 co:T1u:0'=-90 co:T1u:1=90 co:TT:0=30
-co:TT:1=-5 co:Tu:0=-40 co:Tu:1=5 co:X:a=-70 co:bout:0=-80 co:bout:1=-15 co:bu:0=-85 co:bu:1=-80 co:nu:0=10 co:nu:1=85
-co:ui:a=-40 ga:e:0=-30 ga:e:0'=-20 ga:e:1=55 ga:e:1'=40 ga:xg:0=15 ga:xg:0'=-45 ga:xg:1=-25 ga:xg:1'=15 ga:xj:a=45
-ga:z:0=-10 ga:z:0'=45 ga:z:1=-20 ga:z:1'=30 mm:Dsmax:0=5 mm:Dsmax:1=75 mm:Dsmin:0=90 mm:K:0=5 mm:K:1=-80 mm:M:0=-30
-mm:M:1=-40 mm:M:a=-30 mm:Scmp:0=10 mm:Sfree:0=40 mm:Sfree:1=20 mm:Z0:a=15 mm:Z272:a=40 mm:Z312:1=-90 sc:ks:0=5
-sc:ks:1=85 sc:smax:0=-10 sc:smax:1=-75 sc:smax:1'=70 sc:smin:0=-70 sc:smin:0'=-10 sc:smin:1=90 sc:smin:1'=15
-st:bout:a=50 tr:kt:0=-60 tr:kt:1=-5 ts:Spar:0=-15 ts:Spar:0'=35 ts:Spar:1=75
-ts:bbf:a=50 ts:bi:0=-75 ts:bi:1=40 ts:fbk:a=-5 ts:half:a=70 ts:nn:0=-25 ts:nn:1=25 ts:offu:a=40 ts:p1:a=-25 ts:p2:a=-90
-ts:par:a=10 ts:srcb:0=-60 ts:srcb:1=-30 ts:u7:a=80 tt:E:a=40 tt:SS:0=55 tt:SS:1=-15 tt:SdH:0=-20 tt:SdH:0'=-90
-tt:SdH:1=5 tt:Sland:0=15 tt:Sland:0'=10 tt:Sland:1=90 tt:Sm8:0=60 tt:Sm8:1=75 tt:Snr:0=-65 tt:Snr:1=-50 tt:cmp2:0=90
-tt:cmp2:1=-15 tt:cmp:0=25 tt:cmp:0'=-50 tt:cmp:1=-60 tt:cmp:1'=-15 tt:dH:0=30 tt:dH:1=-55 tt:free:a=80 tt:ji:a=30
-tt:ki:0=-40 tt:ki:1=-15 tt:ni:0=-30 tt:ni:1=50 tt:srcT:0=-60 tt:srcT:1=90 ts:SS:0=30 ts:SS:0'=-5 ts:SS:1=-20
-ac:K:1=-115 ac:ab:1=25 ac:nr:1=55 ac:xb:a=-25 co:Tu:1=-35 co:X:a=40 co:bu:0=25 co:ju:a=-70 ga:e:0'=75 mm:Dsmax:0=30
-mm:Scmp:0=60 sc:smax:0=-5 sc:smax:1=20 sc:smin:0=-15 tr:kt:1=55 ts:SS:1=-65 ts:bbf:a=-20 ts:fbk:a=20 ts:offu:a=-45
-ts:p1:a=-50 ts:srcb:1=-20 ts:u7:a=-140 tt:E:a=-35 tt:SS:1=20 tt:Snr:0=-25 tt:cmp2:1=-20 tt:cmp:0'=-35 tt:dH:1=-30
-io:pi:a=900 as:I:a=800 as:B1:a=700 io:rr:a=600 as:Ash:a=500 io:jc:a=400 io:iot:a=300 me:ones:a=900 me:onesF:a=800
-me:Cmat:a=100 Vga:xg:1'@0=-100 ga:xg:1@0=200 ga:xg:1'@0=200 co:Tu:1@0=300 co:Hu:1@0=100 co:bu:1@0=200 tt:cmp:1@0=150
-tt:cmp:1'@0=120 co:Tu:0@0=300 co:bu:0@0=200 lo:X:a=900 lo:TTi:a=500 lo:Tin:a=500
-co:Hu:0@0=50 co:TT:1@0=15 co:X:a@0=-20 co:ju:a@0=-55 ga:e:0@0=-70 sc:smax:0'@0=-85 sc:smax:1'@0=-80 sc:smin:0'@0=-90
-sc:smin:0@0=30 tr:kt:0@0=-90 ts:SS:0'@0=45 ts:fbk:a@0=-90 ts:offu:a@0=-80 ts:p1:a@0=-15 ts:p2:a@0=-65 ts:srcb:1@0=35
-tt:E:a@0=-20 tt:SdH:0'@0=90 tt:cmp:0'@0=-30 tt:cmp:0@0=45 tt:cmp:1'@0=-30 tt:cmp:1@0=-65 tt:ki:1@0=15
-ac:hz:a=5 ac:nr:1=-85 co:Hu:0=-75 co:T1u:0'=175 co:TT:1=-15 co:Tu:0=95 co:bu:0=-25 ga:e:0=-30 ga:xg:1=-5 ga:xj:a=-55
-sc:smax:0=-50 sc:smax:1=50 sc:smin:1=-80 ts:Spar:0=55 ts:bbf:a=-15 ts:half:a=-120 ts:offu:a=-35 tt:SdH:0=45
-tt:SdH:0'=110 tt:Sland:0=-35 tt:cmp:0'=5 tt:free:1=75 tt:ki:0=90 tt:ki:1=-45
-ac:K:1=-25 ac:nr:1=55 co:Hu:1=-135 co:T1u:0=-35 co:TT:0=60 co:bu:0=50 co:bu:1=70 co:nu:1=-120 co:ui:a=25 ga:e:0=50
-ga:xg:0=-105 ga:xj:a=50 sc:smax:0=-15 sc:smax:0'=-15 sc:smax:1=-45 sc:smax:1'=-40 sc:smin:0'=-15 tr:kt:0=95
-ts:bi:1=-110 ts:half:a=-35 ts:srcb:1=20 tt:SS:0=-145 tt:SS:1=-10 tt:cmp:0'=-10 tt:cmp:1=-30 tt:free:1=-70
-"""
-CFG = {"nch": 2, "pw": 1024, "slack": 100.0, "tau": 2500.0, "flex": 1, "trans": 1, "raw": 0,
-       "ns": [0, 0], "f1": [64, 128], "f2": [128, 128], "mg": 1, "nrA": 1, "frA": 0, "xnA": 1, "up": {}}
-for _t in UP.split():
-    CFG["up"][_t.split("=")[0]] = CFG["up"].get(_t.split("=")[0], 0) + int(_t.split("=")[1])
+H = L // 2
+ORDER = ["""Hu:1 ki:0- bi:0- Hf:1 bs:0- cmp:1 cmp:1' nbb:a half:a- Hu:0 vb:a- Hf:0 sgn:1 prod:1 T1u:1 cmp:0 cmp:0'
+prod:0 smax:1 T1u:0 smin:1 E:a prod:0' smin:1' T1u:0' P:1 fbk:a ni:1 smax:1' nn:1 smin:0 nu:1 free:1 smax:0 nf:1 smin:0'
+offu:a P:0 smax:0' ni:0 q2:1 nn:0 cmp2:1a nu:0 nf:0 cmp2:1b cmp2:1c q8:a cmp2:1d ju:a cmp2:0b cmp2:0a prod2:1 q2:0 T2:1
+TT:1 T2u:1 TT:1 free:0 TT:1 TT:1 xb:a TT:1 kt:1 TT:1 TT:1 ks:1 TT:1 cmp2:0c cmp2:0d ki:1 Xsc:a bi:1 prod2:0 bs:1 T2:0
+TT:0 TT:0 TT:0 TT:0 TT:0 TT:0 kt:0 TT:0 ks:0 TT:0 T2u:0""",
+"""xg:1 xg:1' has:a- xg:0 bb:a xg:0' z:1 sgn:0 z:1' sgn:0' z:0 z:0' e:1 e:1' ab:1a e:0 ab:1b rdy:1 ab:1c xj:a ab:1d e:0'
+ab:0a ab:0b rdy:0 ab:0c ab:0d""",
+"""pD:1 pvote:1 ppar:a- pvote:1' pT1:1 pZd:a pD:0 pK:1 pvote:0 pT1:0 pvote:0' pT1:0' poff:a pK:0 pm:1 pM:1c pD2:1 pM:1a
+pd:1a pd:1b pu:a pc2:1a pD2:0 pd:1c pM:0a pj:a pc2:1b pc2:1c pc2:1d pk:1a pM:0c pd:1d pk:1b pm:0 pk:1c px:a pk:1d pkey:1
+pc2:0a pd:0a pc2:0b pd:0b psw:1 pc2:0c pc2:0d pd:0c pd:0d pk:0a pk:0b pk:0c pk:0d pkey:0 psw:0"""]
+CFG = {"pw": 1024, "slack": 100.0, "kpe": 0, "onV": ["sgn:1", "free:1", "free:0"], "cut": ["T1:0"], "up": {},
+       "order": ORDER}
 LOW = 2040 * 8192
 BANKS = ("S0", "S1", "M0", "M1", "D0", "D1", "KB", "Z")
 MAGIC = 12582912.0
-REF = {"f": 1.25, "g": 1.56, "s": 3.8, "ov": 40.0, "pe": 0.42, "lat": 100.0, "same": 50.0, "rem": 2200.0, "rb": 0.02,
+REF = {"f": 1.2, "g": 1.56, "s": 3.8, "ov": 50.0, "pe": 0.42, "lat": 150.0, "same": 100.0, "rem": 2200.0, "rb": 0.02,
        "dma": 1800.0, "db": 0.006, "tt2": 1.0}
+SCALED = (("negI", -1.0), ("I16", 16.0), ("I37", 37.0), ("Ipen", 2.0 ** 25), ("I2", 0.5), ("I4", 0.25), ("nI4", -0.25),
+          ("nI2", -0.5), ("Ipen2", 2.0 ** 26), ("I8x", 8.0), ("I8", 0.125), ("I16th", 0.0625), ("nI512", -512.0))
 
 
 def scratch(cfg):
-    w = L // cfg["nch"]; nc = w // 16
     s = {}
     def sb(names, n, dtp):
         for nm in names.split():
             s[nm] = ("sbuf", [128, n], dtp)
     sb("X", W, "bfloat16"); sb("TTi", B, "int32"); sb("TT", B + 16, "float32")
-    sb("Tin ni nn p1 xn", L, "int32"); sb("bin ki bi ui u7 ji jc j8", 16, "int32")
-    sb("cin0 cin1 cin2 cin3 cout0 cout1 cout2 cout3 p2 free nr E xj xb hz rr ones", L, "bfloat16")
-    for v in range(VISITS - 1):
-        sb("src%d land%d" % (v, v), L + 16, "int32")
-    sb("Tout dH m8 K kt ks maskK xr", L, "float32"); sb("bout fbk junk cols", 16, "float32")
-    sb("Tu Hu T1u nu", L, "uint16"); sb("bu ju", 16, "uint16"); sb("offu", 32, "uint16")
+    sb("Tin ni nn", L, "int32"); sb("bin ki bi jc", 16, "int32")
+    sb("cin0 cin1 cin2 cin3 cout0 cout1 cout2 cout3 sgn rdy free q2 E xj xb bb maskZ rr ones", L, "bfloat16")
+    sb("Tf0 Tf1 Tf2 Tf3 Ts0 Ts1 Ts2 Hf prod nf prod2", L, "float16"); sb("q8 j8", 16, "float16")
+    sb("bu0 bu1 bu2 bu3 bs0 bs1 bs2 ju", 16, "uint16"); sb("offu", 32, "uint16")
+    sb("Tu0 Tu1 Tu2 Tu3 Us0 Us1 Us2 Hu T1u nu", L, "uint16")
+    sb("Tout P kt ks", L, "float32"); sb("bout fbk cols", 16, "float32")
     sb("xg cmp z smin smax e cmp2 ab", 16 * L, "bfloat16")
-    sb("bbf nh", 16, "bfloat16"); sb("scol par", 8, "float32"); sb("half pi p15 h1", 8, "int32")
-    sb("I negI I16 I37 Ipen Iq BD Cmat", 128, "bfloat16"); sb("B1 B8 BH", 144, "bfloat16")
-    sb("onesF Ash A0 A1", 160, "float32"); sb("rmin rmax", cfg["pw"], "bfloat16"); sb("rk", w, "float32")
-    sb("iot", B, "float32")
+    sb("nbb has c35", 16, "bfloat16"); sb("scol vb", 8, "float32"); sb("half pi p15 h1", 8, "int32")
+    sb("I Cmat CK " + " ".join(nm for nm, _ in SCALED), 128, "bfloat16"); sb("B1 B8", 144, "bfloat16")
+    sb("onesF Ash A0 A1", 160, "float32"); sb("BDh rk", 128, "float32"); sb("rmin rmax", cfg["pw"], "bfloat16")
+    if cfg["kpe"]:
+        sb("selT", W, "bfloat16")
+    else:
+        sb("iot", B, "bfloat16")
     for b in BANKS:
         s[b] = ("psum", [128, 512], "float32")
     return s
@@ -70,7 +52,7 @@ def scratch(cfg):
 def semaphores(cfg):
     n = ["qV", "qA", "qP", "qG", "sent"] + ["ld%d" % i for i in range(5)] + ["st%d" % i for i in range(5)]
     for v in range(VISITS - 1):
-        n += ["arr%s%d_%d" % (x, v, ch) for ch in range(cfg["nch"]) for x in "Tb"] + ["arrc%d" % v]
+        n += ["arr%s%d_%d" % (x, v, ch) for ch in range(2) for x in "TUb"] + ["arrc%d" % v]
     return n
 
 
@@ -104,21 +86,21 @@ def parts(a):
 
 def program(cfg):
     sc = scratch(cfg)
-    nch, pw = cfg["nch"], cfg["pw"]
-    w = L // nch; nc = w // 16; pl = pw // 16
+    pw = cfg["pw"]
+    w = H; nc = w // 16; pl = pw // 16
     ops = []
-    cur = ["a", "@c"]
+    cur = ["a", "c"]
 
     def turns():
-        for ch in range(nch - 1, -1, -1):
+        for ch in (1, 0):
             cur[0] = str(ch)
             yield ch
         cur[0] = "a"
 
     def two(a):
-        return sc[a[0]][2] in ("bfloat16", "uint16") and sc[a[0]][0] == "sbuf"
+        return sc[a[0]][2] in ("bfloat16", "uint16", "float16") and sc[a[0]][0] == "sbuf"
 
-    def add(eng, kind, args, reads, writes, n, cls, **kw):
+    def add(eng, kind, args, reads, writes, n, cls, name=None, **kw):
         rd = []
         for a in reads:
             rd += parts(a)
@@ -129,13 +111,8 @@ def program(cfg):
             else:
                 wr.append(a)
         o = {"eng": eng, "kind": kind, "args": args, "rd": rd, "wr": wr, "n": n, "cls": cls}
-        a = wr[0] if wr else rd[0]
-        nm = a[0]
-        if nm in BANKS:
-            nm = nm[0] + (rd[-1][0].rstrip("012").replace("Tin", "land") if nm[0] in "DS" else str(a[1]) if nm == "Z" else "")
-        elif nm[:3] in ("src", "lan", "cin", "cou", "Tou"):
-            nm = nm[:3].replace("Tou", "src") + "Tb"[a[1] // L]
-        o["tag"] = "%s:%s:%s" % (kind[:2], nm, cur[0])
+        nm = (wr[0] if wr else rd[0])[0]
+        o["tag"] = "%s:%s" % (name or (nm[:-1] if nm[:-1] in ("Tf", "Tu", "bu", "bs", "cout", "cin") else nm), cur[0])
         o["vis"] = cur[1]
         o.update(kw); ops.append(o)
         return o
@@ -147,21 +124,23 @@ def program(cfg):
             return "g"
         return "h" if two(out) and all(two(a) for a in ins) else "c"
 
-    def copy(out, in_):
-        add("V", "copy", (out, in_), [in_], [out], cnt(in_ if out[0] == "ind" else out), cls_of(out, [in_]))
+    def copy(out, in_, name=None):
+        add("V", "copy", (out, in_), [in_], [out], cnt(in_ if out[0] == "ind" else out), cls_of(out, [in_]), name)
 
     def gather(out, win, off):
         a = ("ind", win, off)
-        add("F" if cfg["flex"] else "A", "gather", (out, a), [a], [out], cnt(out), "g")
+        tag = "%s:%s" % (out[0], cur[0])
+        eng = "V" if tag in cfg["onV"] or tag + "@" + cur[1] in cfg["onV"] else "A"
+        add(eng, "gather", (out, a), [a], [out], cnt(out), "g")
 
-    def tt(out, a, b, op):
+    def tt(out, a, b, op, name=None):
         c = cls_of(out, [a, b])
         if c in "hc" and sc[a[0]][0] == "sbuf" and sc[b[0]][0] == "sbuf":
             c = "t" + c
-        add("V", "tt", (out, a, b, op), [a, b], [out], cnt(out), c)
+        add("V", "tt", (out, a, b, op), [a, b], [out], cnt(out), c, name)
 
-    def ts(out, a, s1, s2, op0, op1=None):
-        add("V", "ts", (out, a, s1, s2, op0, op1), [a, s1, s2], [out], cnt(out), cls_of(out, [a]))
+    def ts(out, a, s1, s2, op0, op1=None, name=None):
+        add("V", "ts", (out, a, s1, s2, op0, op1), [a, s1, s2], [out], cnt(out), cls_of(out, [a]), name)
 
     def scan(out, d0, d1, op0, op1):
         add("V", "scan", (out, d0, d1, op0, op1), [d0, d1], [out], cnt(out), cls_of(out, [d0, d1]))
@@ -170,13 +149,16 @@ def program(cfg):
         add("A", "act", (out, in_, fn, bias, scale, acc), [in_, bias, scale], [out] + ([acc] if acc else []), cnt(out),
             "g" if in_[0] == "ind" else "c")
 
-    def pe(mms, grp=None):
+    def pe(name, mms, grp=None):
         cyc = 0
         rd, wr = [], []
         for o, l, r, st, sp in mms:
             cyc += max(64, cnt(r)) * (4 if sc[r[0]][2] == "float32" else 1)
             rd += [l, r]; wr.append(o)
-        add("P", "mm", mms, rd, wr, cyc, "p", grp=grp, first=mms[0][3], last=mms[-1][4])
+        return add("P", "mm", mms, rd, wr, cyc, "p", name, grp=grp, first=mms[0][3], last=mms[-1][4])
+
+    def acc(out, terms):
+        return [(out, l, r, i == 0, i == len(terms) - 1) for i, (l, r) in enumerate(terms)]
 
     def memset(out, val):
         add("V", "memset", (out, val), [], [out], cnt(out), "h" if two(out) else "c")
@@ -191,10 +173,10 @@ def program(cfg):
         add(q, "load", (buf, src), [], [buf], nbytes, "d", sem=("ld%d" % k, 16))
 
     def store(q, dst, buf, k, nbytes):
-        add(q, "store", (dst, buf), [buf], [], nbytes, "d", sem=("st%d" % k, 16))
+        add(q, "store", (dst, buf), [buf], [], nbytes, "d", "st" + dst, sem=("st%d" % k, 16))
 
     def send(src, dst, sem, nbytes):
-        add("G", "send", (src, dst, sem), [src], [dst], nbytes, "r", sem=(sem, None))
+        add("G", "send", (src, dst, sem), [src], [dst], nbytes, "r", "send" + sem[3], sem=(sem, None))
 
     def whole(nm):
         return R(nm, 0, sc[nm][1][1])
@@ -210,50 +192,49 @@ def program(cfg):
     asel(b1, R("ones", 0, 144), [[0, 9], [1, 16]], Op.is_equal, -15, 0)
     asel(b1, b1, [[1, 144]], Op.is_ge, 0, -1)
     asel(b1, b1, [[-1, 144]], Op.is_ge, 15, 1)
-    ts(whole("B8"), b1, 8192.0, None, Op.mult)
-    ts(whole("BH"), b1, 0.5, None, Op.mult)
+    act(whole("B8"), b1, Fn.Identity, 0.0, 8192.0)
     asel(I, R("ones", 0, 128), [[-1, 128]], Op.is_equal, 0, 1)
-    for nm, val in (("negI", -1.0), ("I16", 8.0 if cfg["frA"] else 16.0), ("Iq", -0.5), ("I37", 37.0), ("Ipen", -2.0 ** 26)):
-        ts(whole(nm), I, val, None, Op.mult)
+    for nm, val in SCALED:
+        act(whole(nm), I, Fn.Identity, 0.0, val)
     memset(whole("rmin"), 0.0); memset(R("rmin", 0, pw, 16), 255.0)
     memset(whole("rmax"), 255.0); memset(R("rmax", 0, pw, 16), 0.0)
     iota(whole("rr"), [[0, 16], [256, 16]], 0, 0)
-    iota(whole("iot"), [[1, B]], -256, 0)
+    if cfg["kpe"]:
+        memset(R("ab", 0, W), -37.0)
+        for q in range(4):
+            asel(R("selT", 512 * q, 512 * q + 512), R("ab", 0, 512), [[-1, 4], [-16, 8], [0, 16]], Op.is_equal, -4 * q, 1)
+    else:
+        iota(whole("iot"), [[1, B]], -256, 0)
     iota(R("pi", 0, 1), [[1, 1]], 0, 1)
     ts(R("p15", 0, 1), R("pi", 0, 1), 15, None, Op.bitwise_and)
-    ts(R("p15", 1, 2), R("pi", 0, 1), 3, None, Op.bitwise_and)
     ts(R("h1", 0, 1), R("pi", 0, 1), 4, 1, Op.logical_shift_right, Op.bitwise_and)
-    vcol, c512, c8, c256, h0f, h1f = [R("cols", i, i + 1) for i in range(6)]
-    t0 = 20.0 if cfg["frA"] else 28.0
-    thb = {}
-    for ns in sorted(set(cfg["ns"])):
-        thb[ns] = R("cols", 6 + len(thb), 7 + len(thb))
-        ts(thb[ns], R("p15", 1, 2), 4.0 - ns // 4, -8.0, Op.is_ge, Op.mult)
-        if cfg["nrA"]:
-            ts(thb[ns], thb[ns], 250.0, 250.0 * t0 - 125.0, Op.mult, Op.add)
-        else:
-            ts(thb[ns], thb[ns], t0, None, Op.add)
-    ts(vcol, R("p15", 0, 1), 613.0, 37.0 * 256 - 7.0 / 16, Op.mult, Op.add)
+    c512, c8, c256, h0f, h1f, cpar = [R("cols", i, i + 1) for i in range(6)]
     ts(c512, R("p15", 0, 1), float(B), None, Op.add)
     ts(c8, R("p15", 0, 1), 8.0, None, Op.mult)
     ts(c256, R("p15", 0, 1), 256.0, None, Op.mult)
     ts(h0f, R("h1", 0, 1), -1.0, 1.0, Op.mult, Op.add)
     ts(h1f, R("h1", 0, 1), 1.0, None, Op.mult)
+    memset(cpar, 136.5); memset(whole("c35"), -3.5)
     asel(whole("Ash"), whole("onesF"), [[-1, 160]], Op.is_equal, 16, 1)
-    ts(whole("A0"), whole("Ash"), h0f, None, Op.mult)
-    ts(whole("A1"), whole("Ash"), h1f, None, Op.mult)
-    bd = whole("BD")
-    asel(bd, R("ones", 0, 128), [[16, 8], [0, 16]], Op.is_ge, 15, -1)
+    act(whole("A0"), whole("Ash"), Fn.Identity, 0.0, h0f)
+    act(whole("A1"), whole("Ash"), Fn.Identity, 0.0, h1f)
+    bd = whole("BDh")
+    memset(bd, -0.5)
+    asel(bd, bd, [[16, 8], [0, 16]], Op.is_ge, 15, -1)
     asel(bd, bd, [[-16, 8], [0, 16]], Op.is_ge, 0, 1)
-    memset(whole("Cmat"), 0.0)
-    memset(R("Cmat", 0, 128, 1, 0, 1), -float(LOW))
-    iota(R("Cmat", 0, 128, 1, 32, 33), [[0, 8], [-512, 16]], 15 * 512 + 256, 0)
+    def row(nm, p):
+        return R(nm, 0, 128, 1, p, p + 1)
+    memset(whole("Cmat"), 0.0); memset(whole("CK"), 0.0)
+    memset(row("Cmat", 0), -float(LOW)); memset(row("Cmat", 64), -2.0 ** 25)
+    iota(row("Cmat", 32), [[0, 8], [-512, 16]], 144 * 512, 0)
+    memset(row("CK", 96), -7.0 / 16)
+    for p, step, base in ((0, 512, 37 * 256), (32, 96, 0), (64, 5, 0)):
+        iota(row("CK", p), [[0, 8], [step, 16]], base, 0)
     ts(whole("rk"), R("rmax", 0, w), 0.0, -2.0 ** 28, Op.is_equal, Op.mult)
-    ts(whole("maskK"), whole("rr"), c256, 0.25, Op.is_le, Op.mult)
-    ts(whole("maskK"), whole("maskK"), vcol, None, Op.add)
+    ts(whole("maskZ"), whole("rr"), c256, 0.5, Op.is_le, Op.mult)
     iota(whole("jc"), [[128, 16]], 0, 0)
     ts(whole("j8"), whole("jc"), c8, None, Op.add)
-    copy(R("TT", 0, B), whole("TTi"))
+    copy(R("TT", 0, B), whole("TTi"), "TTinit")
 
     def sel(nm, k):
         return R(nm, 15 - k, 143 - k)
@@ -262,165 +243,176 @@ def program(cfg):
     dturn = [0]
     for v in range(VISITS):
         last = v == VISITS - 1
-        cur[1] = "@%d" % v
+        cur[1] = str(v)
         tab = whole("TTi") if v == 0 else R("TT", 0, B)
-        def Tin(ch):
-            return R("Tin", ch * w, ch * w + w) if v == 0 else R("land%d" % (v - 1), ch * w, ch * w + w)
-        def bin_(ch):
-            return R("bin", ch * nc, ch * nc + nc) if v == 0 else R("land%d" % (v - 1), L + ch * nc, L + ch * nc + nc)
-        def Tout(ch, a, b):
-            return R("Tout" if last else "src%d" % v, ch * w + a, ch * w + b)
+        Tf, Tu, bu, cin, cout = "Tf%d" % v, "Tu%d" % v, "bu%d" % v, "cin%d" % v, "cout%d" % v
+        Tout = "Tout" if last else "Ts%d" % v
         def ln(nm, ch):
             return R(nm, ch * w, ch * w + w)
         def lc(nm, ch):
             return R(nm, ch * nc, ch * nc + nc)
         def ps(ch, k):
-            o = (ch // 2) * 3 * w + k * w
-            return R("S%d" % (ch % 2), o, o + w)
-        def pm(ch):
-            return R("M%d" % ch, 0, 512, 4)
+            return R("S%d" % ch, k * w, k * w + w)
         def strided(nm, ch, k):
             return R(nm, 16 * ch * w + k, 16 * (ch + 1) * w, 16)
         def pieces(ch):
-            return [(a, min(a + pl, (ch + 1) * w)) for a in range(ch * w, (ch + 1) * w, pl)]
-        cin, cout = "cin%d" % v, "cout%d" % v
-        for ch in turns():
-            copy(ln("Tu", ch), Tin(ch))
-            copy(lc("bu", ch), bin_(ch))
-            copy(ln("Hu", ch), ("ind", tab, lc("bu", ch)))
-            tt(ln("dH", ch), ("ind", tab, lc("bu", ch)), Tin(ch), Op.subtract)
-            act(ln("K", ch), ("ind", whole("iot"), lc("bu", ch)), Fn.Identity, vcol, 37.0)
+            for k, a in enumerate(range((ch + 1) * w - pl, ch * w - 1, -pl)):
+                cur[0] = "%d%s" % (ch, "'" * k)
+                yield a, a + pl
+            cur[0] = str(ch)
+        def cuts(nm, ch):
+            if "%s:%d" % (nm, ch) not in cfg["cut"]:
+                yield lambda r: r
+                return
             for a, b in pieces(ch):
-                cur[0] = "%d%s" % (ch, "'" * ((a - ch * w) // pl))
-                gather(R("xg", 16 * a, 16 * b), Xw, R("Tu", a, b))
+                lo, hi = a - ch * w, b - ch * w
+                yield lambda r: R(r[0], r[1] + lo * r[3], r[1] + (hi - 1) * r[3] + 1, r[3])
+        def t1(half, full, ch):
+            return [(whole(half), ln(Tf, ch)), (whole(half), ln("Hf", ch)), (whole(full), ln("prod", ch))]
+        def onV(nm, ch):
+            return "%s:%d" % (nm, ch) in cfg["onV"]
+        for ch in turns():
+            if v == 0:
+                copy(ln(Tu, ch), ln("Tin", ch))
+                ts(ln(Tf, ch), ln(Tu, ch), 0.0, None, Op.add)
+                copy(lc(bu, ch), lc("bin", ch))
+            copy(ln("Hu", ch), ("ind", tab, lc(bu, ch)))
+            ts(ln("Hf", ch), ln("Hu", ch), 0.0, None, Op.add)
+            plus, minus = ("I", "negI") if onV("sgn", ch) else ("nI2", "I2")
+            pe("pD", acc(ps(ch, 1), [(whole(plus), ln("Hf", ch)), (whole(minus), ln(Tf, ch))]))
+            for a, b in pieces(ch):
+                gather(R("xg", 16 * a, 16 * b), Xw, R(Tu, a, b))
                 tt(R("cmp", 16 * a, 16 * b), ("ind", Xw, R("Hu", a, b)), R("xg", 16 * a, 16 * b), Op.is_ge)
-        ball = whole("bin") if v == 0 else R("land%d" % (v - 1), L, L + 16)
-        ts(whole("bbf"), ball, -256.0, None, Op.add)
-        ts(whole("fbk"), ball, 97.0 - LOW - 8192, None, Op.add)
-        pe([(R("Z", 0, L), R("Ash", 16, 144), whole("maskK"), True, False)] +
-           [(R("Z", r, L, 16), whole("I37"), whole("bbf"), False, r == 15) for r in range(16)])
-        tt(whole("E"), R("Z", 0, L), whole("K"), Op.is_equal)
-        pe([(R("Z", 256, 272), I, whole("bbf"), True, False)] +
-           [(R("Z", 256, 272), sel("B8", r), R("E", r, L, 16), False, r == 15) for r in range(16)])
+        nbb = whole("nbb")
+        ts(nbb, whole(bu), -1.0, 256.0, Op.mult, Op.add)
+        ts(whole("fbk"), whole(bu), 97.0 - LOW - 8192, None, Op.add)
+        zd = R("Z", 0, L)
+        if cfg["kpe"]:
+            mm = [(R("Z", r, L, 16), R("selT", 128 * r, 128 * r + 128), nbb, False, False) for r in range(16)]
+        else:
+            act(whole("bb"), ("ind", whole("iot"), whole(bu)), Fn.Copy)
+            mm = [(zd, whole("I37"), whole("bb"), False, False)]
+        pe("pZd", [(zd, I, whole("maskZ"), True, False)] + mm +
+           [(R("Z", r, L, 16), whole("I37"), nbb, False, r == 15) for r in range(16)])
+        ts(whole("E"), zd, 0.0, None, Op.is_equal)
+        pe("poff", acc(R("Z", 256, 272), [(whole("negI"), nbb)] + [(sel("B8", r), R("E", r, L, 16)) for r in range(16)]))
         ts(R("offu", 0, 32, 2), R("Z", 256, 272), 256.0, c512, Op.add, Op.min)
         for ch in turns():
-            t1 = ps(ch, 0)
-            for a in range(0, w, 64):
-                pe([(R(t1[0], t1[1] + a, t1[1] + a + 64), sel("B1", k),
-                     R("cmp", 16 * (ch * w + a) + k, 16 * (ch * w + a + 64), 16), k == 0, k == 15) for k in range(16)])
-            def sub(r, a, b):
-                return R(r[0], r[1] + a * r[3], r[1] + (b - 1) * r[3] + 1, r[3])
-            s1 = cfg["f1"][ch]
-            for a in range(0, w, s1):
-                cur[0] = "%d%s" % (ch, "'" * (a // s1))
-                u = sub(t1, a, a + s1)
-                if v == 0:
-                    ts(u, u, 9.0, None, Op.is_ge)
-                else:
-                    ts(u, u, -9.0, R("par", v, v + 1), Op.add, Op.is_ge)
-                tt(u, u, sub(ln("dH", ch), a, a + s1), Op.mult)
-                tt(u, u, sub(Tin(ch), a, a + s1), Op.add)
-                copy(sub(ln("T1u", ch), a, a + s1), u)
-            cur[0] = str(ch)
+            tq, kq = ps(ch, 2), ps(ch, 3)
             for a, b in pieces(ch):
-                cur[0] = "%d%s" % (ch, "'" * ((a - ch * w) // pl))
+                pe("pvote", acc(R("KB", L + a, L + b), [
+                    (sel("B1", k), R("cmp", 16 * a + k, 16 * b, 16)) for k in range(16)]))
+            thr = 8.5 if v == 0 else R("vb", v, v + 1)
+            for u in cuts("T1", ch):
+                votes = u(R("KB", L + ch * w, L + ch * w + w))
+                if onV("sgn", ch):
+                    ts(u(ln("sgn", ch)), votes, thr, 0.5, Op.is_ge, Op.subtract)
+                else:
+                    act(u(ln("sgn", ch)), votes, Fn.Sign, thr, -1.0)
+                tt(u(ln("prod", ch)), u(ps(ch, 1)), u(ln("sgn", ch)), Op.mult)
+                pe("pT1", acc(u(tq), [(l, u(r)) for l, r in t1("I8", "I4", ch)]))
+                ts(u(ln("T1u", ch)), u(tq), 4.0, None, Op.mult)
+            mm = acc(kq, [(whole("CK"), R("ones", 0, w))] + t1("I16th", "I8", ch))
+            if cfg["kpe"]:
+                mm[1:1] = [(R(kq[0], kq[1] + r, kq[2], 16), R("selT", 128 * r, 128 * r + 128), lc("nbb", ch), False, False)
+                           for r in range(16)]
+            else:
+                mm[1:1] = [(kq, whole("I37"), ln("bb", ch), False, False)]
+            pe("pK", mm)
+            for a, b in pieces(ch):
                 zz = R("z", 16 * a, 16 * b)
                 gather(zz, Xw, R("T1u", a, b))
                 scan(R("smin", 16 * a, 16 * b), R("rmin", 0, 16 * (b - a)), zz, Op.max, Op.min)
                 scan(R("smax", 16 * a, 16 * b), R("rmax", 0, 16 * (b - a)), zz, Op.min, Op.max)
-            cur[0] = str(ch)
             m = strided("smin", ch, 15)
-            pe([(R("M%d" % ch, j, 512, 4), I, m, True, True) for j in range(4)])
-            act(ln(cout, ch), m, Fn.Copy)
-            s2 = cfg["f2"][ch]
-            for a in range(0, w, s2):
-                cur[0] = "%d%s" % (ch, "'" * (a // s2))
-                def u(r):
-                    return sub(r, a, a + s2)
-                act(u(ln("m8", ch)), u(m), Fn.Identity, 0.125, 0.25)
-                tt(u(ps(ch, 1)), u(t1), u(ln("m8", ch)), Op.mult)
-                tt(u(ln("ni", ch)), u(ps(ch, 1)), u(ln("K", ch)), Op.add)
+            for u in cuts("n", ch):
+                tt(u(ln("P", ch)), u(tq), u(m), Op.mult)
+                tt(u(ln("ni", ch)), u(kq), u(ln("P", ch)), Op.add)
                 ts(u(ln("nn", ch)), u(ln("ni", ch)), W - 1, None, Op.bitwise_and)
                 copy(u(ln("nu", ch)), u(ln("nn", ch)))
-            cur[0] = str(ch)
-            tt(ps(ch, 2), ln("nn", ch), t1, Op.subtract)
-            if cfg["frA"]:
-                o = ps(ch, 3)
-                pe([(o, I, m, True, False), (o, whole("negI"), ln(cin, ch), False, True)])
-                act(ln("free", ch), o, Fn.Sign, -0.5)
-            else:
-                tt(ln("free", ch), pm(ch), ln(cin, ch), Op.is_gt)
-            if not cfg["mg"]:
-                ts(ln("p1", ch), ln("ni", ch), B - 1, None, Op.bitwise_and)
-                ts(ln("p2", ch), ln("p1", ch), -256.0, None, Op.add)
             for a, b in pieces(ch):
-                cur[0] = "%d%s" % (ch, "'" * ((a - ch * w) // pl))
                 gather(R("e", 16 * a, 16 * b), Xw, R("nu", a, b))
-        if cfg["mg"]:
-            ts(whole("p1"), whole("ni"), B - 1, None, Op.bitwise_and)
-            ts(whole("p2"), whole("p1"), -256.0, None, Op.add)
+            if onV("free", ch):
+                pe("pm", acc(tq, [(I, m)]))
+                tt(ln("free", ch), tq, ln(cin, ch), Op.is_gt)
+            else:
+                pe("pm", acc(tq, [(I, m), (whole("negI"), ln(cin, ch))]))
+                act(ln("free", ch), tq, Fn.Sign, -0.5)
+            ts(ln("nf", ch), ln("nu", ch), 0.0, None, Op.add)
+            ts(ln("q2", ch), ln("nu", ch), 1.0 / B, 128.5 + 0.5 / B, Op.mult, Op.add)
+            full = onV("rdy", ch)
+            pe("pD2", acc(ps(ch, 1), t1(*(("nI2", "negI") if full else ("nI4", "nI2")), ch) +
+                          [(whole("I" if full else "I2"), ln("nf", ch))]) +
+               acc(ps(ch, 0), t1("I4", "I2", ch) + [(whole("I2"), ln("nf", ch))]))
+        asel(whole(cout), R("smin", 15, 16 * L, 16), [[0, L]], Op.is_ge, 0, 0)
         if not last:
             send(whole(cout), whole("cin%d" % (v + 1)), "arrc%d" % v, 128 * L * 2)
         else:
             store("S", "ylast", whole(cout), 0, 128 * L * 2)
-        pe([(R("Z", 272, 288), sel("B1", r), R("smax", 15 + 16 * r, 16 * L, 256), r == 0, r == 15) for r in range(16)])
-        copy(whole("ui"), R("Z", 272, 288))
-        ts(whole("u7"), whole("ui"), 7, None, Op.bitwise_and)
-        tt(whole("ji"), whole("u7"), whole("j8"), Op.add)
-        copy(whole("ju"), whole("ji"))
+        u = [(sel("B1", r), R("smax", 15 + 16 * r, 16 * L, 256)) for r in range(16)]
+        uj = R("Z", 272, 288)
+        pe("pu", acc(uj, u + [(I, whole("c35"))]))
+        ts(whole("q8"), uj, 8 * MAGIC, -8 * MAGIC, Op.add, Op.add)
+        uj = R("Z", 288, 304)
+        pe("pj", acc(uj, u + [(I, whole("j8")), (whole("negI"), whole("q8"))]))
+        copy(whole("ju"), uj)
         gather(whole("xj"), Xw, whole("ju"))
-        mm = [(R("Z", 0, L), I, whole("xj"), True, False), (R("Z", 0, L), I, R("smax", 15, 16 * L, 16), False, not cfg["xnA"])]
-        if cfg["xnA"]:
-            pe(mm + [(R("Z", 0, L), whole("Iq"), ones, False, True)])
-            act(whole("xr"), R("Z", 0, L), Fn.Identity, MAGIC, 0.5)
-            act(whole("xb"), whole("xr"), Fn.Identity, -MAGIC)
-            copy(("ind", Xw, whole("ju")), whole("xb"))
-        else:
-            pe(mm)
-            ts(whole("xn"), R("Z", 0, L), 0.5, -0.25, Op.mult, Op.add)
-            copy(("ind", Xw, whole("ju")), whole("xn"))
+        pe("px", acc(zd, [(whole("I2"), R("smax", 15, 16 * L, 16)), (whole("nI4"), ones), (whole("I2"), whole("xj"))]))
+        ts(whole("xb"), zd, MAGIC, -MAGIC, Op.add, Op.add)
+        copy(("ind", Xw, whole("ju")), whole("xb"), "Xsc")
         if last:
             store("S", "yclk", Xw, 1, 128 * W * 2)
         for ch in turns():
-            M = strided("smax", ch, 15)
-            def blk(nm, p, k=1):
-                return R(nm, 16 * ch * w + p * w, 16 * ch * w + (p + k) * w)
-            c2 = ps(ch, 1)
-            ns = cfg["ns"][ch]
-            m = strided("smin", ch, 15)
-            def diff(q, sub):
-                d = "D%d" % (dturn[0] % 2); dturn[0] += 1
-                pe([(R(d, 0, 512), I, R("e", 16 * ch * w + q, 16 * (ch + 1) * w, 4), True, False)] +
-                   [(R(d, j, 512, 4), whole("negI"), sub, False, j == 3) for j in range(4)])
-                return R(d, 0, 512)
+            def blk(nm, q):
+                return R(nm, 16 * ch * w + 512 * q, 16 * ch * w + 512 * (q + 1))
             def of(nm, q, j):
-                return R(nm, 16 * ch * w + 512 * q + j, 16 * ch * w + 512 * (q + 1), 4)
-            for q in range(3, -1, -1):
-                sign = 4 * q >= 16 - ns
-                if sign:
-                    act(blk("cmp2", 4 * q, 4), diff(q, m), Fn.Sign, 0.5)
-                else:
-                    tt(blk("cmp2", 4 * q, 4), R("e", 16 * ch * w + q, 16 * (ch + 1) * w, 4), R("M%d" % ch, 0, 512), Op.is_ge)
-                mm = [(c2, whole("I16"), ln("free", ch), False, True)] if q == 0 else []
-                pe([(c2, sel("BH" if sign else "B1", 4 * j + q), of("cmp2", q, j), q == 3 and j == 0, False)
-                    for j in range(4)] + mm, grp=("c", v, ch))
-            if cfg["nrA"]:
-                act(ln("nr", ch), c2, Fn.Sigmoid, thb[ns], -250.0)
-            else:
-                ts(ln("nr", ch), c2, thb[ns], None, Op.is_lt)
-            tt(ps(ch, 2), ps(ch, 2), ln("nr", ch), Op.mult)
-            tt(Tout(ch, 0, w), ln("nn", ch), ps(ch, 2), Op.subtract)
-            if not last:
-                send(Tout(ch, 0, w), R("land%d" % v, ch * w, ch * w + w), "arrT%d_%d" % (v, ch), 128 * w * 4)
-            for c in range(nc - 1, -1, -1):
-                cc = ch * nc + c
-                copy(("ind", whole("TT"), R("offu", 2 * cc, 2 * cc + 1)), Tout(ch, 16 * c, 16 * c + 16))
-            key = R("KB", ch * w, ch * w + w)
+                return R(nm, 16 * ch * w + 512 * q + j, 16 * ch * w + 512 * (q + 1), 8)
+            def eq(q):
+                o = 16 * ch * w + 1024 * (1 - q // 2)
+                return R("e", o + q % 2, o + 1024, 2)
+            def ends(nm, q):
+                o = 16 * ch * w + 1024 * (1 - q // 2)
+                return R(nm, o + 15, o + 1024, 16)
+            def part(r, q):
+                return R(r[0], r[1] + 64 * (1 - q // 2), r[1] + 64 * (1 - q // 2) + 64)
+            c2 = ps(ch, 3)
             for q in range(4):
-                act(blk("ab", 4 * q, 4), diff(q, M), Fn.Abs)
-                mm = [(key, whole("Cmat"), R("ones", 0, w), True, False)] if q == 0 else []
-                pe(mm + [(key, sel("B8", 4 * j + q), of("ab", q, j), False, False) for j in range(4)], grp=("k", v, ch))
-            pe([(key, I, ln("p2", ch), False, False), (key, whole("Ipen"), ln("nr", ch), False, True)], grp=("k", v, ch))
+                cur[0] = "%d%s" % (ch, "abcd"[q])
+                mb = "M%d" % (q // 2)
+                if q % 2 == 0:
+                    pe("pM", [(R(mb, j, 512, 8), I, ends("smin", q), True, True) for j in range(8)])
+                tt(blk("cmp2", q), eq(q), R(mb, 0, 512), Op.is_ge)
+                mm = [(c2, whole("I16" if onV("free", ch) else "I8x"), ln("free", ch), True, False)] if q == 0 else []
+                pe("pc2", mm + [(part(c2, q), sel("B1", 2 * j + q % 2), of("cmp2", q, j), False, q == 3 and j == 7)
+                                for j in range(8)], grp=("c", v, ch))
+            cur[0] = str(ch)
+            thr = 27.5 if onV("free", ch) else 19.5
+            if onV("rdy", ch):
+                ts(ln("rdy", ch), c2, thr, 0.5, Op.is_ge, Op.subtract)
+            else:
+                act(ln("rdy", ch), c2, Fn.Sign, -thr)
+            tt(ln("prod2", ch), ps(ch, 1), ln("rdy", ch), Op.mult)
+            tt(ln(Tout, ch), ps(ch, 0), ln("prod2", ch), Op.add, "T2")
+            if not last:
+                ts(ln("Us%d" % v, ch), ln(Tout, ch), 0.0, None, Op.add, name="T2u")
+                send(ln("Us%d" % v, ch), ln("Tu%d" % (v + 1), ch), "arrU%d_%d" % (v, ch), 128 * w * 2)
+                send(ln(Tout, ch), ln("Tf%d" % (v + 1), ch), "arrT%d_%d" % (v, ch), 128 * w * 2)
+            for cc in range(ch * nc + nc - 1, ch * nc - 1, -1):
+                copy(("ind", whole("TT"), R("offu", 2 * cc, 2 * cc + 1)), R(Tout, 16 * cc, 16 * cc + 16))
+            key = ln("KB", ch)
+            for q in range(4):
+                cur[0] = "%d%s" % (ch, "abcd"[q])
+                d = R("D%d" % (dturn[0] % 2), 0, 512); dturn[0] += 1
+                pe("pd", [(d, I, eq(q), True, False)] +
+                   [(R(d[0], j, 512, 8), whole("negI"), ends("smax", q), False, j == 7) for j in range(8)])
+                act(blk("ab", q), d, Fn.Abs)
+                mm = [(key, whole("Cmat"), R("ones", 0, w), True, False),
+                      (key, whole("nI512"), ln("q2", ch), False, False)] if q == 0 else []
+                pe("pk", mm + [(part(key, q), sel("B8", 2 * j + q % 2), of("ab", q, j), False, False) for j in range(8)],
+                   grp=("k", v, ch))
+            cur[0] = str(ch)
+            pe("pkey", [(key, whole("Ipen2" if onV("rdy", ch) else "Ipen"), ln("rdy", ch), False, False),
+                        (key, I, ln("nf", ch), False, True)], grp=("k", v, ch))
             add("V", "tr", (ln("kt", ch), key), [key], [ln("kt", ch)], w, "c")
             scan(ln("ks", ch), whole("rk"), ln("kt", ch), Op.add, Op.max)
             sw = 304 + ch * nc
@@ -428,26 +420,26 @@ def program(cfg):
             for h in (0, 1):
                 o = R("Z", sw + h, sw + nc, 2)
                 far = 32 * h
-                mm += [(o, R("A%d" % h, 16, 144), R("ks", ch * w + 15 + 16 * h, ch * w + w, 32), True, False),
-                       (o, R("A%d" % h, far, far + 128), R("ks", ch * w + 31 - 16 * h, ch * w + w, 32), False, True)]
-            pe(mm)
+                mm += acc(o, [(R("A%d" % h, 16, 144), R("ks", ch * w + 15 + 16 * h, ch * w + w, 32)),
+                              (R("A%d" % h, far, far + 128), R("ks", ch * w + 31 - 16 * h, ch * w + w, 32))])
+            pe("psw", mm)
             tt(lc("ki", ch), R("Z", sw, sw + nc), lc("fbk", ch), Op.max)
+            ts(lc("bi", ch), lc("ki", ch), B - 1, None, Op.bitwise_and)
             if last:
-                ts(lc("bi", ch), lc("ki", ch), B - 1, None, Op.bitwise_and)
                 copy(lc("bout", ch), lc("bi", ch))
             else:
-                bo = L + ch * nc
-                ts(R("src%d" % v, bo, bo + nc), lc("ki", ch), B - 1, None, Op.bitwise_and)
-                send(R("src%d" % v, bo, bo + nc), R("land%d" % v, bo, bo + nc), "arrb%d_%d" % (v, ch), 128 * nc * 4)
+                copy(lc("bs%d" % v, ch), lc("bi", ch))
+                send(lc("bs%d" % v, ch), lc("bu%d" % (v + 1), ch), "arrb%d_%d" % (v, ch), 128 * nc * 2)
         if last:
             store("S", "ytrav", whole("Tout"), 2, 128 * L * 4)
             store("S", "yttab", R("TT", 0, B), 3, 128 * B * 4)
             store("A", "yslot", whole("bout"), 4, 128 * 64)
         else:
-            pe([(R("Z", 0, L), bd, whole("nr"), True, True)])
-            act(whole("hz"), R("Z", 0, L), Fn.Relu, -15.0, acc=R("scol", 0, 1))
-            ts(R("half", 0, 1), R("scol", 0, 1), 0.5, -0.25, Op.mult, Op.add)
-            ts(R("par", v + 1, v + 2), R("half", 0, 1), -2.0, R("scol", 0, 1), Op.mult, Op.add)
+            act(whole("has"), R("Z", 304, 320), Fn.Sign, LOW + 8192.0, acc=R("scol", 0, 1))
+            y = R("Z", 320, 321)
+            pe("ppar", acc(y, [(bd, R("scol", 0, 1)), (R("Ash", 16, 144), cpar)]))
+            ts(R("half", 0, 1), y, 0.5, -4.5, Op.mult, Op.add)
+            ts(R("vb", v + 1, v + 2), R("half", 0, 1), -2.0, y, Op.mult, Op.add)
     seen = {}
     for i, o in enumerate(ops):
         dep = set()
@@ -455,13 +447,10 @@ def program(cfg):
             for lo, hi, j, wr in seen.get(a[0], []):
                 if wr and lo < a[2] and a[1] < hi:
                     dep.add(j)
-        o["raw"] = set(dep) if cfg["raw"] else None
         for a in o["wr"]:
             for lo, hi, j, wr in seen.get(a[0], []):
                 if lo < a[2] and a[1] < hi:
                     dep.add(j)
-                    if wr and cfg["raw"]:
-                        o["raw"].add(j)
         for a in o["wr"]:
             if a[3] == 1 and a[4] == 0 and a[5] == 128:
                 seen[a[0]] = [t for t in seen.get(a[0], []) if not (a[1] <= t[0] and t[1] <= a[2])]
@@ -469,6 +458,8 @@ def program(cfg):
             seen.setdefault(a[0], []).append((a[1], a[2], i, True))
         for a in o["rd"]:
             seen.setdefault(a[0], []).append((a[1], a[2], i, False))
+        if o.get("grp") and o["last"]:
+            dep.update(j for j in range(i) if ops[j].get("grp") == o["grp"])
         dep.discard(i)
         o["dep"] = sorted(dep)
         o["banks"] = sorted(set(a[0] for a in o["rd"] + o["wr"] if a[0] in BANKS))
@@ -494,52 +485,68 @@ def cost(o, eng, m):
     return t, t
 
 
-def loose(o, j, a, b):
-    return a == b and (a == "P" or (a in "VA" and o["raw"] is not None and j not in o["raw"] and o["cls"] != "d"))
-
-
-def gap(o, j, a, b, m):
-    if loose(o, j, a, b):
-        return 0.0
-    return m["same"] if a == b else m["lat"]
+def gap(a, b, m):
+    if a == b:
+        return 0.0 if a == "P" else m["same"]
+    return m["lat"]
 
 
 def schedule(ops, cfg, m):
     n = len(ops)
+    on = [o["eng"] for o in ops]
     succ = [[] for _ in ops]
+    after = [set(o["dep"]) for o in ops]
+    named = {}
     for i, o in enumerate(ops):
-        for j in o["dep"]:
+        named.setdefault((o["tag"], o["vis"]), []).append(i)
+    for line in cfg["order"]:
+        chain = []
+        for v in range(-1, VISITS + 1):
+            words = line.split()
+            for k, t in enumerate(words):
+                have = named.get((t.rstrip("+-"), str(v + t.count("+") - t.count("-"))), [])
+                first = words[:k].count(t)
+                chain += have[first:first + 1] if t in words[k + 1:] else have[first:]
+        for j, i in zip(chain, chain[1:]):
+            after[i].add(j)
+    for i in range(n):
+        for j in after[i]:
             succ[j].append(i)
+    back, left = [], [len(a) for a in after]
+    todo = [i for i in range(n) if not left[i]]
+    while todo:
+        i = todo.pop(); back.append(i)
+        for j in succ[i]:
+            left[j] -= 1
+            if not left[j]:
+                todo.append(j)
+    assert len(back) == n
     rank = [0.0] * n
-    for i in range(n - 1, -1, -1):
-        rank[i] = cost(ops[i], "A", m)[1] + max([rank[j] + m["lat"] for j in succ[i]] + [0.0])
+    for i in reversed(back):
+        hold, fin = cost(ops[i], on[i], m)
+        rank[i] = max([fin] + [rank[j] + (fin + gap(on[i], on[j], m) if i in ops[j]["dep"] else hold) for j in succ[i]])
     up = cfg["up"]
-    prio = [rank[i] + 100.0 * (up.get(o["tag"], 0) + up.get(o["tag"] + o["vis"], 0)) for i, o in enumerate(ops)]
-    tau = [cfg["tau"] + 100.0 * (up.get("V" + o["tag"], 0) + up.get("V" + o["tag"] + o["vis"], 0)) for o in ops]
-    left = [len(o["dep"]) for o in ops]
+    prio = [rank[i] + 100.0 * (up.get(o["tag"], 0) + up.get(o["tag"] + "@" + o["vis"], 0)) for i, o in enumerate(ops)]
+    left = [len(a) for a in after]
     ready = [i for i in range(n) if left[i] == 0]
-    done = [0.0] * n; on = [None] * n; extra = [[] for _ in ops]
+    done = [0.0] * n; extra = [[] for _ in ops]
     free = {e: 0.0 for e in "VAPGS"}
     lastb = {b: {} for b in BANKS}; opened = {}
     seq = []; lastg = []; fed = {}
     while ready:
         cand = {e: [] for e in "VAPGS"}
         for i in ready:
-            o = ops[i]
-            if o["eng"] == "P" and o["first"] and any(b in opened for b in o["banks"]):
+            o = ops[i]; e = on[i]
+            if e == "P" and o["first"] and any(b in opened for b in o["banks"]):
                 continue
-            for e in ("AV" if o["eng"] == "F" else o["eng"]):
-                if (i, e) not in fed:
-                    fed[i, e] = max([done[j] + gap(o, j, on[j], e, m) for j in o["dep"]] + [0.0])
-                t = max(free[e], fed[i, e])
-                for b in o["banks"]:
-                    for e2, j in lastb[b].items():
-                        if e2 != e:
-                            t = max(t, done[j] + m["lat"])
-                if o["eng"] == "F" and e == "V":
-                    cand[e].append((t + max(0.0, tau[i]), i, t))
-                else:
-                    cand[e].append((t, i, t))
+            if i not in fed:
+                fed[i] = max([done[j] + gap(on[j], e, m) for j in o["dep"]] + [0.0])
+            t = max(free[e], fed[i])
+            for b in o["banks"]:
+                for e2, j in lastb[b].items():
+                    if e2 != e:
+                        t = max(t, done[j] + m["lat"])
+            cand[e].append((t, i))
         best = None
         for e in "VAPGS":
             if cand[e]:
@@ -547,10 +554,10 @@ def schedule(ops, cfg, m):
                 c = max((c for c in cand[e] if c[0] <= t0 + cfg["slack"]), key=lambda c: prio[c[1]])
                 if best is None or t0 < best[0]:
                     best = (t0, e, c)
-        e, i, t = best[1], best[2][1], best[2][2]
+        e, (t, i) = best[1], best[2]
         o = ops[i]
         hold, fin = cost(o, e, m)
-        free[e] = t + hold; done[i] = t + fin; on[i] = e
+        free[e] = t + hold; done[i] = t + fin
         if o["kind"] in ("iota", "asel"):
             extra[i] += lastg; lastg[:] = [i]
         for b in o["banks"]:
@@ -570,40 +577,28 @@ def schedule(ops, cfg, m):
     return seq, on, extra, max(done)
 
 
-def replay(ops, seq, on, extra, m):
-    free = {e: 0.0 for e in "VAPGS"}; done = {}; busy = {e: 0.0 for e in "VAPGS"}
-    for i in seq:
-        e = on[i]; t = free[e]
-        for j in ops[i]["dep"] + extra[i]:
-            t = max(t, done[j] + gap(ops[i], j, on[j], e, m))
-        hold, fin = cost(ops[i], e, m)
-        free[e] = t + hold; done[i] = t + fin; busy[e] += hold
-    return max(done.values()), busy, done
-
-
 def plan(cfg):
     ops = program(cfg)
     seq, on, extra, _ = schedule(ops, cfg, REF)
-    pos = {}; num = {e: 0 for e in "VAPGS"}
-    for i in seq:
-        num[on[i]] += 1; pos[i] = num[on[i]]
+    pos = {}; num = {e: 0 for e in "VAPGS"}; at = {}
+    for k, i in enumerate(seq):
+        num[on[i]] += 1; pos[i] = num[on[i]]; at[i] = k
     known = {e: {} for e in "VAPGS"}; clock = {}; waits = {}; signals = set()
     for i in seq:
         e = on[i]; need = {}
         for j in ops[i]["dep"] + extra[i]:
-            if loose(ops[i], j, on[j], e) and "sem" not in ops[j]:
+            if on[j] == e == "P":
                 continue
             key = ops[j]["sem"][0] if "sem" in ops[j] else on[j]
             if known[e].get(key, 0) < pos[j] and (key not in need or pos[need[key]] < pos[j]):
                 need[key] = j
-        js = sorted(need.values(), key=lambda j: -seq.index(j))
         ws = []
-        for j in js:
+        for j in sorted(need.values(), key=lambda j: -at[j]):
             key = ops[j]["sem"][0] if "sem" in ops[j] else on[j]
             if known[e].get(key, 0) >= pos[j]:
                 continue
             ws.append(j); signals.add(j)
-            for k2, val in (clock[j].items() if cfg["trans"] else [(key, pos[j])]):
+            for k2, val in clock[j].items():
                 known[e][k2] = max(known[e].get(k2, 0), val)
         waits[i] = ws
         if ops[i]["kind"] == "send":

@@ -3,25 +3,28 @@ from concourse.mybir import AluOpType as Op, ActivationFunctionType as Fn
 NR, VISITS, STEP = 8, 4, 5
 W, B, L = 2048, 512, 256
 H = L // 2
-ORDER = ["""Hu:1 ki:0- bi:0- Hf:1 bs:0- cmp:1 cmp:1' nbb:a half:a- Hu:0 vb:a- Hf:0 sgn:1 prod:1 T1u:1 cmp:0 cmp:0'
-prod:0 smax:1 T1u:0 smin:1 E:a prod:0' smin:1' T1u:0' P:1 fbk:a ni:1 smax:1' nn:1 smin:0 nu:1 free:1 smax:0 nf:1 smin:0'
-offu:a P:0 smax:0' ni:0 q2:1 nn:0 cmp2:1a nu:0 nf:0 cmp2:1b cmp2:1c q8:a cmp2:1d ju:a cmp2:0b cmp2:0a prod2:1 q2:0 T2:1
-TT:1 T2u:1 TT:1 free:0 TT:1 TT:1 xb:a TT:1 kt:1 TT:1 TT:1 ks:1 TT:1 cmp2:0c cmp2:0d ki:1 Xsc:a bi:1 prod2:0 bs:1 T2:0
-TT:0 TT:0 TT:0 TT:0 TT:0 TT:0 kt:0 TT:0 ks:0 TT:0 T2u:0""",
-"""xg:1 xg:1' has:a- xg:0 bb:a xg:0' z:1 sgn:0 z:1' sgn:0' z:0 z:0' e:1 e:1' ab:1a e:0 ab:1b rdy:1 ab:1c xj:a ab:1d e:0'
-ab:0a ab:0b rdy:0 ab:0c ab:0d""",
-"""pD:1 pvote:1 ppar:a- pvote:1' pT1:1 pZd:a pD:0 pK:1 pvote:0 pT1:0 pvote:0' pT1:0' poff:a pK:0 pm:1 pM:1c pD2:1 pM:1a
-pd:1a pd:1b pu:a pc2:1a pD2:0 pd:1c pM:0a pj:a pc2:1b pc2:1c pc2:1d pk:1a pM:0c pd:1d pk:1b pm:0 pk:1c px:a pk:1d pkey:1
-pc2:0a pd:0a pc2:0b pd:0b psw:1 pc2:0c pc2:0d pd:0c pd:0d pk:0a pk:0b pk:0c pk:0d pkey:0 psw:0"""]
-CFG = {"pw": 1024, "slack": 100.0, "kpe": 0, "onV": ["sgn:1", "free:1", "free:0"], "cut": ["T1:0"], "up": {},
+ORDER = ["""ki:0- bi:0- Hu:1 bs:0- cmp:1 cmp:1' half:a- TTinit:a Hf:1 vb:a- Hu:0 sgn:1 prod:1 fbk:a Hf:0 T1u:1 cmp:0 cmp:0'
+sgn:0 nbb:a prod:0 smin:1 T1u:0 smin:1' sgn:0' P:1 prod:0' ni:1 nn:1 T1u:0' smax:1 E:a nu:1 smax:0 smax:0' nf:1 smin:0'
+smin:0 cmp2:1b cmp2:1a P:0 free:1 ni:0 q8:a nn:0 u7:a nu:0 cmp2:1c cmp2:1d q2:a offu:a nf:0 ju:a e:0x xj:a rdy:1 cmp2:0b
+prod2:1 cmp2:0a kt:1 T2:1 ks:1 TT:1 free:0 T2u:1 cmp2:0c xb:a ki:1 TT:1 cmp2:0d bi:1 Xsc:a bs:1 rdy:0 TT:1 prod2:0 TT:1
+T2:0 kt:0 TT:0 ks:0 TT:0 T2u:0 TT:0 TT:0""",
+"""xg:1 xg:1' has:a- xg:0 bb:a xg:0' z:1 z:1' z:0 z:0' e:1 e:1' ab:1a ab:1b e:0 ab:1c ab:1d e:0' ab:0b ab:0a ab:0d ab:0c""",
+"""ppar:a- pvote:1 pvote:1' pD:1 pT1:1 pvote:0 pD:0 pK:1 pZd:a pT1:0 pvote:0' pZd:a pT1:0' pZd:a pM:1c pM:1a pK:0 pm:1
+poff:a poff:a poff:a pu:a pD2:1 pd:1b pd:1a pM:0a pc2:1a pc2:1b pm:0 pd:1c pj:a pd:1d pc2:1c pk:1a pc2:1d pk:1b pD2:0
+pk:1c pd:0a pk:1d pkey:1 pM:0c pd:0b psw:1 pc2:0a pc2:0b pd:0d pd:0c pk:0a pc2:0c pc2:0d pk:0b pk:0c pk:0d pkey:0 psw:0"""]
+CFG = {"pw": 1024, "slack": 100.0, "kpe": 0, "onV": ["free:1", "free:0", "e:0x", "rdy:0", "sgn:1", "rdy:1", "sgn:0"],
+       "cut": ["T1:0"], "up": {}, "free": [], "share": {"e:0": 16}, "xjV": 1, "dd": 0, "sides": 1,
+       "merge": ["smax:1", "q2"], "pair": 1, "two": 0, "onA": {}, "u3": 1, "wide": [], "mb": ["M0", "M1", "M0", "M1"],
        "order": ORDER}
 LOW = 2040 * 8192
-BANKS = ("S0", "S1", "M0", "M1", "D0", "D1", "KB", "Z")
+ZS = 384
+BANKS = ("S0", "S1", "M0", "M1", "D0", "D1", "KB", "Z", "DD")
 MAGIC = 12582912.0
-REF = {"f": 1.2, "g": 1.56, "s": 3.8, "ov": 50.0, "pe": 0.42, "lat": 150.0, "same": 100.0, "rem": 2200.0, "rb": 0.02,
+REF = {"f": 1.2, "g": 1.56, "s": 3.8, "ov": 50.0, "ova": 150.0, "pov": 0.0, "pe": 0.42, "lat": 150.0, "same": 100.0, "rem": 2200.0, "rb": 0.02,
        "dma": 1800.0, "db": 0.006, "tt2": 1.0}
-SCALED = (("negI", -1.0), ("I16", 16.0), ("I37", 37.0), ("Ipen", 2.0 ** 25), ("I2", 0.5), ("I4", 0.25), ("nI4", -0.25),
-          ("nI2", -0.5), ("Ipen2", 2.0 ** 26), ("I8x", 8.0), ("I8", 0.125), ("I16th", 0.0625), ("nI512", -512.0))
+SCALED = (("negI", -1.0), ("I16", 16.0), ("I37", 37.0), ("Ipen", 2.0 ** 26), ("I2", 0.5), ("I4", 0.25), ("nI4", -0.25),
+          ("I8", 0.125), ("nI512", -512.0))
+STEEP = 256.0
 
 
 def scratch(cfg):
@@ -29,28 +32,33 @@ def scratch(cfg):
     def sb(names, n, dtp):
         for nm in names.split():
             s[nm] = ("sbuf", [128, n], dtp)
-    sb("X", W, "bfloat16"); sb("TTi", B, "int32"); sb("TT", B + 16, "float32")
-    sb("Tin ni nn", L, "int32"); sb("bin ki bi jc", 16, "int32")
-    sb("cin0 cin1 cin2 cin3 cout0 cout1 cout2 cout3 sgn rdy free q2 E xj xb bb maskZ rr ones", L, "bfloat16")
+    sb("X0 X1", W, "bfloat16"); sb("TTi", B, "int32"); sb("TT", B + 32, "float32")
+    sb("Tin ni nn xn", L, "int32"); sb("bin ki bi jc", 16, "int32"); sb("E maskZ", ZS, "bfloat16")
+    sb("cin0 cin1 cin2 cin3 cout0 cout1 cout2 cout3 sgn rdy free q2 xj xb bb rr ones", L, "bfloat16")
     sb("Tf0 Tf1 Tf2 Tf3 Ts0 Ts1 Ts2 Hf prod nf prod2", L, "float16"); sb("q8 j8", 16, "float16")
     sb("bu0 bu1 bu2 bu3 bs0 bs1 bs2 ju", 16, "uint16"); sb("offu", 32, "uint16")
     sb("Tu0 Tu1 Tu2 Tu3 Us0 Us1 Us2 Hu T1u nu", L, "uint16")
-    sb("Tout P kt ks", L, "float32"); sb("bout fbk cols", 16, "float32")
+    sb("Tout P kt ks xr", L, "float32"); sb("bout fbk cols", 16, "float32")
     sb("xg cmp z smin smax e cmp2 ab", 16 * L, "bfloat16")
-    sb("nbb has c35", 16, "bfloat16"); sb("scol vb", 8, "float32"); sb("half pi p15 h1", 8, "int32")
+    sb("nB8", 144, "bfloat16"); sb("xs", L, "float16"); sb("xu", L, "uint16")
+    sb("nbb has c35 u7 c272", 16, "bfloat16"); sb("scol vb", 8, "float32"); sb("half pi p15 h1", 8, "int32")
     sb("I Cmat CK " + " ".join(nm for nm, _ in SCALED), 128, "bfloat16"); sb("B1 B8", 144, "bfloat16")
-    sb("onesF Ash A0 A1", 160, "float32"); sb("BDh rk", 128, "float32"); sb("rmin rmax", cfg["pw"], "bfloat16")
+    sb("onesF Ash A0 A1", 160, "float32"); sb("BDh rk", 128, "float32");
+    for nm in ("min", "max"):
+        sb("r" + nm, 2048 if any(t[:4] == "s" + nm for t in cfg["merge"]) else 1024, "bfloat16")
     if cfg["kpe"]:
         sb("selT", W, "bfloat16")
     else:
         sb("iot", B, "bfloat16")
     for b in BANKS:
-        s[b] = ("psum", [128, 512], "float32")
+        if b[0] != "D" or (b == "DD") == bool(cfg["dd"]):
+            s[b] = ("psum", [128, 1024 if b == "DD" else 512], "float32")
     return s
 
 
 def semaphores(cfg):
     n = ["qV", "qA", "qP", "qG", "sent"] + ["ld%d" % i for i in range(5)] + ["st%d" % i for i in range(5)]
+    n += ["dup%d" % v for v in range(VISITS) if cfg["two"]]
     for v in range(VISITS - 1):
         n += ["arr%s%d_%d" % (x, v, ch) for ch in range(2) for x in "TUb"] + ["arrc%d" % v]
     return n
@@ -130,6 +138,12 @@ def program(cfg):
     def gather(out, win, off):
         a = ("ind", win, off)
         tag = "%s:%s" % (out[0], cur[0])
+        k = cfg["share"].get(tag)
+        if k:
+            cur[0] += "x"
+            gather(R(out[0], out[2] - 16 * k, out[2]), win, R(off[0], off[2] - k, off[2]))
+            cur[0] = cur[0][:-1]
+            out = R(out[0], out[1], out[2] - 16 * k); a = ("ind", win, R(off[0], off[1], off[2] - k))
         eng = "V" if tag in cfg["onV"] or tag + "@" + cur[1] in cfg["onV"] else "A"
         add(eng, "gather", (out, a), [a], [out], cnt(out), "g")
 
@@ -181,70 +195,81 @@ def program(cfg):
     def whole(nm):
         return R(nm, 0, sc[nm][1][1])
 
-    load("S", whole("X"), "clk", 0, 128 * W * 2 + 128 * L * 4)
+    load("S", whole("X0"), "clk", 0, 128 * W * 2 + 128 * L * 4)
     load("A", whole("Tin"), "trav", 1, 128 * L * 8)
     load("A", whole("bin"), "slot", 2, 128 * L * 8)
     load("S", whole("TTi"), "ttab", 3, 128 * W * 2 + 128 * (L + B) * 4)
     load("S", whole("cin0"), "last", 4, 128 * W * 2 + 128 * (L + B) * 4 + 128 * L * 2)
     I, ones = whole("I"), whole("ones")
-    memset(ones, 1.0); memset(whole("onesF"), 1.0)
+    memset(ones, 1.0)
+    iota(R("pi", 0, 1), [[1, 1]], 0, 1)
+    c512, c8, c256, h0f, h1f, cpar, c528 = [R("cols", i, i + 1) for i in range(7)]
+    ts(R("h1", 0, 1), R("pi", 0, 1), 4, 1, Op.logical_shift_right, Op.bitwise_and)
+    ts(h1f, R("h1", 0, 1), 1.0, None, Op.mult)
+    ts(h0f, R("h1", 0, 1), -1.0, 1.0, Op.mult, Op.add)
+    iota(whole("jc"), [[128, 16]], 0, 0)
+    asel(I, R("ones", 0, 128), [[-1, 128]], Op.is_equal, 0, 1)
+    for nm, val in SCALED:
+        act(whole(nm), I, Fn.Identity, 0.0, 8.0 if nm == "I16" and "free" in cfg["merge"] else val)
+    memset(whole("onesF"), 1.0)
+    asel(whole("Ash"), whole("onesF"), [[-1, 160]], Op.is_equal, 16, 1)
+    ts(whole("A0"), whole("Ash"), h0f, None, Op.mult)
+    ts(whole("A1"), whole("Ash"), h1f, None, Op.mult)
+    iota(whole("rr"), [[0, 16], [256, 16]], 0, 0)
     b1 = whole("B1")
     asel(b1, R("ones", 0, 144), [[0, 9], [1, 16]], Op.is_equal, -15, 0)
     asel(b1, b1, [[1, 144]], Op.is_ge, 0, -1)
     asel(b1, b1, [[-1, 144]], Op.is_ge, 15, 1)
-    act(whole("B8"), b1, Fn.Identity, 0.0, 8192.0)
-    asel(I, R("ones", 0, 128), [[-1, 128]], Op.is_equal, 0, 1)
-    for nm, val in SCALED:
-        act(whole(nm), I, Fn.Identity, 0.0, val)
-    memset(whole("rmin"), 0.0); memset(R("rmin", 0, pw, 16), 255.0)
-    memset(whole("rmax"), 255.0); memset(R("rmax", 0, pw, 16), 0.0)
-    iota(whole("rr"), [[0, 16], [256, 16]], 0, 0)
+    ts(whole("B8"), b1, 8192.0, None, Op.mult)
+    memset(R("rmin", 0, 512), 0.0); memset(R("rmin", 0, 512, 16), 255.0)
+    act(R("rmax", 0, 512), R("rmin", 0, 512), Fn.Identity, 255.0, -1.0)
+    for nm in ("rmin", "rmax"):
+        for n in (512, 1024):
+            if n < sc[nm][1][1]:
+                act(R(nm, n, 2 * n), R(nm, 0, n), Fn.Copy)
     if cfg["kpe"]:
-        memset(R("ab", 0, W), -37.0)
+        memset(R("ab", 0, 512), -37.0)
         for q in range(4):
             asel(R("selT", 512 * q, 512 * q + 512), R("ab", 0, 512), [[-1, 4], [-16, 8], [0, 16]], Op.is_equal, -4 * q, 1)
     else:
         iota(whole("iot"), [[1, B]], -256, 0)
-    iota(R("pi", 0, 1), [[1, 1]], 0, 1)
     ts(R("p15", 0, 1), R("pi", 0, 1), 15, None, Op.bitwise_and)
-    ts(R("h1", 0, 1), R("pi", 0, 1), 4, 1, Op.logical_shift_right, Op.bitwise_and)
-    c512, c8, c256, h0f, h1f, cpar = [R("cols", i, i + 1) for i in range(6)]
-    ts(c512, R("p15", 0, 1), float(B), None, Op.add)
+    ts(c512, R("p15", 0, 1), 0.0 if cfg["sides"] else float(B), None, Op.add)
+    T0 = 16 if cfg["sides"] else 0
+    if cfg["sides"]:
+        memset(whole("c272"), 272.0)
+        act(whole("nB8"), b1, Fn.Identity, 0.0, -8192.0)
     ts(c8, R("p15", 0, 1), 8.0, None, Op.mult)
     ts(c256, R("p15", 0, 1), 256.0, None, Op.mult)
-    ts(h0f, R("h1", 0, 1), -1.0, 1.0, Op.mult, Op.add)
-    ts(h1f, R("h1", 0, 1), 1.0, None, Op.mult)
-    memset(cpar, 136.5); memset(whole("c35"), -3.5)
-    asel(whole("Ash"), whole("onesF"), [[-1, 160]], Op.is_equal, 16, 1)
-    act(whole("A0"), whole("Ash"), Fn.Identity, 0.0, h0f)
-    act(whole("A1"), whole("Ash"), Fn.Identity, 0.0, h1f)
-    bd = whole("BDh")
-    memset(bd, -0.5)
-    asel(bd, bd, [[16, 8], [0, 16]], Op.is_ge, 15, -1)
-    asel(bd, bd, [[-16, 8], [0, 16]], Op.is_ge, 0, 1)
+    memset(cpar, -136.5 * STEEP); memset(whole("c35"), -3.5)
     def row(nm, p):
         return R(nm, 0, 128, 1, p, p + 1)
     memset(whole("Cmat"), 0.0); memset(whole("CK"), 0.0)
-    memset(row("Cmat", 0), -float(LOW)); memset(row("Cmat", 64), -2.0 ** 25)
-    iota(row("Cmat", 32), [[0, 8], [-512, 16]], 144 * 512, 0)
+    memset(row("Cmat", 0), -float(LOW)); memset(row("Cmat", 64), -2.0 ** 26)
     memset(row("CK", 96), -7.0 / 16)
     for p, step, base in ((0, 512, 37 * 256), (32, 96, 0), (64, 5, 0)):
         iota(row("CK", p), [[0, 8], [step, 16]], base, 0)
+    iota(row("Cmat", 32), [[0, 8], [-512, 16]], 144 * 512, 0)
+    bd = whole("BDh")
+    memset(bd, 0.5 * STEEP)
+    asel(bd, bd, [[16, 8], [0, 16]], Op.is_ge, 15, -1)
+    asel(bd, bd, [[-16, 8], [0, 16]], Op.is_ge, 0, 1)
     ts(whole("rk"), R("rmax", 0, w), 0.0, -2.0 ** 28, Op.is_equal, Op.mult)
-    ts(whole("maskZ"), whole("rr"), c256, 0.5, Op.is_le, Op.mult)
-    iota(whole("jc"), [[128, 16]], 0, 0)
+    ts(R("maskZ", 0, L), whole("rr"), c256, 0.5, Op.is_le, Op.mult)
+    if cfg["pair"]:
+        memset(R("maskZ", L, ZS), 0.0)
+        ts(c528, R("p15", 0, 1), B + 16.0, None, Op.add)
     ts(whole("j8"), whole("jc"), c8, None, Op.add)
-    copy(R("TT", 0, B), whole("TTi"), "TTinit")
 
     def sel(nm, k):
         return R(nm, 15 - k, 143 - k)
 
-    Xw = whole("X")
     dturn = [0]
     for v in range(VISITS):
         last = v == VISITS - 1
         cur[1] = str(v)
-        tab = whole("TTi") if v == 0 else R("TT", 0, B)
+        Xw = whole("X%d" % (v % 2 if cfg["two"] else 0)); Xn = whole("X%d" % ((v + 1) % 2 if cfg["two"] else 0))
+        tab = whole("TTi") if v == 0 else R("TT", T0, T0 + B)
         Tf, Tu, bu, cin, cout = "Tf%d" % v, "Tu%d" % v, "bu%d" % v, "cin%d" % v, "cout%d" % v
         Tout = "Tout" if last else "Ts%d" % v
         def ln(nm, ch):
@@ -260,6 +285,8 @@ def program(cfg):
                 cur[0] = "%d%s" % (ch, "'" * k)
                 yield a, a + pl
             cur[0] = str(ch)
+        def spans(nm, ch):
+            return [(ch * w, ch * w + w)] if "%s:%d" % (nm, ch) in cfg["merge"] else pieces(ch)
         def cuts(nm, ch):
             if "%s:%d" % (nm, ch) not in cfg["cut"]:
                 yield lambda r: r
@@ -267,10 +294,15 @@ def program(cfg):
             for a, b in pieces(ch):
                 lo, hi = a - ch * w, b - ch * w
                 yield lambda r: R(r[0], r[1] + lo * r[3], r[1] + (hi - 1) * r[3] + 1, r[3])
-        def t1(half, full, ch):
-            return [(whole(half), ln(Tf, ch)), (whole(half), ln("Hf", ch)), (whole(full), ln("prod", ch))]
+        def t1(scale, ch):
+            return [(whole(scale), ln(Tf, ch)), (whole(scale), ln("prod", ch))]
         def onV(nm, ch):
             return "%s:%d" % (nm, ch) in cfg["onV"]
+        def above(nm, ch, out, count, thr):
+            if onV(nm, ch):
+                ts(out, count, -STEEP, thr, Op.mult, Op.is_le)
+            else:
+                act(out, count, Fn.Sigmoid, thr, STEEP)
         for ch in turns():
             if v == 0:
                 copy(ln(Tu, ch), ln("Tin", ch))
@@ -278,144 +310,213 @@ def program(cfg):
                 copy(lc(bu, ch), lc("bin", ch))
             copy(ln("Hu", ch), ("ind", tab, lc(bu, ch)))
             ts(ln("Hf", ch), ln("Hu", ch), 0.0, None, Op.add)
-            plus, minus = ("I", "negI") if onV("sgn", ch) else ("nI2", "I2")
-            pe("pD", acc(ps(ch, 1), [(whole(plus), ln("Hf", ch)), (whole(minus), ln(Tf, ch))]))
-            for a, b in pieces(ch):
+            pe("pD", acc(ps(ch, 1), [(I, ln("Hf", ch)), (whole("negI"), ln(Tf, ch))]))
+            for a, b in spans("xg", ch):
                 gather(R("xg", 16 * a, 16 * b), Xw, R(Tu, a, b))
+            for a, b in spans("cmp", ch):
                 tt(R("cmp", 16 * a, 16 * b), ("ind", Xw, R("Hu", a, b)), R("xg", 16 * a, 16 * b), Op.is_ge)
+        if cfg["two"]:
+            add("S", "dup", (Xn, Xw), [Xw, ln("Hu", 0)], [Xn], 128 * W * 2, "d", "dup", sem=("dup%d" % v, 16))
+        if v == 0:
+            copy(R("TT", T0, T0 + B), whole("TTi"), "TTinit")
         nbb = whole("nbb")
         ts(nbb, whole(bu), -1.0, 256.0, Op.mult, Op.add)
         ts(whole("fbk"), whole(bu), 97.0 - LOW - 8192, None, Op.add)
         zd = R("Z", 0, L)
+        wz = ZS if cfg["pair"] else L
+        def spread(r):
+            return R("selT", 128 * r, 128 * r + 128)
+        lumps = [[(R("Z", 0, wz), I, R("maskZ", 0, wz), True, False)]]
         if cfg["kpe"]:
-            mm = [(R("Z", r, L, 16), R("selT", 128 * r, 128 * r + 128), nbb, False, False) for r in range(16)]
+            lumps.append([(R("Z", r, L, 16), spread(r), nbb, False, False) for r in range(16)])
         else:
             act(whole("bb"), ("ind", whole("iot"), whole(bu)), Fn.Copy)
-            mm = [(zd, whole("I37"), whole("bb"), False, False)]
-        pe("pZd", [(zd, I, whole("maskZ"), True, False)] + mm +
-           [(R("Z", r, L, 16), whole("I37"), nbb, False, r == 15) for r in range(16)])
-        ts(whole("E"), zd, 0.0, None, Op.is_equal)
-        pe("poff", acc(R("Z", 256, 272), [(whole("negI"), nbb)] + [(sel("B8", r), R("E", r, L, 16)) for r in range(16)]))
-        ts(R("offu", 0, 32, 2), R("Z", 256, 272), 256.0, c512, Op.add, Op.min)
+            lumps[0].append((zd, whole("I37"), whole("bb"), False, False))
+        if cfg["pair"]:
+            if cfg["kpe"]:
+                lumps.append([(R("Z", L + r, ZS, 16), spread(r), R("nbb", 1, 16, 2), False, False) for r in range(16)])
+            else:
+                lumps[0] += [(R("Z", L + 16 * c, L + 16 * c + 16), whole("I37"), R("bb", 32 * c + 16, 32 * c + 32), False, False)
+                             for c in range(8)]
+            lumps.append([(R("Z", L + r, ZS, 16), whole("I37"), R("nbb", 0, 16, 2), False, False) for r in range(16)])
+        lumps.append([(R("Z", r, L, 16), whole("I37"), nbb, False, r == 15) for r in range(16)])
+        if cfg["kpe"]:
+            lumps[0:2] = [lumps[0] + lumps[1]]
+        for mm in lumps:
+            pe("pZd", mm, grp=("z", v))
+        off = R("Z", ZS, ZS + 16)
+        ts(R("E", 0, wz), R("Z", 0, wz), 0.0, None, Op.is_equal)
+        mm = acc(off, [(whole("negI"), nbb)] + [(sel("B8", r), R("E", r, L, 16)) for r in range(16)])
+        if cfg["sides"]:
+            even, odd = R("Z", ZS, ZS + 16, 2), R("Z", ZS + 1, ZS + 16, 2)
+            pe("poff", mm[:1] + [(off, I, whole("c272"), False, False)] +
+               [(odd, sel("nB8", r), R("E", L + r, ZS, 16), False, False) for r in range(16)], grp=("o", v))
+            pe("poff", [(odd, sel("nB8", r), R("E", 16 + r, L, 32), False, False) for r in range(16)], grp=("o", v))
+            pe("poff", [(even, sel("B8", r), R("E", r, L, 32), False, r == 15) for r in range(16)], grp=("o", v))
+            ts(R("offu", 0, 16), off, c512, c528, Op.max, Op.min)
+        elif cfg["pair"]:
+            odd = [(R("Z", ZS + 1, ZS + 16, 2), sel("B8", r), R("E", L + r, ZS, 16), False, False) for r in range(16)]
+            pe("poff", mm[:1] + odd, grp=("o", v))
+            pe("poff", mm[1:], grp=("o", v))
+        else:
+            pe("poff", mm)
+        if cfg["sides"]:
+            pass
+        elif cfg["pair"]:
+            ts(R("offu", 0, 16, 2), R("Z", ZS, ZS + 16, 2), 256.0, c512, Op.add, Op.min)
+            ts(R("offu", 1, 16, 2), R("Z", ZS + 1, ZS + 16, 2), 256.0, c528, Op.add, Op.min)
+        else:
+            ts(R("offu", 0, 32, 2), off, 256.0, c512, Op.add, Op.min)
         for ch in turns():
             tq, kq = ps(ch, 2), ps(ch, 3)
             for a, b in pieces(ch):
                 pe("pvote", acc(R("KB", L + a, L + b), [
                     (sel("B1", k), R("cmp", 16 * a + k, 16 * b, 16)) for k in range(16)]))
-            thr = 8.5 if v == 0 else R("vb", v, v + 1)
+            thr = -STEEP * 8.5 if v == 0 else R("vb", v, v + 1)
             for u in cuts("T1", ch):
-                votes = u(R("KB", L + ch * w, L + ch * w + w))
-                if onV("sgn", ch):
-                    ts(u(ln("sgn", ch)), votes, thr, 0.5, Op.is_ge, Op.subtract)
-                else:
-                    act(u(ln("sgn", ch)), votes, Fn.Sign, thr, -1.0)
+                above("sgn", ch, u(ln("sgn", ch)), u(R("KB", L + ch * w, L + ch * w + w)), thr)
                 tt(u(ln("prod", ch)), u(ps(ch, 1)), u(ln("sgn", ch)), Op.mult)
-                pe("pT1", acc(u(tq), [(l, u(r)) for l, r in t1("I8", "I4", ch)]))
+                pe("pT1", acc(u(tq), [(l, u(r)) for l, r in t1("I4", ch)]))
                 ts(u(ln("T1u", ch)), u(tq), 4.0, None, Op.mult)
-            mm = acc(kq, [(whole("CK"), R("ones", 0, w))] + t1("I16th", "I8", ch))
+            mm = acc(kq, [(whole("CK"), R("ones", 0, w))] + t1("I8", ch)) + acc(ps(ch, 0), t1("I", ch))
             if cfg["kpe"]:
                 mm[1:1] = [(R(kq[0], kq[1] + r, kq[2], 16), R("selT", 128 * r, 128 * r + 128), lc("nbb", ch), False, False)
                            for r in range(16)]
             else:
                 mm[1:1] = [(kq, whole("I37"), ln("bb", ch), False, False)]
             pe("pK", mm)
-            for a, b in pieces(ch):
-                zz = R("z", 16 * a, 16 * b)
-                gather(zz, Xw, R("T1u", a, b))
-                scan(R("smin", 16 * a, 16 * b), R("rmin", 0, 16 * (b - a)), zz, Op.max, Op.min)
-                scan(R("smax", 16 * a, 16 * b), R("rmax", 0, 16 * (b - a)), zz, Op.min, Op.max)
+            for a, b in spans("z", ch):
+                gather(R("z", 16 * a, 16 * b), Xw, R("T1u", a, b))
+            for a, b in spans("smin", ch):
+                scan(R("smin", 16 * a, 16 * b), R("rmin", 0, 16 * (b - a)), R("z", 16 * a, 16 * b), Op.max, Op.min)
+            for a, b in spans("smax", ch):
+                scan(R("smax", 16 * a, 16 * b), R("rmax", 0, 16 * (b - a)), R("z", 16 * a, 16 * b), Op.min, Op.max)
             m = strided("smin", ch, 15)
             for u in cuts("n", ch):
                 tt(u(ln("P", ch)), u(tq), u(m), Op.mult)
                 tt(u(ln("ni", ch)), u(kq), u(ln("P", ch)), Op.add)
                 ts(u(ln("nn", ch)), u(ln("ni", ch)), W - 1, None, Op.bitwise_and)
                 copy(u(ln("nu", ch)), u(ln("nn", ch)))
-            for a, b in pieces(ch):
+            for a, b in spans("e", ch):
                 gather(R("e", 16 * a, 16 * b), Xw, R("nu", a, b))
-            if onV("free", ch):
+            if "free" in cfg["merge"]:
+                pass
+            elif onV("free", ch):
                 pe("pm", acc(tq, [(I, m)]))
                 tt(ln("free", ch), tq, ln(cin, ch), Op.is_gt)
             else:
                 pe("pm", acc(tq, [(I, m), (whole("negI"), ln(cin, ch))]))
-                act(ln("free", ch), tq, Fn.Sign, -0.5)
-            ts(ln("nf", ch), ln("nu", ch), 0.0, None, Op.add)
-            ts(ln("q2", ch), ln("nu", ch), 1.0 / B, 128.5 + 0.5 / B, Op.mult, Op.add)
-            full = onV("rdy", ch)
-            pe("pD2", acc(ps(ch, 1), t1(*(("nI2", "negI") if full else ("nI4", "nI2")), ch) +
-                          [(whole("I" if full else "I2"), ln("nf", ch))]) +
-               acc(ps(ch, 0), t1("I4", "I2", ch) + [(whole("I2"), ln("nf", ch))]))
+                act(ln("free", ch), tq, Fn.Sigmoid, -STEEP * 0.5, STEEP)
+            if "nf" not in cfg["merge"]:
+                ts(ln("nf", ch), ln("nu", ch), 0.0, None, Op.add)
+                pe("pD2", acc(ps(ch, 1), t1("negI", ch) + [(I, ln("nf", ch))]))
+            if "q2" not in cfg["merge"]:
+                ts(ln("q2", ch), ln("nu", ch), 1.0 / B, 128.5 + 0.5 / B, Op.mult, Op.add)
+        if "free" in cfg["merge"]:
+            pe("pm", acc(zd, [(I, R("smin", 15, 16 * L, 16)), (whole("negI"), whole(cin))]))
+            act(whole("free"), zd, Fn.Sign, -0.5)
+        if "nf" in cfg["merge"]:
+            ts(whole("nf"), whole("nu"), 0.0, None, Op.add)
+            for ch in turns():
+                pe("pD2", acc(ps(ch, 1), t1("negI", ch) + [(I, ln("nf", ch))]))
+        if "q2" in cfg["merge"]:
+            ts(whole("q2"), whole("nu"), 1.0 / B, 128.5 + 0.5 / B, Op.mult, Op.add)
         asel(whole(cout), R("smin", 15, 16 * L, 16), [[0, L]], Op.is_ge, 0, 0)
         if not last:
             send(whole(cout), whole("cin%d" % (v + 1)), "arrc%d" % v, 128 * L * 2)
         else:
             store("S", "ylast", whole(cout), 0, 128 * L * 2)
         u = [(sel("B1", r), R("smax", 15 + 16 * r, 16 * L, 256)) for r in range(16)]
-        uj = R("Z", 272, 288)
+        uj = R("Z", ZS + 16, ZS + 32)
         pe("pu", acc(uj, u + [(I, whole("c35"))]))
         ts(whole("q8"), uj, 8 * MAGIC, -8 * MAGIC, Op.add, Op.add)
-        uj = R("Z", 288, 304)
-        pe("pj", acc(uj, u + [(I, whole("j8")), (whole("negI"), whole("q8"))]))
-        copy(whole("ju"), uj)
-        gather(whole("xj"), Xw, whole("ju"))
-        pe("px", acc(zd, [(whole("I2"), R("smax", 15, 16 * L, 16)), (whole("nI4"), ones), (whole("I2"), whole("xj"))]))
-        ts(whole("xb"), zd, MAGIC, -MAGIC, Op.add, Op.add)
-        copy(("ind", Xw, whole("ju")), whole("xb"), "Xsc")
+        if cfg["u3"]:
+            tt(whole("u7"), uj, whole("q8"), Op.subtract)
+            pe("pj", acc(uj, [(I, whole("j8")), (I, whole("u7"))]))
+            ts(whole("ju"), uj, 3.5, None, Op.add)
+        else:
+            uj = R("Z", ZS + 32, ZS + 48)
+            pe("pj", acc(uj, u + [(I, whole("j8")), (whole("negI"), whole("q8"))]))
+            copy(whole("ju"), uj)
+        if cfg["xjV"]:
+            tt(whole("xs"), ("ind", Xw, whole("ju")), R("smax", 15, 16 * L, 16), Op.add, "xj")
+            ts(whole("xu"), whole("xs"), 0.5, -0.25, Op.mult, Op.add, "xb")
+            copy(("ind", Xn, whole("ju")), whole("xu"), "Xsc")
+        else:
+            gather(whole("xj"), Xw, whole("ju"))
+            pe("px", acc(zd, [(whole("I2"), R("smax", 15, 16 * L, 16)), (whole("nI4"), ones), (whole("I2"), whole("xj"))]))
+            ts(whole("xb"), zd, MAGIC, -MAGIC, Op.add, Op.add)
+            copy(("ind", Xn, whole("ju")), whole("xb"), "Xsc")
         if last:
-            store("S", "yclk", Xw, 1, 128 * W * 2)
+            store("S", "yclk", Xn, 1, 128 * W * 2)
         for ch in turns():
             def blk(nm, q):
                 return R(nm, 16 * ch * w + 512 * q, 16 * ch * w + 512 * (q + 1))
+            ns = 4 if ch in cfg["wide"] else 2; nj = 16 // ns; wl = 512 // nj
+            def top(q):
+                return w - wl * (1 + q // ns)
             def of(nm, q, j):
-                return R(nm, 16 * ch * w + 512 * q + j, 16 * ch * w + 512 * (q + 1), 8)
+                return R(nm, 16 * ch * w + 512 * q + j, 16 * ch * w + 512 * (q + 1), nj)
             def eq(q):
-                o = 16 * ch * w + 1024 * (1 - q // 2)
-                return R("e", o + q % 2, o + 1024, 2)
+                o = 16 * (ch * w + top(q))
+                return R("e", o + q % ns, o + 16 * wl, ns)
             def ends(nm, q):
-                o = 16 * ch * w + 1024 * (1 - q // 2)
-                return R(nm, o + 15, o + 1024, 16)
+                o = 16 * (ch * w + top(q))
+                return R(nm, o + 15, o + 16 * wl, 16)
             def part(r, q):
-                return R(r[0], r[1] + 64 * (1 - q // 2), r[1] + 64 * (1 - q // 2) + 64)
+                return R(r[0], r[1] + top(q), r[1] + top(q) + wl)
+            def diff(name, bank, q, sub, o=0):
+                pe(name, [(R(bank, o, o + 512), I, eq(q), True, False)] +
+                   [(R(bank, o + j, o + 512, nj), whole("negI"), ends(sub, q), False, j == nj - 1) for j in range(nj)])
+                return R(bank, o, o + 512)
             c2 = ps(ch, 3)
+            filled = set()
             for q in range(4):
                 cur[0] = "%d%s" % (ch, "abcd"[q])
-                mb = "M%d" % (q // 2)
-                if q % 2 == 0:
-                    pe("pM", [(R(mb, j, 512, 8), I, ends("smin", q), True, True) for j in range(8)])
-                tt(blk("cmp2", q), eq(q), R(mb, 0, 512), Op.is_ge)
-                mm = [(c2, whole("I16" if onV("free", ch) else "I8x"), ln("free", ch), True, False)] if q == 0 else []
-                pe("pc2", mm + [(part(c2, q), sel("B1", 2 * j + q % 2), of("cmp2", q, j), False, q == 3 and j == 7)
-                                for j in range(8)], grp=("c", v, ch))
+                mb = cfg["mb"][2 * ch + q // ns]
+                mm = [(c2, whole("I16"), ln("free", ch), True, False)] if q == 0 else []
+                bank = cfg["onA"].get("cmp2:" + cur[0])
+                if bank:
+                    act(blk("cmp2", q), diff("ps", bank, q, "smin"), Fn.Sigmoid, STEEP * 0.5, STEEP)
+                else:
+                    if q // ns not in filled:
+                        pe("pM", [(R(mb, j, 512, nj), I, ends("smin", q), True, True) for j in range(nj)])
+                        filled.add(q // ns)
+                    tt(blk("cmp2", q), eq(q), R(mb, 0, 512), Op.is_ge)
+                pe("pc2", mm + [(part(c2, q), sel("B1", ns * j + q % ns), of("cmp2", q, j), False, q == 3 and j == nj - 1)
+                                for j in range(nj)], grp=("c", v, ch))
             cur[0] = str(ch)
-            thr = 27.5 if onV("free", ch) else 19.5
-            if onV("rdy", ch):
-                ts(ln("rdy", ch), c2, thr, 0.5, Op.is_ge, Op.subtract)
-            else:
-                act(ln("rdy", ch), c2, Fn.Sign, -thr)
+            above("rdy", ch, ln("rdy", ch), c2, -STEEP * (19.5 if "free" in cfg["merge"] else 27.5))
             tt(ln("prod2", ch), ps(ch, 1), ln("rdy", ch), Op.mult)
             tt(ln(Tout, ch), ps(ch, 0), ln("prod2", ch), Op.add, "T2")
             if not last:
                 ts(ln("Us%d" % v, ch), ln(Tout, ch), 0.0, None, Op.add, name="T2u")
                 send(ln("Us%d" % v, ch), ln("Tu%d" % (v + 1), ch), "arrU%d_%d" % (v, ch), 128 * w * 2)
                 send(ln(Tout, ch), ln("Tf%d" % (v + 1), ch), "arrT%d_%d" % (v, ch), 128 * w * 2)
-            for cc in range(ch * nc + nc - 1, ch * nc - 1, -1):
-                copy(("ind", whole("TT"), R("offu", 2 * cc, 2 * cc + 1)), R(Tout, 16 * cc, 16 * cc + 16))
+            if cfg["pair"]:
+                for cc in range(ch * nc + nc - 2, ch * nc - 1, -2):
+                    copy(("ind", whole("TT"), R("offu", cc, cc + 2)), R(Tout, 16 * cc, 16 * cc + 32))
+            else:
+                for cc in range(ch * nc + nc - 1, ch * nc - 1, -1):
+                    copy(("ind", whole("TT"), R("offu", 2 * cc, 2 * cc + 1)), R(Tout, 16 * cc, 16 * cc + 16))
             key = ln("KB", ch)
             for q in range(4):
                 cur[0] = "%d%s" % (ch, "abcd"[q])
-                d = R("D%d" % (dturn[0] % 2), 0, 512); dturn[0] += 1
-                pe("pd", [(d, I, eq(q), True, False)] +
-                   [(R(d[0], j, 512, 8), whole("negI"), ends("smax", q), False, j == 7) for j in range(8)])
-                act(blk("ab", q), d, Fn.Abs)
+                if not cfg["dd"]:
+                    act(blk("ab", q), diff("pd", "D%d" % (q % 2), q, "smax"), Fn.Abs)
+                elif q % 2 == 0:
+                    diff("pd", "DD", q, "smax"); diff("pd", "DD", q + 1, "smax", 512)
+                    act(R("ab", blk("ab", q)[1], blk("ab", q + 1)[2]), whole("DD"), Fn.Abs)
                 mm = [(key, whole("Cmat"), R("ones", 0, w), True, False),
                       (key, whole("nI512"), ln("q2", ch), False, False)] if q == 0 else []
-                pe("pk", mm + [(part(key, q), sel("B8", 2 * j + q % 2), of("ab", q, j), False, False) for j in range(8)],
+                pe("pk", mm + [(part(key, q), sel("B8", ns * j + q % ns), of("ab", q, j), False, False) for j in range(nj)],
                    grp=("k", v, ch))
             cur[0] = str(ch)
-            pe("pkey", [(key, whole("Ipen2" if onV("rdy", ch) else "Ipen"), ln("rdy", ch), False, False),
+            pe("pkey", [(key, whole("Ipen"), ln("rdy", ch), False, False),
                         (key, I, ln("nf", ch), False, True)], grp=("k", v, ch))
             add("V", "tr", (ln("kt", ch), key), [key], [ln("kt", ch)], w, "c")
             scan(ln("ks", ch), whole("rk"), ln("kt", ch), Op.add, Op.max)
-            sw = 304 + ch * nc
+            sw = ZS + 48 + ch * nc
             mm = []
             for h in (0, 1):
                 o = R("Z", sw + h, sw + nc, 2)
@@ -432,14 +533,14 @@ def program(cfg):
                 send(lc("bs%d" % v, ch), lc("bu%d" % (v + 1), ch), "arrb%d_%d" % (v, ch), 128 * nc * 2)
         if last:
             store("S", "ytrav", whole("Tout"), 2, 128 * L * 4)
-            store("S", "yttab", R("TT", 0, B), 3, 128 * B * 4)
+            store("S", "yttab", R("TT", T0, T0 + B), 3, 128 * B * 4)
             store("A", "yslot", whole("bout"), 4, 128 * 64)
         else:
-            act(whole("has"), R("Z", 304, 320), Fn.Sign, LOW + 8192.0, acc=R("scol", 0, 1))
-            y = R("Z", 320, 321)
+            act(whole("has"), R("Z", ZS + 48, ZS + 64), Fn.Sign, LOW + 8192.0, acc=R("scol", 0, 1))
+            y = R("Z", ZS + 64, ZS + 65)
             pe("ppar", acc(y, [(bd, R("scol", 0, 1)), (R("Ash", 16, 144), cpar)]))
-            ts(R("half", 0, 1), y, 0.5, -4.5, Op.mult, Op.add)
-            ts(R("vb", v + 1, v + 2), R("half", 0, 1), -2.0, y, Op.mult, Op.add)
+            ts(R("half", 0, 1), y, -0.5 / STEEP, -4.5, Op.mult, Op.add)
+            ts(R("vb", v + 1, v + 2), R("half", 0, 1), 2 * STEEP, y, Op.mult, Op.add)
     seen = {}
     for i, o in enumerate(ops):
         dep = set()
@@ -447,10 +548,15 @@ def program(cfg):
             for lo, hi, j, wr in seen.get(a[0], []):
                 if wr and lo < a[2] and a[1] < hi:
                     dep.add(j)
+        hard = set(dep)
         for a in o["wr"]:
             for lo, hi, j, wr in seen.get(a[0], []):
                 if lo < a[2] and a[1] < hi:
                     dep.add(j)
+                    if ("waw" if wr else "war") not in cfg["free"]:
+                        hard.add(j)
+        o["soft"] = set(j for j in dep - hard if ops[j]["eng"] == o["eng"] and o["eng"] in "VA" and "sem" not in ops[j]
+                        and "sem" not in o)
         for a in o["wr"]:
             if a[3] == 1 and a[4] == 0 and a[5] == 128:
                 seen[a[0]] = [t for t in seen.get(a[0], []) if not (a[1] <= t[0] and t[1] <= a[2])]
@@ -473,7 +579,7 @@ def cost(o, eng, m):
     if c == "r":
         return 500.0, m["rem"] + n * m["rb"]
     if c == "p":
-        t = n * m["pe"] * m["f"]
+        t = n * m["pe"] * m["f"] + len(o["args"]) * m["pov"]
         return t, t
     if c == "g":
         t = (50.0 if eng == "V" else 65.0) + n * m["g"] * cyc
@@ -481,7 +587,7 @@ def cost(o, eng, m):
         t = 50.0 + n * m["s"] * cyc
     else:
         k = {"h": 0.5, "c": 1.0, "th": m["tt2"], "tc": 2.0}[c]
-        t = m["ov"] + max(64.0, n * k) * cyc
+        t = m["ova" if eng == "A" else "ov"] + max(64.0, n * k) * cyc
     return t, t
 
 
@@ -489,6 +595,22 @@ def gap(a, b, m):
     if a == b:
         return 0.0 if a == "P" else m["same"]
     return m["lat"]
+
+
+def chained(words, named, mine):
+    chain = []
+    for v in range(-1, VISITS + 1):
+        here = []
+        for t in words:
+            t, _, only = t.partition("@")
+            u = str(v + t.count("+") - t.count("-"))
+            if u in only or (not only and not any(x.startswith(t + "@") and u in x.partition("@")[2] for x in words)):
+                here.append((t.rstrip("+-"), u))
+        for k, t in enumerate(here):
+            have = [i for i in named.get(t, []) if mine[i]]
+            first = here[:k].count(t)
+            chain += have[first:first + 1] if t in here[k + 1:] else have[first:]
+    return chain
 
 
 def schedule(ops, cfg, m):
@@ -499,14 +621,12 @@ def schedule(ops, cfg, m):
     named = {}
     for i, o in enumerate(ops):
         named.setdefault((o["tag"], o["vis"]), []).append(i)
-    for line in cfg["order"]:
-        chain = []
-        for v in range(-1, VISITS + 1):
-            words = line.split()
-            for k, t in enumerate(words):
-                have = named.get((t.rstrip("+-"), str(v + t.count("+") - t.count("-"))), [])
-                first = words[:k].count(t)
-                chain += have[first:first + 1] if t in words[k + 1:] else have[first:]
+    for e, line in zip("VAP", cfg["order"]):
+        chain = chained(line.split(), named, [o["eng"] == e for o in ops])
+        for j, i in zip(chain, chain[1:]):
+            after[i].add(j)
+    for e in "AGS":
+        chain = [i for i, o in enumerate(ops) if o["eng"] == e and o["vis"] == "c"]
         for j, i in zip(chain, chain[1:]):
             after[i].add(j)
     for i in range(n):
@@ -587,7 +707,7 @@ def plan(cfg):
     for i in seq:
         e = on[i]; need = {}
         for j in ops[i]["dep"] + extra[i]:
-            if on[j] == e == "P":
+            if on[j] == e == "P" or j in ops[i]["soft"]:
                 continue
             key = ops[j]["sem"][0] if "sem" in ops[j] else on[j]
             if known[e].get(key, 0) < pos[j] and (key not in need or pos[need[key]] < pos[j]):
@@ -639,8 +759,8 @@ def rank_program(g, core, T, topo):
             g.remote_dma(view(T, a[1]), view(T, a[0]), T.sem[a[2]], T.sem.sent, pid, rid, mask)
             sent += n_out; own.append((a[2], n_in))
             continue
-        if k in ("load", "store"):
-            ins = q.dma_start(view(T, a[0]), T[a[1]][:]) if k == "load" else q.dma_start(T[a[0]][:], view(T, a[1]))
+        if k in ("load", "store", "dup"):
+            ins = q.dma_start(*[view(T, y) if isinstance(y, tuple) else T[y][:] for y in a])
             ins.then_inc(T.sem[o["sem"][0]], 16); own.append(o["sem"])
             continue
         x = [view(T, y) for y in a] if k != "mm" else a

from concourse.mybir import AluOpType as Op, ActivationFunctionType as Fn

NR, VISITS, STEP = 8, 4, 5
W, B, L = 2048, 512, 256
H = L // 2
ORDER = ["""ki:0- bi:0- Hu:1 bs:0- cmp:1 cmp:1' half:a- TTinit:a Hf:1 vb:a- Hu:0 sgn:1 prod:1 fbk:a Hf:0 T1u:1 cmp:0 cmp:0'
sgn:0 nbb:a prod:0 smin:1 T1u:0 smin:1' sgn:0' P:1 prod:0' ni:1 nn:1 T1u:0' smax:1 E:a nu:1 smax:0 smax:0' nf:1 smin:0'
smin:0 cmp2:1b cmp2:1a P:0 free:1 ni:0 q8:a nn:0 u7:a nu:0 cmp2:1c cmp2:1d q2:a offu:a nf:0 ju:a e:0x xj:a rdy:1 cmp2:0b
prod2:1 cmp2:0a kt:1 T2:1 ks:1 TT:1 free:0 T2u:1 cmp2:0c xb:a ki:1 TT:1 cmp2:0d bi:1 Xsc:a bs:1 rdy:0 TT:1 prod2:0 TT:1
T2:0 kt:0 TT:0 ks:0 TT:0 T2u:0 TT:0 TT:0""",
"""xg:1 xg:1' has:a- xg:0 bb:a xg:0' z:1 z:1' z:0 z:0' e:1 e:1' ab:1a ab:1b e:0 ab:1c ab:1d e:0' ab:0b ab:0a ab:0d ab:0c""",
"""ppar:a- pvote:1 pvote:1' pD:1 pT1:1 pvote:0 pD:0 pK:1 pZd:a pT1:0 pvote:0' pZd:a pT1:0' pZd:a pM:1c pM:1a pK:0 pm:1
poff:a poff:a poff:a pu:a pD2:1 pd:1b pd:1a pM:0a pc2:1a pc2:1b pm:0 pd:1c pj:a pd:1d pc2:1c pk:1a pc2:1d pk:1b pD2:0
pk:1c pd:0a pk:1d pkey:1 pM:0c pd:0b psw:1 pc2:0a pc2:0b pd:0d pd:0c pk:0a pc2:0c pc2:0d pk:0b pk:0c pk:0d pkey:0 psw:0"""]
CFG = {"pw": 1024, "slack": 100.0, "kpe": 0, "onV": ["free:1", "free:0", "e:0x", "rdy:0", "sgn:1", "rdy:1", "sgn:0"],
       "cut": ["T1:0"], "up": {}, "free": [], "share": {"e:0": 16}, "xjV": 1, "dd": 0, "sides": 1,
       "merge": ["smax:1", "q2"], "pair": 1, "two": 0, "onA": {}, "u3": 1, "wide": [], "mb": ["M0", "M1", "M0", "M1"],
       "order": ORDER}
LOW = 2040 * 8192
ZS = 384
BANKS = ("S0", "S1", "M0", "M1", "D0", "D1", "KB", "Z", "DD")
MAGIC = 12582912.0
REF = {"f": 1.2, "g": 1.56, "s": 3.8, "ov": 50.0, "ova": 150.0, "pov": 0.0, "pe": 0.42, "lat": 150.0, "same": 100.0, "rem": 2200.0, "rb": 0.02,
       "dma": 1800.0, "db": 0.006, "tt2": 1.0}
SCALED = (("negI", -1.0), ("I16", 16.0), ("I37", 37.0), ("Ipen", 2.0 ** 26), ("I2", 0.5), ("I4", 0.25), ("nI4", -0.25),
          ("I8", 0.125), ("nI512", -512.0))
STEEP = 256.0


def scratch(cfg):
    s = {}
    def sb(names, n, dtp):
        for nm in names.split():
            s[nm] = ("sbuf", [128, n], dtp)
    sb("X0 X1", W, "bfloat16"); sb("TTi", B, "int32"); sb("TT", B + 32, "float32")
    sb("Tin ni nn xn", L, "int32"); sb("bin ki bi jc", 16, "int32"); sb("E maskZ", ZS, "bfloat16")
    sb("cin0 cin1 cin2 cin3 cout0 cout1 cout2 cout3 sgn rdy free q2 xj xb bb rr ones", L, "bfloat16")
    sb("Tf0 Tf1 Tf2 Tf3 Ts0 Ts1 Ts2 Hf prod nf prod2", L, "float16"); sb("q8 j8", 16, "float16")
    sb("bu0 bu1 bu2 bu3 bs0 bs1 bs2 ju", 16, "uint16"); sb("offu", 32, "uint16")
    sb("Tu0 Tu1 Tu2 Tu3 Us0 Us1 Us2 Hu T1u nu", L, "uint16")
    sb("Tout P kt ks xr", L, "float32"); sb("bout fbk cols", 16, "float32")
    sb("xg cmp z smin smax e cmp2 ab", 16 * L, "bfloat16")
    sb("nB8", 144, "bfloat16"); sb("xs", L, "float16"); sb("xu", L, "uint16")
    sb("nbb has c35 u7 c272", 16, "bfloat16"); sb("scol vb", 8, "float32"); sb("half pi p15 h1", 8, "int32")
    sb("I Cmat CK " + " ".join(nm for nm, _ in SCALED), 128, "bfloat16"); sb("B1 B8", 144, "bfloat16")
    sb("onesF Ash A0 A1", 160, "float32"); sb("BDh rk", 128, "float32");
    for nm in ("min", "max"):
        sb("r" + nm, 2048 if any(t[:4] == "s" + nm for t in cfg["merge"]) else 1024, "bfloat16")
    if cfg["kpe"]:
        sb("selT", W, "bfloat16")
    else:
        sb("iot", B, "bfloat16")
    for b in BANKS:
        if b[0] != "D" or (b == "DD") == bool(cfg["dd"]):
            s[b] = ("psum", [128, 1024 if b == "DD" else 512], "float32")
    return s


def semaphores(cfg):
    n = ["qV", "qA", "qP", "qG", "sent"] + ["ld%d" % i for i in range(5)] + ["st%d" % i for i in range(5)]
    n += ["dup%d" % v for v in range(VISITS) if cfg["two"]]
    for v in range(VISITS - 1):
        n += ["arr%s%d_%d" % (x, v, ch) for ch in range(2) for x in "TUb"] + ["arrc%d" % v]
    return n


SCRATCH = scratch(CFG)
SEMAPHORES = semaphores(CFG)


def R(name, lo, hi, step=1, p0=0, p1=128):
    return (name, lo, hi, step, p0, p1)


def cnt(a):
    return (a[2] - a[1] + a[3] - 1) // a[3]


def view(T, a):
    if not isinstance(a, tuple):
        return a
    if a[0] == "ind":
        return view(T, a[1]).indirect(view(T, a[2]))
    if a[3] == 1:
        return T[a[0]][a[4]:a[5], a[1]:a[2]]
    return T[a[0]][a[4]:a[5], a[1]:a[2]:a[3]]


def parts(a):
    if not isinstance(a, tuple):
        return []
    return [a[1], a[2]] if a[0] == "ind" else [a]


def program(cfg):
    sc = scratch(cfg)
    pw = cfg["pw"]
    w = H; nc = w // 16; pl = pw // 16
    ops = []
    cur = ["a", "c"]

    def turns():
        for ch in (1, 0):
            cur[0] = str(ch)
            yield ch
        cur[0] = "a"

    def two(a):
        return sc[a[0]][2] in ("bfloat16", "uint16", "float16") and sc[a[0]][0] == "sbuf"

    def add(eng, kind, args, reads, writes, n, cls, name=None, **kw):
        rd = []
        for a in reads:
            rd += parts(a)
        wr = []
        for a in writes:
            if a[0] == "ind":
                wr.append(a[1]); rd.append(a[2])
            else:
                wr.append(a)
        o = {"eng": eng, "kind": kind, "args": args, "rd": rd, "wr": wr, "n": n, "cls": cls}
        nm = (wr[0] if wr else rd[0])[0]
        o["tag"] = "%s:%s" % (name or (nm[:-1] if nm[:-1] in ("Tf", "Tu", "bu", "bs", "cout", "cin") else nm), cur[0])
        o["vis"] = cur[1]
        o.update(kw); ops.append(o)
        return o

    def cls_of(out, ins):
        if out[0] == "ind":
            return "s"
        if ins[0][0] == "ind":
            return "g"
        return "h" if two(out) and all(two(a) for a in ins) else "c"

    def copy(out, in_, name=None):
        add("V", "copy", (out, in_), [in_], [out], cnt(in_ if out[0] == "ind" else out), cls_of(out, [in_]), name)

    def gather(out, win, off):
        a = ("ind", win, off)
        tag = "%s:%s" % (out[0], cur[0])
        k = cfg["share"].get(tag)
        if k:
            cur[0] += "x"
            gather(R(out[0], out[2] - 16 * k, out[2]), win, R(off[0], off[2] - k, off[2]))
            cur[0] = cur[0][:-1]
            out = R(out[0], out[1], out[2] - 16 * k); a = ("ind", win, R(off[0], off[1], off[2] - k))
        eng = "V" if tag in cfg["onV"] or tag + "@" + cur[1] in cfg["onV"] else "A"
        add(eng, "gather", (out, a), [a], [out], cnt(out), "g")

    def tt(out, a, b, op, name=None):
        c = cls_of(out, [a, b])
        if c in "hc" and sc[a[0]][0] == "sbuf" and sc[b[0]][0] == "sbuf":
            c = "t" + c
        add("V", "tt", (out, a, b, op), [a, b], [out], cnt(out), c, name)

    def ts(out, a, s1, s2, op0, op1=None, name=None):
        add("V", "ts", (out, a, s1, s2, op0, op1), [a, s1, s2], [out], cnt(out), cls_of(out, [a]), name)

    def scan(out, d0, d1, op0, op1):
        add("V", "scan", (out, d0, d1, op0, op1), [d0, d1], [out], cnt(out), cls_of(out, [d0, d1]))

    def act(out, in_, fn, bias=0.0, scale=1.0, acc=None):
        add("A", "act", (out, in_, fn, bias, scale, acc), [in_, bias, scale], [out] + ([acc] if acc else []), cnt(out),
            "g" if in_[0] == "ind" else "c")

    def pe(name, mms, grp=None):
        cyc = 0
        rd, wr = [], []
        for o, l, r, st, sp in mms:
            cyc += max(64, cnt(r)) * (4 if sc[r[0]][2] == "float32" else 1)
            rd += [l, r]; wr.append(o)
        return add("P", "mm", mms, rd, wr, cyc, "p", name, grp=grp, first=mms[0][3], last=mms[-1][4])

    def acc(out, terms):
        return [(out, l, r, i == 0, i == len(terms) - 1) for i, (l, r) in enumerate(terms)]

    def memset(out, val):
        add("V", "memset", (out, val), [], [out], cnt(out), "h" if two(out) else "c")

    def iota(out, pat, base, cm):
        add("G", "iota", (out, pat, base, cm, sc[out[0]][2] != "int32"), [], [out], 2 * cnt(out) + 150, "c")

    def asel(out, in_, pat, cmp, base, cm):
        add("G", "asel", (out, in_, pat, cmp, base, cm), [in_], [out], 2 * cnt(out) + 200, "c")

    def load(q, buf, src, k, nbytes):
        add(q, "load", (buf, src), [], [buf], nbytes, "d", sem=("ld%d" % k, 16))

    def store(q, dst, buf, k, nbytes):
        add(q, "store", (dst, buf), [buf], [], nbytes, "d", "st" + dst, sem=("st%d" % k, 16))

    def send(src, dst, sem, nbytes):
        add("G", "send", (src, dst, sem), [src], [dst], nbytes, "r", "send" + sem[3], sem=(sem, None))

    def whole(nm):
        return R(nm, 0, sc[nm][1][1])

    load("S", whole("X0"), "clk", 0, 128 * W * 2 + 128 * L * 4)
    load("A", whole("Tin"), "trav", 1, 128 * L * 8)
    load("A", whole("bin"), "slot", 2, 128 * L * 8)
    load("S", whole("TTi"), "ttab", 3, 128 * W * 2 + 128 * (L + B) * 4)
    load("S", whole("cin0"), "last", 4, 128 * W * 2 + 128 * (L + B) * 4 + 128 * L * 2)
    I, ones = whole("I"), whole("ones")
    memset(ones, 1.0)
    iota(R("pi", 0, 1), [[1, 1]], 0, 1)
    c512, c8, c256, h0f, h1f, cpar, c528 = [R("cols", i, i + 1) for i in range(7)]
    ts(R("h1", 0, 1), R("pi", 0, 1), 4, 1, Op.logical_shift_right, Op.bitwise_and)
    ts(h1f, R("h1", 0, 1), 1.0, None, Op.mult)
    ts(h0f, R("h1", 0, 1), -1.0, 1.0, Op.mult, Op.add)
    iota(whole("jc"), [[128, 16]], 0, 0)
    asel(I, R("ones", 0, 128), [[-1, 128]], Op.is_equal, 0, 1)
    for nm, val in SCALED:
        act(whole(nm), I, Fn.Identity, 0.0, 8.0 if nm == "I16" and "free" in cfg["merge"] else val)
    memset(whole("onesF"), 1.0)
    asel(whole("Ash"), whole("onesF"), [[-1, 160]], Op.is_equal, 16, 1)
    ts(whole("A0"), whole("Ash"), h0f, None, Op.mult)
    ts(whole("A1"), whole("Ash"), h1f, None, Op.mult)
    iota(whole("rr"), [[0, 16], [256, 16]], 0, 0)
    b1 = whole("B1")
    asel(b1, R("ones", 0, 144), [[0, 9], [1, 16]], Op.is_equal, -15, 0)
    asel(b1, b1, [[1, 144]], Op.is_ge, 0, -1)
    asel(b1, b1, [[-1, 144]], Op.is_ge, 15, 1)
    ts(whole("B8"), b1, 8192.0, None, Op.mult)
    memset(R("rmin", 0, 512), 0.0); memset(R("rmin", 0, 512, 16), 255.0)
    act(R("rmax", 0, 512), R("rmin", 0, 512), Fn.Identity, 255.0, -1.0)
    for nm in ("rmin", "rmax"):
        for n in (512, 1024):
            if n < sc[nm][1][1]:
                act(R(nm, n, 2 * n), R(nm, 0, n), Fn.Copy)
    if cfg["kpe"]:
        memset(R("ab", 0, 512), -37.0)
        for q in range(4):
            asel(R("selT", 512 * q, 512 * q + 512), R("ab", 0, 512), [[-1, 4], [-16, 8], [0, 16]], Op.is_equal, -4 * q, 1)
    else:
        iota(whole("iot"), [[1, B]], -256, 0)
    ts(R("p15", 0, 1), R("pi", 0, 1), 15, None, Op.bitwise_and)
    ts(c512, R("p15", 0, 1), 0.0 if cfg["sides"] else float(B), None, Op.add)
    T0 = 16 if cfg["sides"] else 0
    if cfg["sides"]:
        memset(whole("c272"), 272.0)
        act(whole("nB8"), b1, Fn.Identity, 0.0, -8192.0)
    ts(c8, R("p15", 0, 1), 8.0, None, Op.mult)
    ts(c256, R("p15", 0, 1), 256.0, None, Op.mult)
    memset(cpar, -136.5 * STEEP); memset(whole("c35"), -3.5)
    def row(nm, p):
        return R(nm, 0, 128, 1, p, p + 1)
    memset(whole("Cmat"), 0.0); memset(whole("CK"), 0.0)
    memset(row("Cmat", 0), -float(LOW)); memset(row("Cmat", 64), -2.0 ** 26)
    memset(row("CK", 96), -7.0 / 16)
    for p, step, base in ((0, 512, 37 * 256), (32, 96, 0), (64, 5, 0)):
        iota(row("CK", p), [[0, 8], [step, 16]], base, 0)
    iota(row("Cmat", 32), [[0, 8], [-512, 16]], 144 * 512, 0)
    bd = whole("BDh")
    memset(bd, 0.5 * STEEP)
    asel(bd, bd, [[16, 8], [0, 16]], Op.is_ge, 15, -1)
    asel(bd, bd, [[-16, 8], [0, 16]], Op.is_ge, 0, 1)
    ts(whole("rk"), R("rmax", 0, w), 0.0, -2.0 ** 28, Op.is_equal, Op.mult)
    ts(R("maskZ", 0, L), whole("rr"), c256, 0.5, Op.is_le, Op.mult)
    if cfg["pair"]:
        memset(R("maskZ", L, ZS), 0.0)
        ts(c528, R("p15", 0, 1), B + 16.0, None, Op.add)
    ts(whole("j8"), whole("jc"), c8, None, Op.add)

    def sel(nm, k):
        return R(nm, 15 - k, 143 - k)

    dturn = [0]
    for v in range(VISITS):
        last = v == VISITS - 1
        cur[1] = str(v)
        Xw = whole("X%d" % (v % 2 if cfg["two"] else 0)); Xn = whole("X%d" % ((v + 1) % 2 if cfg["two"] else 0))
        tab = whole("TTi") if v == 0 else R("TT", T0, T0 + B)
        Tf, Tu, bu, cin, cout = "Tf%d" % v, "Tu%d" % v, "bu%d" % v, "cin%d" % v, "cout%d" % v
        Tout = "Tout" if last else "Ts%d" % v
        def ln(nm, ch):
            return R(nm, ch * w, ch * w + w)
        def lc(nm, ch):
            return R(nm, ch * nc, ch * nc + nc)
        def ps(ch, k):
            return R("S%d" % ch, k * w, k * w + w)
        def strided(nm, ch, k):
            return R(nm, 16 * ch * w + k, 16 * (ch + 1) * w, 16)
        def pieces(ch):
            for k, a in enumerate(range((ch + 1) * w - pl, ch * w - 1, -pl)):
                cur[0] = "%d%s" % (ch, "'" * k)
                yield a, a + pl
            cur[0] = str(ch)
        def spans(nm, ch):
            return [(ch * w, ch * w + w)] if "%s:%d" % (nm, ch) in cfg["merge"] else pieces(ch)
        def cuts(nm, ch):
            if "%s:%d" % (nm, ch) not in cfg["cut"]:
                yield lambda r: r
                return
            for a, b in pieces(ch):
                lo, hi = a - ch * w, b - ch * w
                yield lambda r: R(r[0], r[1] + lo * r[3], r[1] + (hi - 1) * r[3] + 1, r[3])
        def t1(scale, ch):
            return [(whole(scale), ln(Tf, ch)), (whole(scale), ln("prod", ch))]
        def onV(nm, ch):
            return "%s:%d" % (nm, ch) in cfg["onV"]
        def above(nm, ch, out, count, thr):
            if onV(nm, ch):
                ts(out, count, -STEEP, thr, Op.mult, Op.is_le)
            else:
                act(out, count, Fn.Sigmoid, thr, STEEP)
        for ch in turns():
            if v == 0:
                copy(ln(Tu, ch), ln("Tin", ch))
                ts(ln(Tf, ch), ln(Tu, ch), 0.0, None, Op.add)
                copy(lc(bu, ch), lc("bin", ch))
            copy(ln("Hu", ch), ("ind", tab, lc(bu, ch)))
            ts(ln("Hf", ch), ln("Hu", ch), 0.0, None, Op.add)
            pe("pD", acc(ps(ch, 1), [(I, ln("Hf", ch)), (whole("negI"), ln(Tf, ch))]))
            for a, b in spans("xg", ch):
                gather(R("xg", 16 * a, 16 * b), Xw, R(Tu, a, b))
            for a, b in spans("cmp", ch):
                tt(R("cmp", 16 * a, 16 * b), ("ind", Xw, R("Hu", a, b)), R("xg", 16 * a, 16 * b), Op.is_ge)
        if cfg["two"]:
            add("S", "dup", (Xn, Xw), [Xw, ln("Hu", 0)], [Xn], 128 * W * 2, "d", "dup", sem=("dup%d" % v, 16))
        if v == 0:
            copy(R("TT", T0, T0 + B), whole("TTi"), "TTinit")
        nbb = whole("nbb")
        ts(nbb, whole(bu), -1.0, 256.0, Op.mult, Op.add)
        ts(whole("fbk"), whole(bu), 97.0 - LOW - 8192, None, Op.add)
        zd = R("Z", 0, L)
        wz = ZS if cfg["pair"] else L
        def spread(r):
            return R("selT", 128 * r, 128 * r + 128)
        lumps = [[(R("Z", 0, wz), I, R("maskZ", 0, wz), True, False)]]
        if cfg["kpe"]:
            lumps.append([(R("Z", r, L, 16), spread(r), nbb, False, False) for r in range(16)])
        else:
            act(whole("bb"), ("ind", whole("iot"), whole(bu)), Fn.Copy)
            lumps[0].append((zd, whole("I37"), whole("bb"), False, False))
        if cfg["pair"]:
            if cfg["kpe"]:
                lumps.append([(R("Z", L + r, ZS, 16), spread(r), R("nbb", 1, 16, 2), False, False) for r in range(16)])
            else:
                lumps[0] += [(R("Z", L + 16 * c, L + 16 * c + 16), whole("I37"), R("bb", 32 * c + 16, 32 * c + 32), False, False)
                             for c in range(8)]
            lumps.append([(R("Z", L + r, ZS, 16), whole("I37"), R("nbb", 0, 16, 2), False, False) for r in range(16)])
        lumps.append([(R("Z", r, L, 16), whole("I37"), nbb, False, r == 15) for r in range(16)])
        if cfg["kpe"]:
            lumps[0:2] = [lumps[0] + lumps[1]]
        for mm in lumps:
            pe("pZd", mm, grp=("z", v))
        off = R("Z", ZS, ZS + 16)
        ts(R("E", 0, wz), R("Z", 0, wz), 0.0, None, Op.is_equal)
        mm = acc(off, [(whole("negI"), nbb)] + [(sel("B8", r), R("E", r, L, 16)) for r in range(16)])
        if cfg["sides"]:
            even, odd = R("Z", ZS, ZS + 16, 2), R("Z", ZS + 1, ZS + 16, 2)
            pe("poff", mm[:1] + [(off, I, whole("c272"), False, False)] +
               [(odd, sel("nB8", r), R("E", L + r, ZS, 16), False, False) for r in range(16)], grp=("o", v))
            pe("poff", [(odd, sel("nB8", r), R("E", 16 + r, L, 32), False, False) for r in range(16)], grp=("o", v))
            pe("poff", [(even, sel("B8", r), R("E", r, L, 32), False, r == 15) for r in range(16)], grp=("o", v))
            ts(R("offu", 0, 16), off, c512, c528, Op.max, Op.min)
        elif cfg["pair"]:
            odd = [(R("Z", ZS + 1, ZS + 16, 2), sel("B8", r), R("E", L + r, ZS, 16), False, False) for r in range(16)]
            pe("poff", mm[:1] + odd, grp=("o", v))
            pe("poff", mm[1:], grp=("o", v))
        else:
            pe("poff", mm)
        if cfg["sides"]:
            pass
        elif cfg["pair"]:
            ts(R("offu", 0, 16, 2), R("Z", ZS, ZS + 16, 2), 256.0, c512, Op.add, Op.min)
            ts(R("offu", 1, 16, 2), R("Z", ZS + 1, ZS + 16, 2), 256.0, c528, Op.add, Op.min)
        else:
            ts(R("offu", 0, 32, 2), off, 256.0, c512, Op.add, Op.min)
        for ch in turns():
            tq, kq = ps(ch, 2), ps(ch, 3)
            for a, b in pieces(ch):
                pe("pvote", acc(R("KB", L + a, L + b), [
                    (sel("B1", k), R("cmp", 16 * a + k, 16 * b, 16)) for k in range(16)]))
            thr = -STEEP * 8.5 if v == 0 else R("vb", v, v + 1)
            for u in cuts("T1", ch):
                above("sgn", ch, u(ln("sgn", ch)), u(R("KB", L + ch * w, L + ch * w + w)), thr)
                tt(u(ln("prod", ch)), u(ps(ch, 1)), u(ln("sgn", ch)), Op.mult)
                pe("pT1", acc(u(tq), [(l, u(r)) for l, r in t1("I4", ch)]))
                ts(u(ln("T1u", ch)), u(tq), 4.0, None, Op.mult)
            mm = acc(kq, [(whole("CK"), R("ones", 0, w))] + t1("I8", ch)) + acc(ps(ch, 0), t1("I", ch))
            if cfg["kpe"]:
                mm[1:1] = [(R(kq[0], kq[1] + r, kq[2], 16), R("selT", 128 * r, 128 * r + 128), lc("nbb", ch), False, False)
                           for r in range(16)]
            else:
                mm[1:1] = [(kq, whole("I37"), ln("bb", ch), False, False)]
            pe("pK", mm)
            for a, b in spans("z", ch):
                gather(R("z", 16 * a, 16 * b), Xw, R("T1u", a, b))
            for a, b in spans("smin", ch):
                scan(R("smin", 16 * a, 16 * b), R("rmin", 0, 16 * (b - a)), R("z", 16 * a, 16 * b), Op.max, Op.min)
            for a, b in spans("smax", ch):
                scan(R("smax", 16 * a, 16 * b), R("rmax", 0, 16 * (b - a)), R("z", 16 * a, 16 * b), Op.min, Op.max)
            m = strided("smin", ch, 15)
            for u in cuts("n", ch):
                tt(u(ln("P", ch)), u(tq), u(m), Op.mult)
                tt(u(ln("ni", ch)), u(kq), u(ln("P", ch)), Op.add)
                ts(u(ln("nn", ch)), u(ln("ni", ch)), W - 1, None, Op.bitwise_and)
                copy(u(ln("nu", ch)), u(ln("nn", ch)))
            for a, b in spans("e", ch):
                gather(R("e", 16 * a, 16 * b), Xw, R("nu", a, b))
            if "free" in cfg["merge"]:
                pass
            elif onV("free", ch):
                pe("pm", acc(tq, [(I, m)]))
                tt(ln("free", ch), tq, ln(cin, ch), Op.is_gt)
            else:
                pe("pm", acc(tq, [(I, m), (whole("negI"), ln(cin, ch))]))
                act(ln("free", ch), tq, Fn.Sigmoid, -STEEP * 0.5, STEEP)
            if "nf" not in cfg["merge"]:
                ts(ln("nf", ch), ln("nu", ch), 0.0, None, Op.add)
                pe("pD2", acc(ps(ch, 1), t1("negI", ch) + [(I, ln("nf", ch))]))
            if "q2" not in cfg["merge"]:
                ts(ln("q2", ch), ln("nu", ch), 1.0 / B, 128.5 + 0.5 / B, Op.mult, Op.add)
        if "free" in cfg["merge"]:
            pe("pm", acc(zd, [(I, R("smin", 15, 16 * L, 16)), (whole("negI"), whole(cin))]))
            act(whole("free"), zd, Fn.Sign, -0.5)
        if "nf" in cfg["merge"]:
            ts(whole("nf"), whole("nu"), 0.0, None, Op.add)
            for ch in turns():
                pe("pD2", acc(ps(ch, 1), t1("negI", ch) + [(I, ln("nf", ch))]))
        if "q2" in cfg["merge"]:
            ts(whole("q2"), whole("nu"), 1.0 / B, 128.5 + 0.5 / B, Op.mult, Op.add)
        asel(whole(cout), R("smin", 15, 16 * L, 16), [[0, L]], Op.is_ge, 0, 0)
        if not last:
            send(whole(cout), whole("cin%d" % (v + 1)), "arrc%d" % v, 128 * L * 2)
        else:
            store("S", "ylast", whole(cout), 0, 128 * L * 2)
        u = [(sel("B1", r), R("smax", 15 + 16 * r, 16 * L, 256)) for r in range(16)]
        uj = R("Z", ZS + 16, ZS + 32)
        pe("pu", acc(uj, u + [(I, whole("c35"))]))
        ts(whole("q8"), uj, 8 * MAGIC, -8 * MAGIC, Op.add, Op.add)
        if cfg["u3"]:
            tt(whole("u7"), uj, whole("q8"), Op.subtract)
            pe("pj", acc(uj, [(I, whole("j8")), (I, whole("u7"))]))
            ts(whole("ju"), uj, 3.5, None, Op.add)
        else:
            uj = R("Z", ZS + 32, ZS + 48)
            pe("pj", acc(uj, u + [(I, whole("j8")), (whole("negI"), whole("q8"))]))
            copy(whole("ju"), uj)
        if cfg["xjV"]:
            tt(whole("xs"), ("ind", Xw, whole("ju")), R("smax", 15, 16 * L, 16), Op.add, "xj")
            ts(whole("xu"), whole("xs"), 0.5, -0.25, Op.mult, Op.add, "xb")
            copy(("ind", Xn, whole("ju")), whole("xu"), "Xsc")
        else:
            gather(whole("xj"), Xw, whole("ju"))
            pe("px", acc(zd, [(whole("I2"), R("smax", 15, 16 * L, 16)), (whole("nI4"), ones), (whole("I2"), whole("xj"))]))
            ts(whole("xb"), zd, MAGIC, -MAGIC, Op.add, Op.add)
            copy(("ind", Xn, whole("ju")), whole("xb"), "Xsc")
        if last:
            store("S", "yclk", Xn, 1, 128 * W * 2)
        for ch in turns():
            def blk(nm, q):
                return R(nm, 16 * ch * w + 512 * q, 16 * ch * w + 512 * (q + 1))
            ns = 4 if ch in cfg["wide"] else 2; nj = 16 // ns; wl = 512 // nj
            def top(q):
                return w - wl * (1 + q // ns)
            def of(nm, q, j):
                return R(nm, 16 * ch * w + 512 * q + j, 16 * ch * w + 512 * (q + 1), nj)
            def eq(q):
                o = 16 * (ch * w + top(q))
                return R("e", o + q % ns, o + 16 * wl, ns)
            def ends(nm, q):
                o = 16 * (ch * w + top(q))
                return R(nm, o + 15, o + 16 * wl, 16)
            def part(r, q):
                return R(r[0], r[1] + top(q), r[1] + top(q) + wl)
            def diff(name, bank, q, sub, o=0):
                pe(name, [(R(bank, o, o + 512), I, eq(q), True, False)] +
                   [(R(bank, o + j, o + 512, nj), whole("negI"), ends(sub, q), False, j == nj - 1) for j in range(nj)])
                return R(bank, o, o + 512)
            c2 = ps(ch, 3)
            filled = set()
            for q in range(4):
                cur[0] = "%d%s" % (ch, "abcd"[q])
                mb = cfg["mb"][2 * ch + q // ns]
                mm = [(c2, whole("I16"), ln("free", ch), True, False)] if q == 0 else []
                bank = cfg["onA"].get("cmp2:" + cur[0])
                if bank:
                    act(blk("cmp2", q), diff("ps", bank, q, "smin"), Fn.Sigmoid, STEEP * 0.5, STEEP)
                else:
                    if q // ns not in filled:
                        pe("pM", [(R(mb, j, 512, nj), I, ends("smin", q), True, True) for j in range(nj)])
                        filled.add(q // ns)
                    tt(blk("cmp2", q), eq(q), R(mb, 0, 512), Op.is_ge)
                pe("pc2", mm + [(part(c2, q), sel("B1", ns * j + q % ns), of("cmp2", q, j), False, q == 3 and j == nj - 1)
                                for j in range(nj)], grp=("c", v, ch))
            cur[0] = str(ch)
            above("rdy", ch, ln("rdy", ch), c2, -STEEP * (19.5 if "free" in cfg["merge"] else 27.5))
            tt(ln("prod2", ch), ps(ch, 1), ln("rdy", ch), Op.mult)
            tt(ln(Tout, ch), ps(ch, 0), ln("prod2", ch), Op.add, "T2")
            if not last:
                ts(ln("Us%d" % v, ch), ln(Tout, ch), 0.0, None, Op.add, name="T2u")
                send(ln("Us%d" % v, ch), ln("Tu%d" % (v + 1), ch), "arrU%d_%d" % (v, ch), 128 * w * 2)
                send(ln(Tout, ch), ln("Tf%d" % (v + 1), ch), "arrT%d_%d" % (v, ch), 128 * w * 2)
            if cfg["pair"]:
                for cc in range(ch * nc + nc - 2, ch * nc - 1, -2):
                    copy(("ind", whole("TT"), R("offu", cc, cc + 2)), R(Tout, 16 * cc, 16 * cc + 32))
            else:
                for cc in range(ch * nc + nc - 1, ch * nc - 1, -1):
                    copy(("ind", whole("TT"), R("offu", 2 * cc, 2 * cc + 1)), R(Tout, 16 * cc, 16 * cc + 16))
            key = ln("KB", ch)
            for q in range(4):
                cur[0] = "%d%s" % (ch, "abcd"[q])
                if not cfg["dd"]:
                    act(blk("ab", q), diff("pd", "D%d" % (q % 2), q, "smax"), Fn.Abs)
                elif q % 2 == 0:
                    diff("pd", "DD", q, "smax"); diff("pd", "DD", q + 1, "smax", 512)
                    act(R("ab", blk("ab", q)[1], blk("ab", q + 1)[2]), whole("DD"), Fn.Abs)
                mm = [(key, whole("Cmat"), R("ones", 0, w), True, False),
                      (key, whole("nI512"), ln("q2", ch), False, False)] if q == 0 else []
                pe("pk", mm + [(part(key, q), sel("B8", ns * j + q % ns), of("ab", q, j), False, False) for j in range(nj)],
                   grp=("k", v, ch))
            cur[0] = str(ch)
            pe("pkey", [(key, whole("Ipen"), ln("rdy", ch), False, False),
                        (key, I, ln("nf", ch), False, True)], grp=("k", v, ch))
            add("V", "tr", (ln("kt", ch), key), [key], [ln("kt", ch)], w, "c")
            scan(ln("ks", ch), whole("rk"), ln("kt", ch), Op.add, Op.max)
            sw = ZS + 48 + ch * nc
            mm = []
            for h in (0, 1):
                o = R("Z", sw + h, sw + nc, 2)
                far = 32 * h
                mm += acc(o, [(R("A%d" % h, 16, 144), R("ks", ch * w + 15 + 16 * h, ch * w + w, 32)),
                              (R("A%d" % h, far, far + 128), R("ks", ch * w + 31 - 16 * h, ch * w + w, 32))])
            pe("psw", mm)
            tt(lc("ki", ch), R("Z", sw, sw + nc), lc("fbk", ch), Op.max)
            ts(lc("bi", ch), lc("ki", ch), B - 1, None, Op.bitwise_and)
            if last:
                copy(lc("bout", ch), lc("bi", ch))
            else:
                copy(lc("bs%d" % v, ch), lc("bi", ch))
                send(lc("bs%d" % v, ch), lc("bu%d" % (v + 1), ch), "arrb%d_%d" % (v, ch), 128 * nc * 2)
        if last:
            store("S", "ytrav", whole("Tout"), 2, 128 * L * 4)
            store("S", "yttab", R("TT", T0, T0 + B), 3, 128 * B * 4)
            store("A", "yslot", whole("bout"), 4, 128 * 64)
        else:
            act(whole("has"), R("Z", ZS + 48, ZS + 64), Fn.Sign, LOW + 8192.0, acc=R("scol", 0, 1))
            y = R("Z", ZS + 64, ZS + 65)
            pe("ppar", acc(y, [(bd, R("scol", 0, 1)), (R("Ash", 16, 144), cpar)]))
            ts(R("half", 0, 1), y, -0.5 / STEEP, -4.5, Op.mult, Op.add)
            ts(R("vb", v + 1, v + 2), R("half", 0, 1), 2 * STEEP, y, Op.mult, Op.add)
    seen = {}
    for i, o in enumerate(ops):
        dep = set()
        for a in o["rd"]:
            for lo, hi, j, wr in seen.get(a[0], []):
                if wr and lo < a[2] and a[1] < hi:
                    dep.add(j)
        hard = set(dep)
        for a in o["wr"]:
            for lo, hi, j, wr in seen.get(a[0], []):
                if lo < a[2] and a[1] < hi:
                    dep.add(j)
                    if ("waw" if wr else "war") not in cfg["free"]:
                        hard.add(j)
        o["soft"] = set(j for j in dep - hard if ops[j]["eng"] == o["eng"] and o["eng"] in "VA" and "sem" not in ops[j]
                        and "sem" not in o)
        for a in o["wr"]:
            if a[3] == 1 and a[4] == 0 and a[5] == 128:
                seen[a[0]] = [t for t in seen.get(a[0], []) if not (a[1] <= t[0] and t[1] <= a[2])]
        for a in o["wr"]:
            seen.setdefault(a[0], []).append((a[1], a[2], i, True))
        for a in o["rd"]:
            seen.setdefault(a[0], []).append((a[1], a[2], i, False))
        if o.get("grp") and o["last"]:
            dep.update(j for j in range(i) if ops[j].get("grp") == o["grp"])
        dep.discard(i)
        o["dep"] = sorted(dep)
        o["banks"] = sorted(set(a[0] for a in o["rd"] + o["wr"] if a[0] in BANKS))
    return ops


def cost(o, eng, m):
    c, n, cyc = o["cls"], o["n"], 0.83 * m["f"]
    if c == "d":
        return 60.0, m["dma"] + n * m["db"]
    if c == "r":
        return 500.0, m["rem"] + n * m["rb"]
    if c == "p":
        t = n * m["pe"] * m["f"] + len(o["args"]) * m["pov"]
        return t, t
    if c == "g":
        t = (50.0 if eng == "V" else 65.0) + n * m["g"] * cyc
    elif c == "s":
        t = 50.0 + n * m["s"] * cyc
    else:
        k = {"h": 0.5, "c": 1.0, "th": m["tt2"], "tc": 2.0}[c]
        t = m["ova" if eng == "A" else "ov"] + max(64.0, n * k) * cyc
    return t, t


def gap(a, b, m):
    if a == b:
        return 0.0 if a == "P" else m["same"]
    return m["lat"]


def chained(words, named, mine):
    chain = []
    for v in range(-1, VISITS + 1):
        here = []
        for t in words:
            t, _, only = t.partition("@")
            u = str(v + t.count("+") - t.count("-"))
            if u in only or (not only and not any(x.startswith(t + "@") and u in x.partition("@")[2] for x in words)):
                here.append((t.rstrip("+-"), u))
        for k, t in enumerate(here):
            have = [i for i in named.get(t, []) if mine[i]]
            first = here[:k].count(t)
            chain += have[first:first + 1] if t in here[k + 1:] else have[first:]
    return chain


def schedule(ops, cfg, m):
    n = len(ops)
    on = [o["eng"] for o in ops]
    succ = [[] for _ in ops]
    after = [set(o["dep"]) for o in ops]
    named = {}
    for i, o in enumerate(ops):
        named.setdefault((o["tag"], o["vis"]), []).append(i)
    for e, line in zip("VAP", cfg["order"]):
        chain = chained(line.split(), named, [o["eng"] == e for o in ops])
        for j, i in zip(chain, chain[1:]):
            after[i].add(j)
    for e in "AGS":
        chain = [i for i, o in enumerate(ops) if o["eng"] == e and o["vis"] == "c"]
        for j, i in zip(chain, chain[1:]):
            after[i].add(j)
    for i in range(n):
        for j in after[i]:
            succ[j].append(i)
    back, left = [], [len(a) for a in after]
    todo = [i for i in range(n) if not left[i]]
    while todo:
        i = todo.pop(); back.append(i)
        for j in succ[i]:
            left[j] -= 1
            if not left[j]:
                todo.append(j)
    assert len(back) == n
    rank = [0.0] * n
    for i in reversed(back):
        hold, fin = cost(ops[i], on[i], m)
        rank[i] = max([fin] + [rank[j] + (fin + gap(on[i], on[j], m) if i in ops[j]["dep"] else hold) for j in succ[i]])
    up = cfg["up"]
    prio = [rank[i] + 100.0 * (up.get(o["tag"], 0) + up.get(o["tag"] + "@" + o["vis"], 0)) for i, o in enumerate(ops)]
    left = [len(a) for a in after]
    ready = [i for i in range(n) if left[i] == 0]
    done = [0.0] * n; extra = [[] for _ in ops]
    free = {e: 0.0 for e in "VAPGS"}
    lastb = {b: {} for b in BANKS}; opened = {}
    seq = []; lastg = []; fed = {}
    while ready:
        cand = {e: [] for e in "VAPGS"}
        for i in ready:
            o = ops[i]; e = on[i]
            if e == "P" and o["first"] and any(b in opened for b in o["banks"]):
                continue
            if i not in fed:
                fed[i] = max([done[j] + gap(on[j], e, m) for j in o["dep"]] + [0.0])
            t = max(free[e], fed[i])
            for b in o["banks"]:
                for e2, j in lastb[b].items():
                    if e2 != e:
                        t = max(t, done[j] + m["lat"])
            cand[e].append((t, i))
        best = None
        for e in "VAPGS":
            if cand[e]:
                t0 = min(c[0] for c in cand[e])
                c = max((c for c in cand[e] if c[0] <= t0 + cfg["slack"]), key=lambda c: prio[c[1]])
                if best is None or t0 < best[0]:
                    best = (t0, e, c)
        e, (t, i) = best[1], best[2]
        o = ops[i]
        hold, fin = cost(o, e, m)
        free[e] = t + hold; done[i] = t + fin
        if o["kind"] in ("iota", "asel"):
            extra[i] += lastg; lastg[:] = [i]
        for b in o["banks"]:
            extra[i] += [j for e2, j in lastb[b].items() if e2 != e]
            lastb[b][e] = i
        if o.get("grp"):
            if o["first"]:
                opened[o["banks"][0]] = o["grp"]
            if o["last"]:
                del opened[o["banks"][0]]
        seq.append(i); ready.remove(i)
        for j in succ[i]:
            left[j] -= 1
            if left[j] == 0:
                ready.append(j)
    assert len(seq) == n
    return seq, on, extra, max(done)


def plan(cfg):
    ops = program(cfg)
    seq, on, extra, _ = schedule(ops, cfg, REF)
    pos = {}; num = {e: 0 for e in "VAPGS"}; at = {}
    for k, i in enumerate(seq):
        num[on[i]] += 1; pos[i] = num[on[i]]; at[i] = k
    known = {e: {} for e in "VAPGS"}; clock = {}; waits = {}; signals = set()
    for i in seq:
        e = on[i]; need = {}
        for j in ops[i]["dep"] + extra[i]:
            if on[j] == e == "P" or j in ops[i]["soft"]:
                continue
            key = ops[j]["sem"][0] if "sem" in ops[j] else on[j]
            if known[e].get(key, 0) < pos[j] and (key not in need or pos[need[key]] < pos[j]):
                need[key] = j
        ws = []
        for j in sorted(need.values(), key=lambda j: -at[j]):
            key = ops[j]["sem"][0] if "sem" in ops[j] else on[j]
            if known[e].get(key, 0) >= pos[j]:
                continue
            ws.append(j); signals.add(j)
            for k2, val in clock[j].items():
                known[e][k2] = max(known[e].get(k2, 0), val)
        waits[i] = ws
        if ops[i]["kind"] == "send":
            clock[i] = {ops[i]["sem"][0]: pos[i]}
        else:
            clock[i] = dict(known[e]); clock[i][ops[i]["sem"][0] if "sem" in ops[i] else e] = pos[i]
    count = {}; num = {e: 0 for e in "VAPGS"}
    for i in seq:
        if i in signals and "sem" not in ops[i]:
            num[on[i]] += 1; count[i] = num[on[i]]
    return ops, seq, on, waits, count, num


PLAN = []


def rank_program(g, core, T, topo):
    rank = T.rank_of(core)
    if rank is None:
        return
    if not PLAN:
        PLAN.append(plan(CFG))
    ops, seq, on, waits, count, num = PLAN[0]
    dst = T.cores[(rank + STEP) % NR]; frm = T.cores[(rank - STEP) % NR]
    rid, pid = topo.addr(dst, core)
    mask = topo.mask(core, dst)
    n_out, n_in = len(topo.engines(core, dst)), len(topo.engines(frm, core))
    Q = {"V": g.vector, "A": g.scalar, "P": g.tensor, "G": g, "S": g.sync}
    sent = 0; own = []
    for i in seq:
        o = ops[i]; e = on[i]; q = Q[e]; k = o["kind"]; a = o["args"]
        for j in waits[i]:
            if "sem" in ops[j]:
                q.wait_ge(T.sem[ops[j]["sem"][0]], ops[j]["sem"][1] or n_in)
            else:
                q.wait_ge(T.sem["q" + on[j]], count[j])
        if k == "send":
            g.remote_dma(view(T, a[1]), view(T, a[0]), T.sem[a[2]], T.sem.sent, pid, rid, mask)
            sent += n_out; own.append((a[2], n_in))
            continue
        if k in ("load", "store", "dup"):
            ins = q.dma_start(*[view(T, y) if isinstance(y, tuple) else T[y][:] for y in a])
            ins.then_inc(T.sem[o["sem"][0]], 16); own.append(o["sem"])
            continue
        x = [view(T, y) for y in a] if k != "mm" else a
        if k == "mm":
            for out, l, r, st, sp in a:
                ins = q.matmul(view(T, out), view(T, l), view(T, r), st, sp)
        elif k == "copy" or (k == "gather" and e == "V"):
            ins = q.tensor_copy(x[0], x[1])
        elif k == "gather":
            ins = q.activation(x[0], x[1], Fn.Copy)
        elif k == "tt":
            ins = q.tensor_tensor(x[0], x[1], x[2], x[3])
        elif k == "ts":
            ins = q.tensor_scalar(x[0], x[1], x[2], x[3], x[4]) if x[5] is None else q.tensor_scalar(*x)
        elif k == "scan":
            ins = q.tensor_tensor_scan(x[0], x[1], x[2], 0.0, x[3], x[4])
        elif k == "tr":
            ins = q.transpose(x[0], x[1])
        elif k == "act":
            if x[2] == Fn.Copy:
                ins = q.activation(x[0], x[1], x[2])
            else:
                ins = q.activation(x[0], x[1], x[2], bias=x[3], scale=x[4], accum_out=x[5])
        elif k == "memset":
            ins = q.memset(x[0], x[1])
        elif k == "iota":
            if x[4]:
                ins = q.iota(x[0], x[1], x[2], x[3], allow_small_or_imprecise_dtypes=True)
            else:
                ins = q.iota(x[0], x[1], x[2], x[3])
        else:
            ins = q.affine_select(x[0], x[1], x[2], x[3], 0.0, x[4], x[5])
        if i in count:
            ins.then_inc(T.sem["q" + e], 1)
    for e in "VAPG":
        if num[e]:
            g.wait_ge(T.sem["q" + e], num[e])
    g.wait_ge(T.sem.sent, sent)
    for s, val in own:
        g.wait_ge(T.sem[s], val)
